import numpy as np
import ml_dtypes


def mxq(x, axis, fmt="e4m3"):
    dtype, down = {"e4m3": (ml_dtypes.float8_e4m3fn, 7), "e5m2": (ml_dtypes.float8_e5m2, 14)}[fmt]
    v = np.moveaxis(np.asarray(x, np.float32).astype(ml_dtypes.bfloat16).astype(np.float64), axis, -1)
    blocks = v.reshape(v.shape[:-1] + (-1, 32))
    amax = np.abs(blocks).max(-1, keepdims=True)
    byte = np.maximum(np.where(amax > 0, np.frexp(amax)[1] - 1 + 127, 0) - down, 1)
    scale = np.exp2(byte - 127.0)
    codes = (blocks / scale).astype(np.float32).astype(dtype).astype(np.float64)
    return np.moveaxis((codes * scale).reshape(v.shape), -1, axis)


WIDE = False


def mx_kscale(k):
    if not WIDE:
        return np.ones(k)
    levels = np.array([10, -10, 5, -5, 0])
    if k % 512:
        return np.exp2(np.random.permutation(np.resize(levels, k // 32))).repeat(32)
    a = np.empty((k // 512, 16))
    for p in range(k // 512):
        a[p, :8] = np.random.permutation(np.resize(levels, 8))
        for g in range(8):
            far = levels[np.abs(levels - a[p, g]) >= 10]
            a[p, g + 8] = far[np.random.randint(len(far))]
    return np.exp2(a.ravel()).repeat(32)


def f64(x):
    return np.asarray(x).astype(np.float64)


def striped(idx):
    return np.tile(idx.reshape(-1, 16).T, (8, 1)).astype(np.uint16)


def unstriped(offs):
    return offs[:16].T.reshape(-1).astype(np.int64)


E2M1 = np.array([0.0, 0.5, 1.0, 1.5, 2.0, 3.0, 4.0, 6.0, -0.0, -0.5, -1.0, -1.5, -2.0, -3.0, -4.0, -6.0])


def pack_fp4(w):
    k, n = w.shape
    w = f64(np.asarray(w, np.float32).astype(ml_dtypes.bfloat16)).reshape(k // 32, 32, n)
    amax = np.abs(w).max(1)
    mant, ex = np.frexp(amax / 6.0)
    byte = np.clip(np.where(amax > 0, np.where(mant > 0.5, ex, ex - 1) + 127, 1), 1, 254)
    scaled = (w * np.exp2(127.0 - byte)[:, None, :]).reshape(k, n).astype(np.float32)
    c = np.ascontiguousarray(scaled.reshape(k // 512, 128, 4, n).transpose(0, 1, 3, 2)).astype(ml_dtypes.float4_e2m1fn).view(np.uint8) & 0xF
    words = (c[..., 0::2] | (c[..., 1::2] << 4)).reshape(k // 512, 128, 2 * n)
    return np.ascontiguousarray(words), np.ascontiguousarray(byte.astype(np.uint8).reshape(k // 512, 16, n))


def unpack_fp4(words, scales):
    g, _, n = scales.shape
    words = np.ascontiguousarray(words).reshape(g, 128, n, 2)
    nib = np.empty((g, 128, n, 4), np.uint8)
    nib[..., 0::2] = words & 0xF
    nib[..., 1::2] = words >> 4
    vals = E2M1[nib] * np.repeat(np.exp2(scales.astype(np.float64) - 127.0), 8, axis=1)[..., None]
    return vals.transpose(0, 1, 3, 2).reshape(g * 512, n)


def relu(v):
    return np.maximum(v, 0.0)

def planes(y):
    n, m = y.shape
    v = y.astype(np.float32).astype(ml_dtypes.bfloat16).astype(np.float64).reshape(n // 32, 32, m)
    top = np.abs(v).max(1)
    byte = np.clip(np.where(top > 0, np.frexp(top)[1] - 1 + 127 - 7, 1), 1, 254)
    codes = (v * np.exp2(127.0 - byte)[:, None, :]).reshape(n, m).astype(np.float32).astype(ml_dtypes.float8_e4m3fn).view(np.uint8)
    words = codes.reshape(n // 512, 128, 4, m).transpose(0, 1, 3, 2)
    return np.ascontiguousarray(words), np.ascontiguousarray(byte.astype(np.uint8).reshape(n // 512, 16, m))


K, T, H = 512, 512, 512


def setup_inputs():
    n = np.random.standard_normal
    s = mx_kscale(K)[:, None]
    u = mx_kscale(H)
    packed_xT = pack_fp4(n((K, T)) * s)
    return {
        "x_words": packed_xT[0],
        "x_scales": packed_xT[1],
        "w1": (n((K, H)) / np.sqrt(K) / s * u).astype(np.float32),
        "w2": (n((H, H)) / np.sqrt(2 * H) / u[:, None]).astype(np.float32),
        "w3": (n((H, H)) / np.sqrt(2 * H) / u[:, None]).astype(np.float32),
        "pos1": striped(np.random.permutation(T)),
        "pos2": striped(np.random.permutation(T)),
        "pos3": striped(np.random.permutation(T)),
        "pos4": striped(np.random.permutation(T)),
    }


def reference(x_words, x_scales, w1, w2, w3, pos1, pos2, pos3, pos4):
    xq = unpack_fp4(x_words, x_scales)
    h = relu(mxq(f64(w1), 0, "e4m3").T @ xq)
    z = np.maximum(np.maximum(np.maximum(h[:, unstriped(pos1)], h[:, unstriped(pos2)]), h[:, unstriped(pos3)]), h[:, unstriped(pos4)])
    out_0 = mxq(f64(w2), 0, "e4m3").T @ mxq(h, 0, "e4m3") + mxq(f64(w3), 0, "e4m3").T @ mxq(z, 0, "e4m3")
    return (out_0,) + planes(out_0)

@@ -1,0 +1,235 @@
+from contextlib import ExitStack
+
+import concourse.mybir as mybir
+
+F32 = mybir.dt.float32
+BF16 = mybir.dt.bfloat16
+I32 = mybir.dt.int32
+U32 = mybir.dt.uint32
+U16 = mybir.dt.uint16
+U8 = mybir.dt.uint8
+FP8X4 = mybir.dt.float8_e4m3fn_x4
+FP4X4 = mybir.dt.float4_e2m1fn_x4
+RELU = mybir.ActivationFunctionType.Relu
+MAX = mybir.AluOpType.max
+
+P = 128
+PACK = 4
+T = 512
+H = 512
+FLOPS = 3 * 2 * 512 * 512 * 512
+
+
+def tile_picked_wsagecat_max_lo_kernel(
+    tc, x_words, x_scales, w1, w2, w3, pos1, pos2, pos3, pos4, out_0, out_1, out_2
+):
+    nc = tc.nc
+    with ExitStack() as ctx:
+        lists_pool = ctx.enter_context(tc.tile_pool(name="lists", bufs=1))
+        sb = ctx.enter_context(tc.tile_pool(name="sb", bufs=1))
+        psum = ctx.enter_context(tc.psum_pool(name="psum", bufs=1))
+
+        def new_tile(name, shape, dtype):
+            return sb.tile(shape, dtype, name=name, align_bytes=64)
+
+        def quantize(codes, scales, src):
+            nc.vector.quantize_mx(out=codes.bitcast(FP8X4), scales=scales, in_=src)
+
+        xs = new_tile("xs", [P, T], U8)
+        nc.vector.memset(xs[:].bitcast(I32), 0)
+        warm = new_tile("warm", [P, 8], F32)
+        warm_out = new_tile("warm_out", [P, 8], F32)
+        nc.vector.memset(warm[:], 0.0)
+
+        w1_rows = w1.rearrange("(p j) c -> p j c", j=PACK)
+        w1_raw = [new_tile("w1_raw%d" % c, [P, PACK, 256], F32) for c in range(2)]
+        for c in range(2):
+            nc.sync.dma_start(out=w1_raw[c][:], in_=w1_rows[:, :, 256 * c : 256 * (c + 1)])
+        xw = new_tile("xw", [P, 2 * T], U8)
+        nc.sync.dma_start(out=xw[:].bitcast(I32), in_=x_words[0].bitcast(I32))
+        for q in range(4):
+            nc.scalar.dma_start(
+                out=xs[32 * q : 32 * q + 4, :].bitcast(I32), in_=x_scales[0, 4 * q : 4 * q + 4, :].bitcast(I32)
+            )
+        nc.scalar.activation(warm_out[:], warm[:], RELU)
+        lists = []
+        for d, pos in enumerate((pos1, pos2, pos3, pos4)):
+            offsets = lists_pool.tile([P, T // 16], U16, name="pos%d" % d)
+            nc.sync.dma_start(offsets[:], pos)
+            lists.append(offsets)
+        w_raw = []
+        for n, w in enumerate((w2, w3)):
+            raw = new_tile("w_raw%d" % n, [P, PACK, H], F32)
+            rows = w.rearrange("(q s r) c -> s q r c", s=PACK, r=8)
+            for s in range(PACK):
+                nc.sync.dma_start(out=raw[:, s, :], in_=rows[s])
+            w_raw.append(raw)
+
+        banks_p = [psum.tile([P, T], F32, name="bank_p%d" % t) for t in range(PACK)]
+        banks_q = [psum.tile([P, T], F32, name="bank_q%d" % t) for t in range(PACK)]
+
+        w1_bf = [new_tile("w1_bf%d" % t, [P, 512], BF16) for t in range(PACK)]
+        w1_codes = [new_tile("w1_codes%d" % t, [P, P], U32) for t in range(PACK)]
+        w1_scales = [new_tile("w1_scales%d" % t, [P, P], U8) for t in range(PACK)]
+
+        def round_w1(c, t, copy):
+            src = w1_raw[c][:].rearrange("p j (q t a l) -> p t q a j l", t=PACK, a=2, l=4)[:, t]
+            dst = w1_bf[t][:, 256 * c : 256 * (c + 1)].rearrange("p (q a l j) -> p q a j l", a=2, l=4, j=PACK)
+            copy(out=dst, in_=src)
+
+        for t in range(PACK):
+            round_w1(0, t, nc.vector.tensor_copy)
+        for t in range(PACK):
+            round_w1(1, t, nc.vector.tensor_copy if t % 2 == 0 else nc.scalar.copy)
+        h = new_tile("h", [P, PACK, T], F32)
+        for t in range(PACK):
+            quantize(w1_codes[t][:], w1_scales[t][:], w1_bf[t][:])
+            nc.tensor.matmul_mx(
+                out=banks_p[t][:], lhsT=w1_codes[t][:].bitcast(FP8X4), lhsT_scale=w1_scales[t][:],
+                rhs=xw[:].bitcast(FP4X4), rhs_scale=xs[:], start=True, stop=True,
+            )
+            nc.scalar.activation(h[:, t, :], banks_p[t][:], RELU)
+
+        h_bf = new_tile("h_bf", [P, PACK * T], BF16)
+        nc.scalar.copy(
+            out=h_bf[:].rearrange("p (c i t) -> p c t i", i=4, t=PACK),
+            in_=h[:].rearrange("p t (c i) -> p c t i", i=4),
+        )
+        w_bf = []
+        for n in range(2):
+            wb = new_tile("w_bf%d" % n, [P, PACK * H], BF16)
+            nc.scalar.copy(
+                out=wb[:].rearrange("p (t m s) -> p m t s", t=PACK, s=PACK),
+                in_=w_raw[n][:].rearrange("p s (m t) -> p m t s", t=PACK),
+            )
+            w_bf.append(wb)
+        h_codes = new_tile("h_codes", [P, T], U32)
+        h_scales = new_tile("h_scales", [P, T], U8)
+        w_codes = [new_tile("w_codes%d" % n, [P, H], U32) for n in range(2)]
+        w_scales = [new_tile("w_scales%d" % n, [P, H], U8) for n in range(2)]
+
+        chunks = [(0, 256), (256, 128), (384, 128)]
+        y_words = new_tile("y_words", [P, T], U32)
+        y_scales = new_tile("y_scales", [P, T], U8)
+        out_rows = out_0.rearrange("(p t) v -> p t v", t=PACK)
+        out_words = out_1[0].rearrange("p c r -> p (c r)").bitcast(I32)
+
+        def planes(ap):
+            return ap.rearrange("p (u t v) -> p u t v", u=2, t=PACK)
+
+        def gather(ci, d, dst):
+            v0, n = chunks[ci]
+            for t in range(PACK):
+                nc.vector.tensor_copy(
+                    out=planes(dst)[:, :, t, :], in_=h[:, t, :].indirect(lists[d][:, v0 // 16 : (v0 + n) // 16])
+                )
+
+        def fold(acc, other):
+            nc.vector.tensor_tensor(acc, acc, other, MAX)
+
+        def weave_z(copy, dst, src):
+            copy(
+                out=dst.rearrange("p (u c i t) -> p u c t i", u=2, i=4, t=PACK),
+                in_=src.rearrange("p (u t c i) -> p u c t i", u=2, i=4, t=PACK),
+            )
+
+        def own_pass(ci, banks):
+            v0, n = chunks[ci]
+            for t in range(PACK):
+                cols = slice(P * t, P * (t + 1))
+                nc.tensor.matmul_mx(
+                    out=banks[t][:, 0:n], lhsT=w_codes[0][:, cols].bitcast(FP8X4), lhsT_scale=w_scales[0][:, cols],
+                    rhs=h_codes[:, v0 : v0 + n].bitcast(FP8X4), rhs_scale=h_scales[:, v0 : v0 + n],
+                    start=True, stop=False,
+                )
+
+        def neighbour_pass(ci, banks, z_codes, z_scales):
+            n = chunks[ci][1]
+            for t in range(PACK):
+                cols = slice(P * t, P * (t + 1))
+                nc.tensor.matmul_mx(
+                    out=banks[t][:, 0:n], lhsT=w_codes[1][:, cols].bitcast(FP8X4), lhsT_scale=w_scales[1][:, cols],
+                    rhs=z_codes[:].bitcast(FP8X4), rhs_scale=z_scales[:],
+                    start=False, stop=True,
+                )
+
+        def result_out(ci, banks, y, copies):
+            v0, n = chunks[ci]
+            for t in range(PACK):
+                copies[t](out=y[:, t, :], in_=banks[t][:, 0:n])
+            nc.sync.dma_start(out=out_rows[:, :, v0 : v0 + n], in_=y[:])
+
+        def weave_y(copy, dst, y):
+            copy(
+                out=dst[:].rearrange("p (c i t) -> p c t i", i=4, t=PACK),
+                in_=y[:].rearrange("p t (c i) -> p c t i", i=4),
+            )
+
+        def result_planes(ci, y_bf):
+            v0, n = chunks[ci]
+            quantize(y_words[:, v0 : v0 + n], y_scales[:, v0 : v0 + n], y_bf[:])
+            nc.sync.dma_start(out=out_words[:, v0 : v0 + n], in_=y_words[:, v0 : v0 + n].bitcast(I32))
+
+        z_codes = [new_tile("z_codes%d" % ci, [P, n], U32) for ci, (v0, n) in enumerate(chunks)]
+        z_scales = [new_tile("z_scales%d" % ci, [P, n], U8) for ci, (v0, n) in enumerate(chunks)]
+        z_bf = [new_tile("z_bf%d" % ci, [P, PACK * n], BF16) for ci, (v0, n) in enumerate(chunks)]
+        y = [new_tile("y%d" % ci, [P, PACK, n], F32) for ci, (v0, n) in enumerate(chunks)]
+        y_bf = [new_tile("y_bf%d" % ci, [P, PACK * n], BF16) for ci, (v0, n) in enumerate(chunks)]
+        on_scalar = [nc.scalar.copy] * PACK
+
+        z_a = new_tile("z_a", [P, 1024], BF16)
+        g_a = [new_tile("g_a%d" % i, [P, 1024], BF16) for i in range(2)]
+        gather(0, 0, z_a[:])
+        gather(0, 1, g_a[0][:])
+        fold(z_a[:], g_a[0][:])
+        gather(0, 2, g_a[1][:])
+        quantize(h_codes[:], h_scales[:], h_bf[:])
+        fold(z_a[:], g_a[1][:])
+        gather(0, 3, g_a[0][:])
+        quantize(w_codes[0][:], w_scales[0][:], w_bf[0][:])
+        fold(z_a[:], g_a[0][:])
+        own_pass(0, banks_q)
+        own_pass(1, banks_p)
+        weave_z(nc.scalar.copy, z_bf[0][:], z_a[:])
+        z_b = new_tile("z_b", [P, 512], BF16)
+        g_b = new_tile("g_b", [P, 512], BF16)
+        gather(1, 0, z_b[:])
+        quantize(w_codes[1][:], w_scales[1][:], w_bf[1][:])
+        gather(1, 1, g_b[:])
+        fold(z_b[:], g_b[:])
+        quantize(z_codes[0][:], z_scales[0][:], z_bf[0][:])
+        neighbour_pass(0, banks_q, z_codes[0], z_scales[0])
+        lo, hi = z_bf[0][:, 0:512], z_bf[0][:, 512:1024]
+        gather(1, 2, lo)
+        fold(z_b[:], lo)
+        gather(1, 3, hi)
+        fold(z_b[:], hi)
+        result_out(0, banks_q, y[0], on_scalar)
+        weave_z(nc.scalar.copy, z_bf[1][:], z_b[:])
+        weave_y(nc.scalar.copy, y_bf[0], y[0])
+        own_pass(2, banks_q)
+        gather(2, 0, lo)
+        gather(2, 1, hi)
+        fold(lo, hi)
+        quantize(z_codes[1][:], z_scales[1][:], z_bf[1][:])
+        neighbour_pass(1, banks_p, z_codes[1], z_scales[1])
+        result_out(1, banks_p, y[1], on_scalar)
+        weave_y(nc.scalar.copy, y_bf[1], y[1])
+        gather(2, 2, z_bf[1][:])
+        fold(lo, z_bf[1][:])
+        gather(2, 3, hi)
+        for t in range(PACK):
+            fold(planes(lo)[:, :, t, :], planes(hi)[:, :, t, :])
+        result_planes(0, y_bf[0])
+        weave_z(nc.vector.tensor_copy, z_bf[2][:], lo)
+        result_planes(1, y_bf[1])
+        quantize(z_codes[2][:], z_scales[2][:], z_bf[2][:])
+        neighbour_pass(2, banks_q, z_codes[2], z_scales[2])
+        result_out(2, banks_q, y[2], [nc.scalar.copy, nc.vector.tensor_copy] * 2)
+        weave_y(nc.vector.tensor_copy, y_bf[2], y[2])
+        result_planes(2, y_bf[2])
+        for q in range(4):
+            queue = nc.sync if q % 2 else nc.scalar
+            queue.dma_start(
+                out=out_2[0, 4 * q : 4 * q + 4, :].bitcast(I32), in_=y_scales[32 * q : 32 * q + 4, :].bitcast(I32)
+            )

@@ -27,31 +27,31 @@ def tile_picked_wsagecat_max_lo_kernel(
     with ExitStack() as ctx:
         lists_pool = ctx.enter_context(tc.tile_pool(name="lists", bufs=1))
         sb = ctx.enter_context(tc.tile_pool(name="sb", bufs=1))
+        shared = ctx.enter_context(tc.tile_pool(name="shared", bufs=1))
         psum = ctx.enter_context(tc.psum_pool(name="psum", bufs=1))
 
         def new_tile(name, shape, dtype):
             return sb.tile(shape, dtype, name=name, align_bytes=64)
+
+        def tile_at(name, shape, dtype, offset):
+            return shared.tile(shape, dtype, name=name, align_bytes=64, offset=offset)
 
         def quantize(codes, scales, src):
             nc.vector.quantize_mx(out=codes.bitcast(FP8X4), scales=scales, in_=src)
 
         xs = new_tile("xs", [P, T], U8)
         nc.vector.memset(xs[:].bitcast(I32), 0)
-        warm = new_tile("warm", [P, 8], F32)
-        warm_out = new_tile("warm_out", [P, 8], F32)
-        nc.vector.memset(warm[:], 0.0)
 
         w1_rows = w1.rearrange("(p j) c -> p j c", j=PACK)
-        w1_raw = [new_tile("w1_raw%d" % c, [P, PACK, 256], F32) for c in range(2)]
+        w1_raw = [new_tile("w1_raw%d" % c, [P, 2, H], F32) for c in range(2)]
         for c in range(2):
-            nc.sync.dma_start(out=w1_raw[c][:], in_=w1_rows[:, :, 256 * c : 256 * (c + 1)])
+            nc.sync.dma_start(out=w1_raw[c][:], in_=w1_rows[:, 2 * c : 2 * c + 2, :])
         xw = new_tile("xw", [P, 2 * T], U8)
         nc.sync.dma_start(out=xw[:].bitcast(I32), in_=x_words[0].bitcast(I32))
         for q in range(4):
             nc.scalar.dma_start(
                 out=xs[32 * q : 32 * q + 4, :].bitcast(I32), in_=x_scales[0, 4 * q : 4 * q + 4, :].bitcast(I32)
             )
-        nc.scalar.activation(warm_out[:], warm[:], RELU)
         lists = []
         for d, pos in enumerate((pos1, pos2, pos3, pos4)):
             offsets = lists_pool.tile([P, T // 16], U16, name="pos%d" % d)
@@ -59,7 +59,7 @@ def tile_picked_wsagecat_max_lo_kernel(
             lists.append(offsets)
         w_raw = []
         for n, w in enumerate((w2, w3)):
-            raw = new_tile("w_raw%d" % n, [P, PACK, H], F32)
+            raw = tile_at("w_raw%d" % n, [P, PACK, H], F32, 8192 * n)
             rows = w.rearrange("(q s r) c -> s q r c", s=PACK, r=8)
             for s in range(PACK):
                 nc.sync.dma_start(out=raw[:, s, :], in_=rows[s])
@@ -73,17 +73,31 @@ def tile_picked_wsagecat_max_lo_kernel(
         w1_scales = [new_tile("w1_scales%d" % t, [P, P], U8) for t in range(PACK)]
 
         def round_w1(c, t, copy):
-            src = w1_raw[c][:].rearrange("p j (q t a l) -> p t q a j l", t=PACK, a=2, l=4)[:, t]
-            dst = w1_bf[t][:, 256 * c : 256 * (c + 1)].rearrange("p (q a l j) -> p q a j l", a=2, l=4, j=PACK)
+            src = w1_raw[c][:].rearrange("p j (q t r) -> p t q r j", t=PACK, r=8)[:, t]
+            dst = w1_bf[t][:].rearrange("p (q r c j) -> p c q r j", r=8, c=2, j=2)[:, c]
             copy(out=dst, in_=src)
 
         for t in range(PACK):
             round_w1(0, t, nc.vector.tensor_copy)
         for t in range(PACK):
             round_w1(1, t, nc.vector.tensor_copy if t % 2 == 0 else nc.scalar.copy)
-        h = new_tile("h", [P, PACK, T], F32)
+        h_wide = new_tile("h_wide", [P, PACK, 704], F32)
+        nc.gpsimd.memset(h_wide[:, :, T:704], 0.0)
+        h = h_wide[:, :, 0:T]
         for t in range(PACK):
             quantize(w1_codes[t][:], w1_scales[t][:], w1_bf[t][:])
+            if t == 0:
+                pieces = [(0, 256), (256, 128), (384, 128)]
+                for bank, (c0, n) in zip(banks_q, pieces):
+                    nc.tensor.matmul_mx(
+                        out=bank[:, 0:n], lhsT=w1_codes[t][:].bitcast(FP8X4), lhsT_scale=w1_scales[t][:],
+                        rhs=xw[:, 2 * c0 : 2 * (c0 + n)].bitcast(FP4X4), rhs_scale=xs[:, c0 : c0 + n],
+                        start=True, stop=True,
+                    )
+                nc.scalar.activation(h[:, 0, 0:256], banks_q[0][:, 0:256], RELU)
+                nc.vector.tensor_scalar_max(h[:, 0, 256:384], banks_q[1][:, 0:128], 0.0)
+                nc.scalar.activation(h[:, 0, 384:512], banks_q[2][:, 0:128], RELU)
+                continue
             nc.tensor.matmul_mx(
                 out=banks_p[t][:], lhsT=w1_codes[t][:].bitcast(FP8X4), lhsT_scale=w1_scales[t][:],
                 rhs=xw[:].bitcast(FP4X4), rhs_scale=xs[:], start=True, stop=True,
@@ -93,7 +107,7 @@ def tile_picked_wsagecat_max_lo_kernel(
         h_bf = new_tile("h_bf", [P, PACK * T], BF16)
         nc.scalar.copy(
             out=h_bf[:].rearrange("p (c i t) -> p c t i", i=4, t=PACK),
-            in_=h[:].rearrange("p t (c i) -> p c t i", i=4),
+            in_=h.rearrange("p t (c i) -> p c t i", i=4),
         )
         w_bf = []
         for n in range(2):
@@ -108,29 +122,29 @@ def tile_picked_wsagecat_max_lo_kernel(
         w_codes = [new_tile("w_codes%d" % n, [P, H], U32) for n in range(2)]
         w_scales = [new_tile("w_scales%d" % n, [P, H], U8) for n in range(2)]
 
-        chunks = [(0, 256), (256, 128), (384, 128)]
+        chunks = [(0, 128), (128, 256), (384, 128)]
         y_words = new_tile("y_words", [P, T], U32)
         y_scales = new_tile("y_scales", [P, T], U8)
         out_rows = out_0.rearrange("(p t) v -> p t v", t=PACK)
         out_words = out_1[0].rearrange("p c r -> p (c r)").bitcast(I32)
 
-        def planes(ap):
-            return ap.rearrange("p (u t v) -> p u t v", u=2, t=PACK)
+        def planes(ap, runs):
+            return ap.rearrange("p (u t v) -> p u t v", u=runs, t=PACK)
 
-        def gather(ci, d, dst):
-            v0, n = chunks[ci]
-            for t in range(PACK):
+        def gather(v0, n, d, dst, ts=range(PACK)):
+            for k, t in enumerate(ts):
                 nc.vector.tensor_copy(
-                    out=planes(dst)[:, :, t, :], in_=h[:, t, :].indirect(lists[d][:, v0 // 16 : (v0 + n) // 16])
+                    out=dst[:, :, k, :],
+                    in_=(h_wide if n == T else h)[:, t, :].indirect(lists[d][:, v0 // 16 : (v0 + n) // 16]),
                 )
 
-        def fold(acc, other):
-            nc.vector.tensor_tensor(acc, acc, other, MAX)
+        def fold(dst, acc, other):
+            nc.vector.tensor_tensor(dst, acc, other, MAX)
 
-        def weave_z(copy, dst, src):
+        def weave_z(copy, dst, src, runs):
             copy(
-                out=dst.rearrange("p (u c i t) -> p u c t i", u=2, i=4, t=PACK),
-                in_=src.rearrange("p (u t c i) -> p u c t i", u=2, i=4, t=PACK),
+                out=dst.rearrange("p (u c i t) -> p u c t i", u=runs, i=4, t=PACK),
+                in_=src.rearrange("p (u t c i) -> p u c t i", u=runs, i=4, t=PACK),
             )
 
         def own_pass(ci, banks):
@@ -177,55 +191,53 @@ def tile_picked_wsagecat_max_lo_kernel(
         y_bf = [new_tile("y_bf%d" % ci, [P, PACK * n], BF16) for ci, (v0, n) in enumerate(chunks)]
         on_scalar = [nc.scalar.copy] * PACK
 
-        z_a = new_tile("z_a", [P, 1024], BF16)
-        g_a = [new_tile("g_a%d" % i, [P, 1024], BF16) for i in range(2)]
-        gather(0, 0, z_a[:])
-        gather(0, 1, g_a[0][:])
-        fold(z_a[:], g_a[0][:])
-        gather(0, 2, g_a[1][:])
+        g0 = new_tile("g0", [P, 2048], BF16)
+        g1 = new_tile("g1", [P, 2048], BF16)
+        g2 = new_tile("g2", [P, 1536], BF16)
+        g3 = tile_at("g3", [P, 1536], BF16, 0)
+        z_three = tile_at("z_three", [P, 1536], BF16, 3072)
+        z_a = tile_at("z_a", [P, 1536], BF16, 8192)
+        c0 = tile_at("c0", [P, 256], BF16, 8192 + 3072)
+        gather(0, T, 0, planes(g0[:], 4))
+        gather(0, T, 1, planes(g1[:], 4))
+        fold(g1[:], g0[:], g1[:])
+        gather(0, 384, 2, planes(g2[:], 3))
         quantize(h_codes[:], h_scales[:], h_bf[:])
-        fold(z_a[:], g_a[1][:])
-        gather(0, 3, g_a[0][:])
+        fold(z_three[:], g1[:, 0:1536], g2[:])
         quantize(w_codes[0][:], w_scales[0][:], w_bf[0][:])
-        fold(z_a[:], g_a[0][:])
         own_pass(0, banks_q)
         own_pass(1, banks_p)
-        weave_z(nc.scalar.copy, z_bf[0][:], z_a[:])
-        z_b = new_tile("z_b", [P, 512], BF16)
-        g_b = new_tile("g_b", [P, 512], BF16)
-        gather(1, 0, z_b[:])
+        gather(0, 384, 3, planes(g3[:], 3))
         quantize(w_codes[1][:], w_scales[1][:], w_bf[1][:])
-        gather(1, 1, g_b[:])
-        fold(z_b[:], g_b[:])
+        fold(z_a[:, 0:512], z_three[:, 0:512], g3[:, 0:512])
+        fold(z_a[:, 512:1536], z_three[:, 512:1536], g3[:, 512:1536])
+        weave_z(nc.scalar.copy, z_bf[0][:], z_a[:, 0:512], 1)
+        weave_z(nc.scalar.copy, z_bf[1][:], z_a[:, 512:1536], 2)
+        c2 = [ap.rearrange("p (u t v) -> p u t v", u=2, t=2) for ap in (c0[:], z_a[:, 0:256])]
+        z_c, c3 = z_a[:, 512:1024], z_a[:, 1024:1536]
+        z_two = g1[:, 1536:2048].rearrange("p (t u v) -> p u t v", t=PACK, u=2)
+        gather(384, 128, 2, c2[0], (0, 1))
         quantize(z_codes[0][:], z_scales[0][:], z_bf[0][:])
-        neighbour_pass(0, banks_q, z_codes[0], z_scales[0])
-        lo, hi = z_bf[0][:, 0:512], z_bf[0][:, 512:1024]
-        gather(1, 2, lo)
-        fold(z_b[:], lo)
-        gather(1, 3, hi)
-        fold(z_b[:], hi)
-        result_out(0, banks_q, y[0], on_scalar)
-        weave_z(nc.scalar.copy, z_bf[1][:], z_b[:])
-        weave_y(nc.scalar.copy, y_bf[0], y[0])
-        own_pass(2, banks_q)
-        gather(2, 0, lo)
-        gather(2, 1, hi)
-        fold(lo, hi)
+        gather(384, 128, 2, c2[1], (2, 3))
         quantize(z_codes[1][:], z_scales[1][:], z_bf[1][:])
+        for a in range(2):
+            fold(planes(z_c, 2)[:, :, 2 * a : 2 * a + 2, :], z_two[:, :, 2 * a : 2 * a + 2, :], c2[a])
+        neighbour_pass(0, banks_q, z_codes[0], z_scales[0])
         neighbour_pass(1, banks_p, z_codes[1], z_scales[1])
+        result_out(0, banks_q, y[0], on_scalar)
+        own_pass(2, banks_q)
+        weave_y(nc.scalar.copy, y_bf[0], y[0])
         result_out(1, banks_p, y[1], on_scalar)
         weave_y(nc.scalar.copy, y_bf[1], y[1])
-        gather(2, 2, z_bf[1][:])
-        fold(lo, z_bf[1][:])
-        gather(2, 3, hi)
-        for t in range(PACK):
-            fold(planes(lo)[:, :, t, :], planes(hi)[:, :, t, :])
+        gather(384, 128, 3, planes(c3, 2))
+        for ts in range(PACK):
+            fold(planes(z_c, 2)[:, :, ts, :], planes(z_c, 2)[:, :, ts, :], planes(c3, 2)[:, :, ts, :])
         result_planes(0, y_bf[0])
-        weave_z(nc.vector.tensor_copy, z_bf[2][:], lo)
+        weave_z(nc.vector.tensor_copy, z_bf[2][:], z_c, 2)
         result_planes(1, y_bf[1])
         quantize(z_codes[2][:], z_scales[2][:], z_bf[2][:])
         neighbour_pass(2, banks_q, z_codes[2], z_scales[2])
-        result_out(2, banks_q, y[2], [nc.scalar.copy, nc.vector.tensor_copy] * 2)
+        result_out(2, banks_q, y[2], [nc.vector.tensor_copy, nc.scalar.copy] * 2)
         weave_y(nc.vector.tensor_copy, y_bf[2], y[2])
         result_planes(2, y_bf[2])
         for q in range(4):

@@ -118,11 +118,10 @@ def tile_picked_wsagecat_max_lo_kernel(
             )
             w_bf.append(wb)
         h_codes = new_tile("h_codes", [P, T], U32)
-        h_scales = new_tile("h_scales", [P, T], U8)
+        h_scales = tile_at("h_scales", [P, T], U8, 16384)
         w_codes = [new_tile("w_codes%d" % n, [P, H], U32) for n in range(2)]
-        w_scales = [new_tile("w_scales%d" % n, [P, H], U8) for n in range(2)]
+        w_scales = [tile_at("w_scales%d" % n, [P, H], U8, 17408 + 512 * n) for n in range(2)]
 
-        chunks = [(0, 128), (128, 256), (384, 128)]
         y_words = new_tile("y_words", [P, T], U32)
         y_scales = new_tile("y_scales", [P, T], U8)
         out_rows = out_0.rearrange("(p t) v -> p t v", t=PACK)
@@ -131,10 +130,10 @@ def tile_picked_wsagecat_max_lo_kernel(
         def planes(ap, runs):
             return ap.rearrange("p (u t v) -> p u t v", u=runs, t=PACK)
 
-        def gather(v0, n, d, dst, ts=range(PACK)):
-            for k, t in enumerate(ts):
+        def gather(v0, n, d, dst):
+            for t in range(PACK):
                 nc.vector.tensor_copy(
-                    out=dst[:, :, k, :],
+                    out=dst[:, :, t, :],
                     in_=(h_wide if n == T else h)[:, t, :].indirect(lists[d][:, v0 // 16 : (v0 + n) // 16]),
                 )
 
@@ -147,99 +146,91 @@ def tile_picked_wsagecat_max_lo_kernel(
                 in_=src.rearrange("p (u t c i) -> p u c t i", u=runs, i=4, t=PACK),
             )
 
-        def own_pass(ci, banks):
-            v0, n = chunks[ci]
-            for t in range(PACK):
-                cols = slice(P * t, P * (t + 1))
-                nc.tensor.matmul_mx(
-                    out=banks[t][:, 0:n], lhsT=w_codes[0][:, cols].bitcast(FP8X4), lhsT_scale=w_scales[0][:, cols],
-                    rhs=h_codes[:, v0 : v0 + n].bitcast(FP8X4), rhs_scale=h_scales[:, v0 : v0 + n],
-                    start=True, stop=False,
-                )
-
-        def neighbour_pass(ci, banks, z_codes, z_scales):
-            n = chunks[ci][1]
-            for t in range(PACK):
-                cols = slice(P * t, P * (t + 1))
-                nc.tensor.matmul_mx(
-                    out=banks[t][:, 0:n], lhsT=w_codes[1][:, cols].bitcast(FP8X4), lhsT_scale=w_scales[1][:, cols],
-                    rhs=z_codes[:].bitcast(FP8X4), rhs_scale=z_scales[:],
-                    start=False, stop=True,
-                )
-
-        def result_out(ci, banks, y, copies):
-            v0, n = chunks[ci]
-            for t in range(PACK):
-                copies[t](out=y[:, t, :], in_=banks[t][:, 0:n])
-            nc.sync.dma_start(out=out_rows[:, :, v0 : v0 + n], in_=y[:])
-
-        def weave_y(copy, dst, y):
-            copy(
-                out=dst[:].rearrange("p (c i t) -> p c t i", i=4, t=PACK),
-                in_=y[:].rearrange("p t (c i) -> p c t i", i=4),
+        def own_pass(out, t, v0):
+            cols = slice(P * t, P * (t + 1))
+            nc.tensor.matmul_mx(
+                out=out, lhsT=w_codes[0][:, cols].bitcast(FP8X4), lhsT_scale=w_scales[0][:, cols],
+                rhs=h_codes[:, v0 : v0 + P].bitcast(FP8X4), rhs_scale=h_scales[:, v0 : v0 + P],
+                start=True, stop=False,
             )
 
-        def result_planes(ci, y_bf):
-            v0, n = chunks[ci]
-            quantize(y_words[:, v0 : v0 + n], y_scales[:, v0 : v0 + n], y_bf[:])
+        def neighbour_pass(out, t, v0):
+            cols = slice(P * t, P * (t + 1))
+            nc.tensor.matmul_mx(
+                out=out, lhsT=w_codes[1][:, cols].bitcast(FP8X4), lhsT_scale=w_scales[1][:, cols],
+                rhs=z_codes[:, v0 : v0 + P].bitcast(FP8X4), rhs_scale=z_scales[:, v0 : v0 + P],
+                start=False, stop=True,
+            )
+
+        def result_planes(v0, n):
+            quantize(y_words[:, v0 : v0 + n], y_scales[:, v0 : v0 + n], y_bf[:, PACK * v0 : PACK * (v0 + n)])
             nc.sync.dma_start(out=out_words[:, v0 : v0 + n], in_=y_words[:, v0 : v0 + n].bitcast(I32))
 
-        z_codes = [new_tile("z_codes%d" % ci, [P, n], U32) for ci, (v0, n) in enumerate(chunks)]
-        z_scales = [new_tile("z_scales%d" % ci, [P, n], U8) for ci, (v0, n) in enumerate(chunks)]
-        z_bf = [new_tile("z_bf%d" % ci, [P, PACK * n], BF16) for ci, (v0, n) in enumerate(chunks)]
-        y = [new_tile("y%d" % ci, [P, PACK, n], F32) for ci, (v0, n) in enumerate(chunks)]
-        y_bf = [new_tile("y_bf%d" % ci, [P, PACK * n], BF16) for ci, (v0, n) in enumerate(chunks)]
-        on_scalar = [nc.scalar.copy] * PACK
+        z_codes = new_tile("z_codes", [P, T], U32)
+        z_scales = new_tile("z_scales", [P, T], U8)
+        z_bf = tile_at("z_bf", [P, PACK * 384], BF16, 8192)
+        z_bf_last = new_tile("z_bf_last", [P, PACK * P], BF16)
+        y = [new_tile("y%d" % ci, [P, PACK, P], F32) for ci in range(4)]
+        y_bf = new_tile("y_bf", [P, PACK * T], BF16)
 
         g0 = new_tile("g0", [P, 2048], BF16)
         g1 = new_tile("g1", [P, 2048], BF16)
         g2 = new_tile("g2", [P, 1536], BF16)
-        g3 = tile_at("g3", [P, 1536], BF16, 0)
-        z_three = tile_at("z_three", [P, 1536], BF16, 3072)
-        z_a = tile_at("z_a", [P, 1536], BF16, 8192)
-        c0 = tile_at("c0", [P, 256], BF16, 8192 + 3072)
+        g3 = new_tile("g3", [P, 1536], BF16)
         gather(0, T, 0, planes(g0[:], 4))
         gather(0, T, 1, planes(g1[:], 4))
-        fold(g1[:], g0[:], g1[:])
         gather(0, 384, 2, planes(g2[:], 3))
-        quantize(h_codes[:], h_scales[:], h_bf[:])
-        fold(z_three[:], g1[:, 0:1536], g2[:])
-        quantize(w_codes[0][:], w_scales[0][:], w_bf[0][:])
-        own_pass(0, banks_q)
-        own_pass(1, banks_p)
         gather(0, 384, 3, planes(g3[:], 3))
+        fold(g1[:], g0[:], g1[:])
+        fa = tile_at("fa", [P, 512], BF16, 16384)
+        fb = tile_at("fb", [P, 1024], BF16, 17408)
+        fold(fa[:], g2[:, 0:512], g3[:, 0:512])
+        fold(fb[:], g2[:, 512:1536], g3[:, 512:1536])
+        fold(g2[:, 0:512], g1[:, 0:512], fa[:])
+        fold(g2[:, 512:1536], g1[:, 512:1536], fb[:])
+        weave_z(nc.scalar.copy, z_bf[:, 0:512], g2[:, 0:512], 1)
+        weave_z(nc.scalar.copy, z_bf[:, 512:1536], g2[:, 512:1536], 2)
+        quantize(h_codes[:], h_scales[:], h_bf[:])
+        quantize(w_codes[0][:], w_scales[0][:], w_bf[0][:])
         quantize(w_codes[1][:], w_scales[1][:], w_bf[1][:])
-        fold(z_a[:, 0:512], z_three[:, 0:512], g3[:, 0:512])
-        fold(z_a[:, 512:1536], z_three[:, 512:1536], g3[:, 512:1536])
-        weave_z(nc.scalar.copy, z_bf[0][:], z_a[:, 0:512], 1)
-        weave_z(nc.scalar.copy, z_bf[1][:], z_a[:, 512:1536], 2)
-        c2 = [ap.rearrange("p (u t v) -> p u t v", u=2, t=2) for ap in (c0[:], z_a[:, 0:256])]
-        z_c, c3 = z_a[:, 512:1024], z_a[:, 1024:1536]
+        quantize(z_codes[:, 0:128], z_scales[:, 0:128], z_bf[:, 0:512])
+        quantize(z_codes[:, 128:384], z_scales[:, 128:384], z_bf[:, 512:1536])
+        for ci in range(3):
+            v0 = P * ci
+            bank = banks_p[ci]
+            for t in range(PACK):
+                own_pass(bank[:, P * t : P * (t + 1)], t, v0)
+                neighbour_pass(bank[:, P * t : P * (t + 1)], t, v0)
+            nc.scalar.copy(
+                out=y_bf[:, PACK * v0 : PACK * (v0 + P)].rearrange("p (v t) -> p v t", t=PACK),
+                in_=bank[:].rearrange("p (t v) -> p v t", t=PACK),
+            )
+            nc.scalar.copy(out=y[ci][:].rearrange("p t v -> p (t v)"), in_=bank[:])
+            nc.sync.dma_start(out=out_rows[:, :, v0 : v0 + P], in_=y[ci][:])
+        for t in range(PACK):
+            own_pass(banks_q[t][:, 0:P], t, 384)
+        c2, c3 = planes(g2[:, 512:1024], 2), planes(g2[:, 1024:1536], 2)
         z_two = g1[:, 1536:2048].rearrange("p (t u v) -> p u t v", t=PACK, u=2)
-        gather(384, 128, 2, c2[0], (0, 1))
-        quantize(z_codes[0][:], z_scales[0][:], z_bf[0][:])
-        gather(384, 128, 2, c2[1], (2, 3))
-        quantize(z_codes[1][:], z_scales[1][:], z_bf[1][:])
-        for a in range(2):
-            fold(planes(z_c, 2)[:, :, 2 * a : 2 * a + 2, :], z_two[:, :, 2 * a : 2 * a + 2, :], c2[a])
-        neighbour_pass(0, banks_q, z_codes[0], z_scales[0])
-        neighbour_pass(1, banks_p, z_codes[1], z_scales[1])
-        result_out(0, banks_q, y[0], on_scalar)
-        own_pass(2, banks_q)
-        weave_y(nc.scalar.copy, y_bf[0], y[0])
-        result_out(1, banks_p, y[1], on_scalar)
-        weave_y(nc.scalar.copy, y_bf[1], y[1])
-        gather(384, 128, 3, planes(c3, 2))
-        for ts in range(PACK):
-            fold(planes(z_c, 2)[:, :, ts, :], planes(z_c, 2)[:, :, ts, :], planes(c3, 2)[:, :, ts, :])
-        result_planes(0, y_bf[0])
-        weave_z(nc.vector.tensor_copy, z_bf[2][:], z_c, 2)
-        result_planes(1, y_bf[1])
-        quantize(z_codes[2][:], z_scales[2][:], z_bf[2][:])
-        neighbour_pass(2, banks_q, z_codes[2], z_scales[2])
-        result_out(2, banks_q, y[2], [nc.vector.tensor_copy, nc.scalar.copy] * 2)
-        weave_y(nc.vector.tensor_copy, y_bf[2], y[2])
-        result_planes(2, y_bf[2])
+        gather(384, 128, 2, c2)
+        gather(384, 128, 3, c3)
+        fold(c2, z_two, c2)
+        fold(c2[:, :, 0:3, :], c2[:, :, 0:3, :], c3[:, :, 0:3, :])
+        fold(c2[:, :, 3, :], c2[:, :, 3, :], c3[:, :, 3, :])
+        weave_z(nc.vector.tensor_copy, z_bf_last[:], g2[:, 512:1024], 2)
+        quantize(z_codes[:, 384:512], z_scales[:, 384:512], z_bf_last[:])
+        result_planes(0, 256)
+        result_planes(256, 128)
+        for t in range(PACK):
+            neighbour_pass(banks_q[t][:, 0:P], t, 384)
+        for t in range(PACK):
+            copy = nc.scalar.copy if t % 2 else nc.vector.tensor_copy
+            copy(out=y[3][:, t, :], in_=banks_q[t][:, 0:P])
+        nc.sync.dma_start(out=out_rows[:, :, 384:512], in_=y[3][:])
+        nc.vector.tensor_copy(
+            out=y_bf[:, PACK * 384 :].rearrange("p (c i t) -> p c t i", i=4, t=PACK),
+            in_=y[3][:].rearrange("p t (c i) -> p c t i", i=4),
+        )
+        result_planes(384, 128)
         for q in range(4):
             queue = nc.sync if q % 2 else nc.scalar
             queue.dma_start(

@@ -104,18 +104,46 @@ def tile_picked_wsagecat_max_lo_kernel(
             )
             nc.scalar.activation(h[:, t, :], banks_p[t][:], RELU)
 
+        def planes(ap, runs):
+            return ap.rearrange("p (u t v) -> p u t v", u=runs, t=PACK)
+
+        def gather(dst, t, d, v0, n):
+            nc.vector.tensor_copy(
+                out=dst, in_=(h_wide if n == T else h)[:, t, :].indirect(lists[d][:, v0 // 16 : (v0 + n) // 16])
+            )
+
+        PAD = P + 16
+        ga = new_tile("ga", [P, PACK, 4, PAD], BF16)
+        gb = new_tile("gb", [P, PACK, 4, PAD], BF16)
+        g1 = new_tile("g1", [P, 2048], BF16)
+        g2 = new_tile("g2", [P, 1536], BF16)
+        g3 = new_tile("g3", [P, 1536], BF16)
+        for t in range(PACK):
+            gather(ga[:, t, :, 0:P], t, 0, 0, T)
+            gather(gb[:, t, :, 0:P], t, 1, 0, T)
+            gather(planes(g2[:], 3)[:, :, t, :], t, 2, 0, 384)
+            gather(planes(g3[:], 3)[:, :, t, :], t, 3, 0, 384)
+        for t in range(PACK - 1):
+            diff = tile_at("diff%d" % t, [P, 4, P], F32, 20480 + 2048 * t)
+            rise = tile_at("rise%d" % t, [P, 4, P], F32, 20480 + 2048 * (t + 1))
+            nc.gpsimd.tensor_tensor(diff[:], gb[:, t, :, 0:P], ga[:, t, :, 0:P], mybir.AluOpType.subtract)
+            nc.scalar.activation(rise[:], diff[:], RELU)
+            nc.gpsimd.tensor_tensor(planes(g1[:], 4)[:, :, t, :], ga[:, t, :, 0:P], rise[:], mybir.AluOpType.add)
+
         h_bf = new_tile("h_bf", [P, PACK * T], BF16)
-        nc.scalar.copy(
-            out=h_bf[:].rearrange("p (c i t) -> p c t i", i=4, t=PACK),
-            in_=h.rearrange("p t (c i) -> p c t i", i=4),
-        )
+        for u in range(2):
+            nc.scalar.copy(
+                out=h_bf[:, 1024 * u : 1024 * (u + 1)].rearrange("p (c i t) -> p c t i", i=4, t=PACK),
+                in_=h[:, :, 256 * u : 256 * (u + 1)].rearrange("p t (c i) -> p c t i", i=4),
+            )
         w_bf = []
         for n in range(2):
             wb = new_tile("w_bf%d" % n, [P, PACK * H], BF16)
-            nc.scalar.copy(
-                out=wb[:].rearrange("p (t m s) -> p m t s", t=PACK, s=PACK),
-                in_=w_raw[n][:].rearrange("p s (m t) -> p m t s", t=PACK),
-            )
+            for u in range(2):
+                nc.scalar.copy(
+                    out=wb[:].rearrange("p (t m s) -> p m t s", t=PACK, s=PACK)[:, 64 * u : 64 * (u + 1)],
+                    in_=w_raw[n][:].rearrange("p s (m t) -> p m t s", t=PACK)[:, 64 * u : 64 * (u + 1)],
+                )
             w_bf.append(wb)
         h_codes = new_tile("h_codes", [P, T], U32)
         h_scales = tile_at("h_scales", [P, T], U8, 16384)
@@ -126,16 +154,6 @@ def tile_picked_wsagecat_max_lo_kernel(
         y_scales = new_tile("y_scales", [P, T], U8)
         out_rows = out_0.rearrange("(p t) v -> p t v", t=PACK)
         out_words = out_1[0].rearrange("p c r -> p (c r)").bitcast(I32)
-
-        def planes(ap, runs):
-            return ap.rearrange("p (u t v) -> p u t v", u=runs, t=PACK)
-
-        def gather(v0, n, d, dst):
-            for t in range(PACK):
-                nc.vector.tensor_copy(
-                    out=dst[:, :, t, :],
-                    in_=(h_wide if n == T else h)[:, t, :].indirect(lists[d][:, v0 // 16 : (v0 + n) // 16]),
-                )
 
         def fold(dst, acc, other):
             nc.vector.tensor_tensor(dst, acc, other, MAX)
@@ -158,7 +176,7 @@ def tile_picked_wsagecat_max_lo_kernel(
             cols = slice(P * t, P * (t + 1))
             nc.tensor.matmul_mx(
                 out=out, lhsT=w_codes[1][:, cols].bitcast(FP8X4), lhsT_scale=w_scales[1][:, cols],
-                rhs=z_codes[:, v0 : v0 + P].bitcast(FP8X4), rhs_scale=z_scales[:, v0 : v0 + P],
+                rhs=(z_codes[:, v0 : v0 + P] if v0 else z_codes_first[:]).bitcast(FP8X4), rhs_scale=z_scales[:, v0 : v0 + P],
                 start=False, stop=True,
             )
 
@@ -166,6 +184,7 @@ def tile_picked_wsagecat_max_lo_kernel(
             quantize(y_words[:, v0 : v0 + n], y_scales[:, v0 : v0 + n], y_bf[:, PACK * v0 : PACK * (v0 + n)])
             nc.sync.dma_start(out=out_words[:, v0 : v0 + n], in_=y_words[:, v0 : v0 + n].bitcast(I32))
 
+        z_codes_first = tile_at("z_codes_first", [P, P], U32, 28672)
         z_codes = new_tile("z_codes", [P, T], U32)
         z_scales = new_tile("z_scales", [P, T], U8)
         z_bf = tile_at("z_bf", [P, PACK * 384], BF16, 8192)
@@ -173,15 +192,7 @@ def tile_picked_wsagecat_max_lo_kernel(
         y = [new_tile("y%d" % ci, [P, PACK, P], F32) for ci in range(4)]
         y_bf = new_tile("y_bf", [P, PACK * T], BF16)
 
-        g0 = new_tile("g0", [P, 2048], BF16)
-        g1 = new_tile("g1", [P, 2048], BF16)
-        g2 = new_tile("g2", [P, 1536], BF16)
-        g3 = new_tile("g3", [P, 1536], BF16)
-        gather(0, T, 0, planes(g0[:], 4))
-        gather(0, T, 1, planes(g1[:], 4))
-        gather(0, 384, 2, planes(g2[:], 3))
-        gather(0, 384, 3, planes(g3[:], 3))
-        fold(g1[:], g0[:], g1[:])
+        fold(planes(g1[:], 4)[:, :, 3, :], ga[:, 3, :, 0:P], gb[:, 3, :, 0:P])
         fa = tile_at("fa", [P, 512], BF16, 16384)
         fb = tile_at("fb", [P, 1024], BF16, 17408)
         fold(fa[:], g2[:, 0:512], g3[:, 0:512])
@@ -193,7 +204,7 @@ def tile_picked_wsagecat_max_lo_kernel(
         quantize(h_codes[:], h_scales[:], h_bf[:])
         quantize(w_codes[0][:], w_scales[0][:], w_bf[0][:])
         quantize(w_codes[1][:], w_scales[1][:], w_bf[1][:])
-        quantize(z_codes[:, 0:128], z_scales[:, 0:128], z_bf[:, 0:512])
+        quantize(z_codes_first[:], z_scales[:, 0:128], z_bf[:, 0:512])
         quantize(z_codes[:, 128:384], z_scales[:, 128:384], z_bf[:, 512:1536])
         for ci in range(3):
             v0 = P * ci
@@ -209,10 +220,11 @@ def tile_picked_wsagecat_max_lo_kernel(
             nc.sync.dma_start(out=out_rows[:, :, v0 : v0 + P], in_=y[ci][:])
         for t in range(PACK):
             own_pass(banks_q[t][:, 0:P], t, 384)
-        c2, c3 = planes(g2[:, 512:1024], 2), planes(g2[:, 1024:1536], 2)
+        c2, c3 = planes(g2[:, 512:1024], 2), planes(tile_at("c3", [P, 512], BF16, 28672)[:], 2)
         z_two = g1[:, 1536:2048].rearrange("p (t u v) -> p u t v", t=PACK, u=2)
-        gather(384, 128, 2, c2)
-        gather(384, 128, 3, c3)
+        for d, dst in ((2, c2), (3, c3)):
+            for t in range(PACK):
+                gather(dst[:, :, t, :], t, d, 384, P)
         fold(c2, z_two, c2)
         fold(c2[:, :, 0:3, :], c2[:, :, 0:3, :], c3[:, :, 0:3, :])
         fold(c2[:, :, 3, :], c2[:, :, 3, :], c3[:, :, 3, :])

@@ -197,15 +197,23 @@ def tile_picked_wsagecat_max_lo_kernel(
         fb = tile_at("fb", [P, 1024], BF16, 17408)
         fold(fa[:], g2[:, 0:512], g3[:, 0:512])
         fold(fb[:], g2[:, 512:1536], g3[:, 512:1536])
-        fold(g2[:, 0:512], g1[:, 0:512], fa[:])
+        z0 = tile_at("z0", [P, 512], BF16, 30720)
+        fold(z0[:], g1[:, 0:512], fa[:])
         fold(g2[:, 512:1536], g1[:, 512:1536], fb[:])
-        weave_z(nc.scalar.copy, z_bf[:, 0:512], g2[:, 0:512], 1)
-        weave_z(nc.scalar.copy, z_bf[:, 512:1536], g2[:, 512:1536], 2)
+        for ci in range(3):
+            nc.scalar.copy(
+                out=z_bf[:, 512 * ci : 512 * (ci + 1)].rearrange("p (v t) -> p v t", t=PACK),
+                in_=(g2[:, 512 * ci : 512 * (ci + 1)] if ci else z0[:]).rearrange("p (t v) -> p v t", t=PACK),
+            )
         quantize(h_codes[:], h_scales[:], h_bf[:])
         quantize(w_codes[0][:], w_scales[0][:], w_bf[0][:])
         quantize(w_codes[1][:], w_scales[1][:], w_bf[1][:])
         quantize(z_codes_first[:], z_scales[:, 0:128], z_bf[:, 0:512])
-        quantize(z_codes[:, 128:384], z_scales[:, 128:384], z_bf[:, 512:1536])
+        quantize(z_codes[:, 128:256], z_scales[:, 128:256], z_bf[:, 512:1024])
+        c2_flat = tile_at("c2", [P, 512], BF16, 30720)
+        c2 = planes(c2_flat[:], 2)
+        gather(c2[:, :, 0, :], 0, 2, 384, P)
+        quantize(z_codes[:, 256:384], z_scales[:, 256:384], z_bf[:, 1024:1536])
         for ci in range(3):
             v0 = P * ci
             bank = banks_p[ci]
@@ -220,15 +228,15 @@ def tile_picked_wsagecat_max_lo_kernel(
             nc.sync.dma_start(out=out_rows[:, :, v0 : v0 + P], in_=y[ci][:])
         for t in range(PACK):
             own_pass(banks_q[t][:, 0:P], t, 384)
-        c2, c3 = planes(g2[:, 512:1024], 2), planes(tile_at("c3", [P, 512], BF16, 28672)[:], 2)
+        c3 = planes(tile_at("c3", [P, 512], BF16, 28672)[:], 2)
         z_two = g1[:, 1536:2048].rearrange("p (t u v) -> p u t v", t=PACK, u=2)
         for d, dst in ((2, c2), (3, c3)):
-            for t in range(PACK):
+            for t in range(1 if d == 2 else 0, PACK):
                 gather(dst[:, :, t, :], t, d, 384, P)
         fold(c2, z_two, c2)
         fold(c2[:, :, 0:3, :], c2[:, :, 0:3, :], c3[:, :, 0:3, :])
         fold(c2[:, :, 3, :], c2[:, :, 3, :], c3[:, :, 3, :])
-        weave_z(nc.vector.tensor_copy, z_bf_last[:], g2[:, 512:1024], 2)
+        weave_z(nc.vector.tensor_copy, z_bf_last[:], c2_flat[:], 2)
         quantize(z_codes[:, 384:512], z_scales[:, 384:512], z_bf_last[:])
         result_planes(0, 256)
         result_planes(256, 128)

@@ -116,12 +116,12 @@ def tile_picked_wsagecat_max_lo_kernel(
         ga = new_tile("ga", [P, PACK, 4, PAD], BF16)
         gb = new_tile("gb", [P, PACK, 4, PAD], BF16)
         g1 = new_tile("g1", [P, 2048], BF16)
-        g2 = new_tile("g2", [P, 1536], BF16)
+        g2 = new_tile("g2", [P, 2048], BF16)
         g3 = new_tile("g3", [P, 1536], BF16)
         for t in range(PACK):
             gather(ga[:, t, :, 0:P], t, 0, 0, T)
             gather(gb[:, t, :, 0:P], t, 1, 0, T)
-            gather(planes(g2[:], 3)[:, :, t, :], t, 2, 0, 384)
+            gather(planes(g2[:], 4)[:, :, t, :], t, 2, 0, T)
             gather(planes(g3[:], 3)[:, :, t, :], t, 3, 0, 384)
         for t in range(PACK - 1):
             diff = tile_at("diff%d" % t, [P, 4, P], F32, 20480 + 2048 * t)
@@ -146,7 +146,7 @@ def tile_picked_wsagecat_max_lo_kernel(
                 )
             w_bf.append(wb)
         h_codes = new_tile("h_codes", [P, T], U32)
-        h_scales = tile_at("h_scales", [P, T], U8, 16384)
+        h_scales = [tile_at("h_scales%d" % n, [P, 2 * P], U8, 16384 + 2048 * n) for n in range(2)]
         w_codes = [new_tile("w_codes%d" % n, [P, H], U32) for n in range(2)]
         w_scales = [tile_at("w_scales%d" % n, [P, H], U8, 17408 + 512 * n) for n in range(2)]
 
@@ -168,7 +168,7 @@ def tile_picked_wsagecat_max_lo_kernel(
             cols = slice(P * t, P * (t + 1))
             nc.tensor.matmul_mx(
                 out=out, lhsT=w_codes[0][:, cols].bitcast(FP8X4), lhsT_scale=w_scales[0][:, cols],
-                rhs=h_codes[:, v0 : v0 + P].bitcast(FP8X4), rhs_scale=h_scales[:, v0 : v0 + P],
+                rhs=h_codes[:, v0 : v0 + P].bitcast(FP8X4), rhs_scale=h_scales[v0 // 256][:, v0 % 256 : v0 % 256 + P],
                 start=True, stop=False,
             )
 
@@ -176,16 +176,15 @@ def tile_picked_wsagecat_max_lo_kernel(
             cols = slice(P * t, P * (t + 1))
             nc.tensor.matmul_mx(
                 out=out, lhsT=w_codes[1][:, cols].bitcast(FP8X4), lhsT_scale=w_scales[1][:, cols],
-                rhs=(z_codes[:, v0 : v0 + P] if v0 else z_codes_first[:]).bitcast(FP8X4), rhs_scale=z_scales[:, v0 : v0 + P],
+                rhs=z_codes[v0 // P][:].bitcast(FP8X4), rhs_scale=z_scales[:, v0 : v0 + P],
                 start=False, stop=True,
             )
 
         def result_planes(v0, n):
             quantize(y_words[:, v0 : v0 + n], y_scales[:, v0 : v0 + n], y_bf[:, PACK * v0 : PACK * (v0 + n)])
-            nc.sync.dma_start(out=out_words[:, v0 : v0 + n], in_=y_words[:, v0 : v0 + n].bitcast(I32))
 
-        z_codes_first = tile_at("z_codes_first", [P, P], U32, 28672)
-        z_codes = new_tile("z_codes", [P, T], U32)
+        z_codes = [new_tile("z_codes%d" % ci, [P, P], U32) for ci in range(2)]
+        z_codes.extend(tile_at("z_codes%d" % ci, [P, P], U32, 28672) for ci in (2, 3))
         z_scales = new_tile("z_scales", [P, T], U8)
         z_bf = tile_at("z_bf", [P, PACK * 384], BF16, 8192)
         z_bf_last = new_tile("z_bf_last", [P, PACK * P], BF16)
@@ -199,58 +198,72 @@ def tile_picked_wsagecat_max_lo_kernel(
         fold(fb[:], g2[:, 512:1536], g3[:, 512:1536])
         z0 = tile_at("z0", [P, 512], BF16, 30720)
         fold(z0[:], g1[:, 0:512], fa[:])
-        fold(g2[:, 512:1536], g1[:, 512:1536], fb[:])
+        z12 = tile_at("z12", [P, 1024], BF16, 31744)
+        fold(z12[:], g1[:, 512:1536], fb[:])
         for ci in range(3):
             nc.scalar.copy(
                 out=z_bf[:, 512 * ci : 512 * (ci + 1)].rearrange("p (v t) -> p v t", t=PACK),
-                in_=(g2[:, 512 * ci : 512 * (ci + 1)] if ci else z0[:]).rearrange("p (t v) -> p v t", t=PACK),
+                in_=(z12[:, 512 * (ci - 1) : 512 * ci] if ci else z0[:]).rearrange("p (t v) -> p v t", t=PACK),
             )
-        quantize(h_codes[:], h_scales[:], h_bf[:])
+        quantize(h_codes[:, 0:256], h_scales[0][:], h_bf[:, 0:1024])
         quantize(w_codes[0][:], w_scales[0][:], w_bf[0][:])
         quantize(w_codes[1][:], w_scales[1][:], w_bf[1][:])
-        quantize(z_codes_first[:], z_scales[:, 0:128], z_bf[:, 0:512])
-        quantize(z_codes[:, 128:256], z_scales[:, 128:256], z_bf[:, 512:1024])
-        c2_flat = tile_at("c2", [P, 512], BF16, 30720)
-        c2 = planes(c2_flat[:], 2)
-        gather(c2[:, :, 0, :], 0, 2, 384, P)
-        quantize(z_codes[:, 256:384], z_scales[:, 256:384], z_bf[:, 1024:1536])
-        for ci in range(3):
+        quantize(z_codes[0][:], z_scales[:, 0:128], z_bf[:, 0:512])
+        quantize(z_codes[1][:], z_scales[:, 128:256], z_bf[:, 512:1024])
+        quantize(h_codes[:, 256:512], h_scales[1][:], h_bf[:, 1024:2048])
+        z3 = tile_at("z3", [P, PACK, 2, 64], BF16, 30720)
+        fold(z3[:].rearrange("p t u v -> p (t u v)"), g1[:, 1536:2048], g2[:, 1536:2048])
+        quantize(z_codes[2][:], z_scales[:, 256:384], z_bf[:, 1024:1536])
+        for t in range(PACK):
+            own_pass(banks_q[t][:, 0:P], t, 0)
+        for t in range(PACK):
+            neighbour_pass(banks_q[t][:, 0:P], t, 0)
+            nc.scalar.copy(out=y[0][:, t, :], in_=banks_q[t][:, 0:P])
+        nc.sync.dma_start(out=out_rows[:, :, 0:P], in_=y[0][:])
+        nc.scalar.copy(
+            out=y_bf[:, 0 : PACK * P].rearrange("p (c i t) -> p c t i", i=4, t=PACK),
+            in_=y[0][:].rearrange("p t (c i) -> p c t i", i=4),
+        )
+        for ci in range(1, 3):
             v0 = P * ci
             bank = banks_p[ci]
             for t in range(PACK):
                 own_pass(bank[:, P * t : P * (t + 1)], t, v0)
                 neighbour_pass(bank[:, P * t : P * (t + 1)], t, v0)
-            nc.scalar.copy(
-                out=y_bf[:, PACK * v0 : PACK * (v0 + P)].rearrange("p (v t) -> p v t", t=PACK),
-                in_=bank[:].rearrange("p (t v) -> p v t", t=PACK),
-            )
             nc.scalar.copy(out=y[ci][:].rearrange("p t v -> p (t v)"), in_=bank[:])
             nc.sync.dma_start(out=out_rows[:, :, v0 : v0 + P], in_=y[ci][:])
+            if ci == 1:
+                nc.scalar.copy(
+                    out=y_bf[:, PACK * v0 : PACK * (v0 + P)].rearrange("p (v t) -> p v t", t=PACK),
+                    in_=bank[:].rearrange("p (t v) -> p v t", t=PACK),
+                )
         for t in range(PACK):
             own_pass(banks_q[t][:, 0:P], t, 384)
-        c3 = planes(tile_at("c3", [P, 512], BF16, 28672)[:], 2)
-        z_two = g1[:, 1536:2048].rearrange("p (t u v) -> p u t v", t=PACK, u=2)
-        for d, dst in ((2, c2), (3, c3)):
-            for t in range(1 if d == 2 else 0, PACK):
-                gather(dst[:, :, t, :], t, d, 384, P)
-        fold(c2, z_two, c2)
-        fold(c2[:, :, 0:3, :], c2[:, :, 0:3, :], c3[:, :, 0:3, :])
-        fold(c2[:, :, 3, :], c2[:, :, 3, :], c3[:, :, 3, :])
-        weave_z(nc.vector.tensor_copy, z_bf_last[:], c2_flat[:], 2)
-        quantize(z_codes[:, 384:512], z_scales[:, 384:512], z_bf_last[:])
+        gd3 = tile_at("gd3", [P, PACK, 2, 80], BF16, 31744)
+        for t in range(PACK):
+            gather(gd3[:, t, :, 0:64], t, 3, 384, P)
+        fold(z3[:, 0:3], z3[:, 0:3], gd3[:, 0:3, :, 0:64])
+        fold(z3[:, 3], z3[:, 3], gd3[:, 3, :, 0:64])
+        weave_z(nc.vector.tensor_copy, z_bf_last[:], z3[:].rearrange("p t u v -> p (t u v)"), 1)
+        quantize(z_codes[3][:], z_scales[:, 384:512], z_bf_last[:])
         result_planes(0, 256)
+        nc.sync.dma_start(out=out_words[:, 0:256], in_=y_words[:, 0:256].bitcast(I32))
+        nc.vector.tensor_copy(
+            out=y_bf[:, PACK * 256 : PACK * 384].rearrange("p (c i t) -> p c t i", i=4, t=PACK),
+            in_=y[2][:].rearrange("p t (c i) -> p c t i", i=4),
+        )
         result_planes(256, 128)
         for t in range(PACK):
             neighbour_pass(banks_q[t][:, 0:P], t, 384)
         for t in range(PACK):
-            copy = nc.scalar.copy if t % 2 else nc.vector.tensor_copy
-            copy(out=y[3][:, t, :], in_=banks_q[t][:, 0:P])
+            nc.scalar.copy(out=y[3][:, t, :], in_=banks_q[t][:, 0:P])
         nc.sync.dma_start(out=out_rows[:, :, 384:512], in_=y[3][:])
         nc.vector.tensor_copy(
             out=y_bf[:, PACK * 384 :].rearrange("p (c i t) -> p c t i", i=4, t=PACK),
             in_=y[3][:].rearrange("p t (c i) -> p c t i", i=4),
         )
         result_planes(384, 128)
+        nc.sync.dma_start(out=out_words[:, 256:512], in_=y_words[:, 256:512].bitcast(I32))
         for q in range(4):
             queue = nc.sync if q % 2 else nc.scalar
             queue.dma_start(

@@ -59,7 +59,7 @@ def tile_picked_wsagecat_max_lo_kernel(
             lists.append(offsets)
         w_raw = []
         for n, w in enumerate((w2, w3)):
-            raw = tile_at("w_raw%d" % n, [P, PACK, H], F32, 8192 * n)
+            raw = new_tile("w_raw%d" % n, [P, PACK, H], F32)
             rows = w.rearrange("(q s r) c -> s q r c", s=PACK, r=8)
             for s in range(PACK):
                 nc.sync.dma_start(out=raw[:, s, :], in_=rows[s])
@@ -80,7 +80,7 @@ def tile_picked_wsagecat_max_lo_kernel(
         for t in range(PACK):
             round_w1(0, t, nc.vector.tensor_copy)
         for t in range(PACK):
-            round_w1(1, t, nc.vector.tensor_copy if t % 2 == 0 else nc.scalar.copy)
+            round_w1(1, t, nc.vector.tensor_copy if t < 2 else nc.scalar.copy)
         h_wide = new_tile("h_wide", [P, PACK, 704], F32)
         nc.gpsimd.memset(h_wide[:, :, T:704], 0.0)
         h = h_wide[:, :, 0:T]
@@ -104,31 +104,35 @@ def tile_picked_wsagecat_max_lo_kernel(
             )
             nc.scalar.activation(h[:, t, :], banks_p[t][:], RELU)
 
-        def planes(ap, runs):
-            return ap.rearrange("p (u t v) -> p u t v", u=runs, t=PACK)
-
         def gather(dst, t, d, v0, n):
             nc.vector.tensor_copy(
                 out=dst, in_=(h_wide if n == T else h)[:, t, :].indirect(lists[d][:, v0 // 16 : (v0 + n) // 16])
             )
 
-        PAD = P + 16
-        ga = new_tile("ga", [P, PACK, 4, PAD], BF16)
-        gb = new_tile("gb", [P, PACK, 4, PAD], BF16)
-        g1 = new_tile("g1", [P, 2048], BF16)
-        g2 = new_tile("g2", [P, 2048], BF16)
-        g3 = new_tile("g3", [P, 1536], BF16)
+        g0 = [new_tile("g0_%d" % u, [P, T, 2], BF16) for u in range(2)]
+        g1 = [new_tile("g1_%d" % u, [P, T, 2], BF16) for u in range(2)]
+        g2 = new_tile("g2", [P, 2, T, 2], BF16)
+        g3 = new_tile("g3", [P, 2, 384, 2], BF16)
         for t in range(PACK):
-            gather(ga[:, t, :, 0:P], t, 0, 0, T)
-            gather(gb[:, t, :, 0:P], t, 1, 0, T)
-            gather(planes(g2[:], 4)[:, :, t, :], t, 2, 0, T)
-            gather(planes(g3[:], 3)[:, :, t, :], t, 3, 0, 384)
-        for t in range(PACK - 1):
-            diff = tile_at("diff%d" % t, [P, 4, P], F32, 20480 + 2048 * t)
-            rise = tile_at("rise%d" % t, [P, 4, P], F32, 20480 + 2048 * (t + 1))
-            nc.gpsimd.tensor_tensor(diff[:], gb[:, t, :, 0:P], ga[:, t, :, 0:P], mybir.AluOpType.subtract)
+            gather(g0[t // 2][:, :, t % 2], t, 0, 0, T)
+            gather(g1[t // 2][:, :, t % 2], t, 1, 0, T)
+        for t in range(PACK):
+            gather(g2[:, t // 2, :, t % 2], t, 2, 0, T)
+            gather(g3[:, t // 2, :, t % 2], t, 3, 0, 384)
+
+        def flat(ap):
+            return ap.rearrange("p v e -> p (v e)")
+
+        m01 = new_tile("m01", [P, 3, 512], BF16)
+        for u, n, at in ((0, 1024, 0), (1, 512, 4096)):
+            diff = tile_at("diff%d" % u, [P, n], F32, at)
+            rise = tile_at("rise%d" % u, [P, n], F32, at + 4096)
+            a = flat(g0[u][:])[:, 0:n]
+            b = flat(g1[u][:])[:, 0:n]
+            nc.gpsimd.tensor_tensor(diff[:], b, a, mybir.AluOpType.subtract)
             nc.scalar.activation(rise[:], diff[:], RELU)
-            nc.gpsimd.tensor_tensor(planes(g1[:], 4)[:, :, t, :], ga[:, t, :, 0:P], rise[:], mybir.AluOpType.add)
+            dst = m01[:].rearrange("p r c -> p (r c)")[:, 1024 * u : 1024 * u + n]
+            nc.gpsimd.tensor_tensor(dst, a, rise[:], mybir.AluOpType.add)
 
         h_bf = new_tile("h_bf", [P, PACK * T], BF16)
         for u in range(2):
@@ -138,7 +142,7 @@ def tile_picked_wsagecat_max_lo_kernel(
             )
         w_bf = []
         for n in range(2):
-            wb = new_tile("w_bf%d" % n, [P, PACK * H], BF16)
+            wb = tile_at("w_bf%d" % n, [P, PACK * H], BF16, 12288 + 4096 * n)
             for u in range(2):
                 nc.scalar.copy(
                     out=wb[:].rearrange("p (t m s) -> p m t s", t=PACK, s=PACK)[:, 64 * u : 64 * (u + 1)],
@@ -146,9 +150,9 @@ def tile_picked_wsagecat_max_lo_kernel(
                 )
             w_bf.append(wb)
         h_codes = new_tile("h_codes", [P, T], U32)
-        h_scales = [tile_at("h_scales%d" % n, [P, 2 * P], U8, 16384 + 2048 * n) for n in range(2)]
+        h_scales = [tile_at("h_scales0", [P, 2 * P], U8, 9216), tile_at("h_scales1", [P, 2 * P], U8, 20480)]
         w_codes = [new_tile("w_codes%d" % n, [P, H], U32) for n in range(2)]
-        w_scales = [tile_at("w_scales%d" % n, [P, H], U8, 17408 + 512 * n) for n in range(2)]
+        w_scales = [tile_at("w_scales%d" % n, [P, H], U8, 8192 + 512 * n) for n in range(2)]
 
         y_words = new_tile("y_words", [P, T], U32)
         y_scales = new_tile("y_scales", [P, T], U8)
@@ -158,112 +162,108 @@ def tile_picked_wsagecat_max_lo_kernel(
         def fold(dst, acc, other):
             nc.vector.tensor_tensor(dst, acc, other, MAX)
 
-        def weave_z(copy, dst, src, runs):
-            copy(
-                out=dst.rearrange("p (u c i t) -> p u c t i", u=runs, i=4, t=PACK),
-                in_=src.rearrange("p (u t c i) -> p u c t i", u=runs, i=4, t=PACK),
+        def fold_woven(dst, acc, other):
+            fold(
+                dst.rearrange("p (v u e) -> p v u e", u=2, e=2),
+                acc.rearrange("p u (v e) -> p v u e", e=2),
+                other.rearrange("p u v e -> p v u e"),
             )
 
-        def own_pass(out, t, v0):
+        z_codes = new_tile("z_codes", [P, T], U32)
+        z_scales = new_tile("z_scales", [P, T], U8)
+
+        def own_pass(out, t, v0, start):
             cols = slice(P * t, P * (t + 1))
             nc.tensor.matmul_mx(
                 out=out, lhsT=w_codes[0][:, cols].bitcast(FP8X4), lhsT_scale=w_scales[0][:, cols],
                 rhs=h_codes[:, v0 : v0 + P].bitcast(FP8X4), rhs_scale=h_scales[v0 // 256][:, v0 % 256 : v0 % 256 + P],
-                start=True, stop=False,
+                start=start, stop=False,
             )
 
-        def neighbour_pass(out, t, v0):
+        def neighbour_pass(out, t, v0, stop):
             cols = slice(P * t, P * (t + 1))
             nc.tensor.matmul_mx(
                 out=out, lhsT=w_codes[1][:, cols].bitcast(FP8X4), lhsT_scale=w_scales[1][:, cols],
-                rhs=z_codes[v0 // P][:].bitcast(FP8X4), rhs_scale=z_scales[:, v0 : v0 + P],
-                start=False, stop=True,
+                rhs=z_codes[:, v0 : v0 + P].bitcast(FP8X4), rhs_scale=z_scales[:, v0 : v0 + P],
+                start=False, stop=stop,
             )
 
         def result_planes(v0, n):
             quantize(y_words[:, v0 : v0 + n], y_scales[:, v0 : v0 + n], y_bf[:, PACK * v0 : PACK * (v0 + n)])
 
-        z_codes = [new_tile("z_codes%d" % ci, [P, P], U32) for ci in range(2)]
-        z_codes.extend(tile_at("z_codes%d" % ci, [P, P], U32, 28672) for ci in (2, 3))
-        z_scales = new_tile("z_scales", [P, T], U8)
-        z_bf = tile_at("z_bf", [P, PACK * 384], BF16, 8192)
-        z_bf_last = new_tile("z_bf_last", [P, PACK * P], BF16)
         y = [new_tile("y%d" % ci, [P, PACK, P], F32) for ci in range(4)]
         y_bf = new_tile("y_bf", [P, PACK * T], BF16)
 
-        fold(planes(g1[:], 4)[:, :, 3, :], ga[:, 3, :, 0:P], gb[:, 3, :, 0:P])
-        fa = tile_at("fa", [P, 512], BF16, 16384)
-        fb = tile_at("fb", [P, 1024], BF16, 17408)
-        fold(fa[:], g2[:, 0:512], g3[:, 0:512])
-        fold(fb[:], g2[:, 512:1536], g3[:, 512:1536])
-        z0 = tile_at("z0", [P, 512], BF16, 30720)
-        fold(z0[:], g1[:, 0:512], fa[:])
-        z12 = tile_at("z12", [P, 1024], BF16, 31744)
-        fold(z12[:], g1[:, 512:1536], fb[:])
-        for ci in range(3):
-            nc.scalar.copy(
-                out=z_bf[:, 512 * ci : 512 * (ci + 1)].rearrange("p (v t) -> p v t", t=PACK),
-                in_=(z12[:, 512 * (ci - 1) : 512 * ci] if ci else z0[:]).rearrange("p (t v) -> p v t", t=PACK),
-            )
-        quantize(h_codes[:, 0:256], h_scales[0][:], h_bf[:, 0:1024])
-        quantize(w_codes[0][:], w_scales[0][:], w_bf[0][:])
-        quantize(w_codes[1][:], w_scales[1][:], w_bf[1][:])
-        quantize(z_codes[0][:], z_scales[:, 0:128], z_bf[:, 0:512])
-        quantize(z_codes[1][:], z_scales[:, 128:256], z_bf[:, 512:1024])
-        quantize(h_codes[:, 256:512], h_scales[1][:], h_bf[:, 1024:2048])
-        z3 = tile_at("z3", [P, PACK, 2, 64], BF16, 30720)
-        fold(z3[:].rearrange("p t u v -> p (t u v)"), g1[:, 1536:2048], g2[:, 1536:2048])
-        quantize(z_codes[2][:], z_scales[:, 256:384], z_bf[:, 1024:1536])
-        for t in range(PACK):
-            own_pass(banks_q[t][:, 0:P], t, 0)
-        for t in range(PACK):
-            neighbour_pass(banks_q[t][:, 0:P], t, 0)
-            nc.scalar.copy(out=y[0][:, t, :], in_=banks_q[t][:, 0:P])
-        nc.sync.dma_start(out=out_rows[:, :, 0:P], in_=y[0][:])
-        nc.scalar.copy(
-            out=y_bf[:, 0 : PACK * P].rearrange("p (c i t) -> p c t i", i=4, t=PACK),
-            in_=y[0][:].rearrange("p t (c i) -> p c t i", i=4),
-        )
-        for ci in range(1, 3):
+        def own_passes(ci):
+            for t in range(PACK):
+                own_pass(banks_p[ci][:, P * t : P * (t + 1)], t, P * ci, t == 0)
+
+        def finish_chunk(ci):
             v0 = P * ci
             bank = banks_p[ci]
             for t in range(PACK):
-                own_pass(bank[:, P * t : P * (t + 1)], t, v0)
-                neighbour_pass(bank[:, P * t : P * (t + 1)], t, v0)
+                neighbour_pass(bank[:, P * t : P * (t + 1)], t, v0, t == PACK - 1)
             nc.scalar.copy(out=y[ci][:].rearrange("p t v -> p (t v)"), in_=bank[:])
             nc.sync.dma_start(out=out_rows[:, :, v0 : v0 + P], in_=y[ci][:])
-            if ci == 1:
-                nc.scalar.copy(
-                    out=y_bf[:, PACK * v0 : PACK * (v0 + P)].rearrange("p (v t) -> p v t", t=PACK),
-                    in_=bank[:].rearrange("p (t v) -> p v t", t=PACK),
-                )
+            nc.scalar.copy(
+                out=y_bf[:, PACK * v0 : PACK * (v0 + P)].rearrange("p (v t) -> p v t", t=PACK),
+                in_=bank[:].rearrange("p (t v) -> p v t", t=PACK),
+            )
+
+        g2f = g2[:].rearrange("p u v e -> p u (v e)")
+        a0 = tile_at("a0", [P, 2, 512], BF16, 20480)
+        fold(a0[:], m01[:, 0:3:2, :], g2f[:, :, 0:512])
+        quantize(w_codes[0][:], w_scales[0][:], w_bf[0][:])
+        z01 = new_tile("z01", [P, 1024], BF16)
+        fold_woven(z01[:], a0[:], g3[:, :, 0:256, :])
+        quantize(h_codes[:, 0:256], h_scales[0][:], h_bf[:, 0:1024])
+        quantize(w_codes[1][:], w_scales[1][:], w_bf[1][:])
+        quantize(z_codes[:, 0:256], z_scales[:, 0:256], z01[:])
+        own_passes(0)
+        own_passes(1)
+        finish_chunk(0)
+        finish_chunk(1)
+        b1 = tile_at("b1", [P, 512], BF16, 12288)
+        fold(b1[:], flat(g0[1][:])[:, 512:1024], flat(g1[1][:])[:, 512:1024])
+        a1 = tile_at("a1", [P, 2, 512], BF16, 16384)
+        fold(a1[:, 0, :], m01[:, 1, :], g2f[:, 0, 512:1024])
+        fold(a1[:, 1, :], b1[:], g2f[:, 1, 512:1024])
+        quantize(h_codes[:, 256:512], h_scales[1][:], h_bf[:, 1024:2048])
+        z2 = new_tile("z2", [P, 512], BF16)
+        fold_woven(z2[:], a1[:, :, 0:256], g3[:, :, 256:384, :])
+        quantize(z_codes[:, 256:384], z_scales[:, 256:384], z2[:])
+        own_passes(2)
         for t in range(PACK):
-            own_pass(banks_q[t][:, 0:P], t, 384)
-        gd3 = tile_at("gd3", [P, PACK, 2, 80], BF16, 31744)
-        for t in range(PACK):
-            gather(gd3[:, t, :, 0:64], t, 3, 384, P)
-        fold(z3[:, 0:3], z3[:, 0:3], gd3[:, 0:3, :, 0:64])
-        fold(z3[:, 3], z3[:, 3], gd3[:, 3, :, 0:64])
-        weave_z(nc.vector.tensor_copy, z_bf_last[:], z3[:].rearrange("p t u v -> p (t u v)"), 1)
-        quantize(z_codes[3][:], z_scales[:, 384:512], z_bf_last[:])
+            own_pass(banks_q[t // 2][:, P * (t % 2) : P * (t % 2 + 1)], t, 384, t % 2 == 0)
+        finish_chunk(2)
+        g3_last = tile_at("g3_last", [P, 2, P, 2], BF16, 21504)
+        for t in (0, 2, 1, 3):
+            gather(g3_last[:, t // 2, :, t % 2], t, 3, 384, P)
+        z3 = new_tile("z3", [P, 512], BF16)
+        fold_woven(z3[:], a1[:, :, 256:512], g3_last[:])
+        quantize(z_codes[:, 384:512], z_scales[:, 384:512], z3[:])
         result_planes(0, 256)
-        nc.sync.dma_start(out=out_words[:, 0:256], in_=y_words[:, 0:256].bitcast(I32))
-        nc.vector.tensor_copy(
-            out=y_bf[:, PACK * 256 : PACK * 384].rearrange("p (c i t) -> p c t i", i=4, t=PACK),
-            in_=y[2][:].rearrange("p t (c i) -> p c t i", i=4),
-        )
         result_planes(256, 128)
+        nc.sync.dma_start(out=out_words[:, 0:384], in_=y_words[:, 0:384].bitcast(I32))
         for t in range(PACK):
-            neighbour_pass(banks_q[t][:, 0:P], t, 384)
-        for t in range(PACK):
-            nc.scalar.copy(out=y[3][:, t, :], in_=banks_q[t][:, 0:P])
+            neighbour_pass(banks_q[t // 2][:, P * (t % 2) : P * (t % 2 + 1)], t, 384, t % 2 == 1)
+
+        def weave_pair(u):
+            nc.vector.tensor_copy(
+                out=y_bf[:, PACK * 384 :].rearrange("p (v u e) -> p u v e", u=2, e=2)[:, u],
+                in_=banks_q[u][:, 0 : 2 * P].rearrange("p (e v) -> p v e", e=2),
+            )
+
+        def copy_pair(u):
+            nc.scalar.copy(out=y[3][:, 2 * u : 2 * u + 2, :].rearrange("p t v -> p (t v)"), in_=banks_q[u][:, 0 : 2 * P])
+
+        weave_pair(0)
+        copy_pair(1)
+        copy_pair(0)
+        weave_pair(1)
         nc.sync.dma_start(out=out_rows[:, :, 384:512], in_=y[3][:])
-        nc.vector.tensor_copy(
-            out=y_bf[:, PACK * 384 :].rearrange("p (c i t) -> p c t i", i=4, t=PACK),
-            in_=y[3][:].rearrange("p t (c i) -> p c t i", i=4),
-        )
         result_planes(384, 128)
-        nc.sync.dma_start(out=out_words[:, 256:512], in_=y_words[:, 256:512].bitcast(I32))
+        nc.sync.dma_start(out=out_words[:, 384:512], in_=y_words[:, 384:512].bitcast(I32))
         for q in range(4):
             queue = nc.sync if q % 2 else nc.scalar
             queue.dma_start(

@@ -211,17 +211,30 @@ def tile_picked_wsagecat_max_lo_kernel(
             )
 
         g2f = g2[:].rearrange("p u v e -> p u (v e)")
-        a0 = tile_at("a0", [P, 2, 512], BF16, 20480)
-        fold(a0[:], m01[:, 0:3:2, :], g2f[:, :, 0:512])
+        a0 = tile_at("a0", [P, 2, 2, 256], BF16, 20480)
+        z01 = new_tile("z01", [P, 2, 512], BF16)
+
+        def third(ci):
+            fold(a0[:, ci], m01[:, 0:3:2, 256 * ci : 256 * (ci + 1)], g2f[:, :, 256 * ci : 256 * (ci + 1)])
+
+        def fourth(ci):
+            fold_woven(z01[:, ci, :], a0[:, ci], g3[:, :, P * ci : P * (ci + 1), :])
+
+        def z_planes(ci, src):
+            quantize(z_codes[:, P * ci : P * (ci + 1)], z_scales[:, P * ci : P * (ci + 1)], src)
+
+        third(0)
         quantize(w_codes[0][:], w_scales[0][:], w_bf[0][:])
-        z01 = new_tile("z01", [P, 1024], BF16)
-        fold_woven(z01[:], a0[:], g3[:, :, 0:256, :])
+        fourth(0)
         quantize(h_codes[:, 0:256], h_scales[0][:], h_bf[:, 0:1024])
         quantize(w_codes[1][:], w_scales[1][:], w_bf[1][:])
-        quantize(z_codes[:, 0:256], z_scales[:, 0:256], z01[:])
+        z_planes(0, z01[:, 0, :])
         own_passes(0)
         own_passes(1)
         finish_chunk(0)
+        third(1)
+        fourth(1)
+        z_planes(1, z01[:, 1, :])
         finish_chunk(1)
         b1 = tile_at("b1", [P, 512], BF16, 12288)
         fold(b1[:], flat(g0[1][:])[:, 512:1024], flat(g1[1][:])[:, 512:1024])
@@ -243,8 +256,8 @@ def tile_picked_wsagecat_max_lo_kernel(
         fold_woven(z3[:], a1[:, :, 256:512], g3_last[:])
         quantize(z_codes[:, 384:512], z_scales[:, 384:512], z3[:])
         result_planes(0, 256)
+        nc.sync.dma_start(out=out_words[:, 0:256], in_=y_words[:, 0:256].bitcast(I32))
         result_planes(256, 128)
-        nc.sync.dma_start(out=out_words[:, 0:384], in_=y_words[:, 0:384].bitcast(I32))
         for t in range(PACK):
             neighbour_pass(banks_q[t // 2][:, P * (t % 2) : P * (t % 2 + 1)], t, 384, t % 2 == 1)
 
@@ -257,13 +270,12 @@ def tile_picked_wsagecat_max_lo_kernel(
         def copy_pair(u):
             nc.scalar.copy(out=y[3][:, 2 * u : 2 * u + 2, :].rearrange("p t v -> p (t v)"), in_=banks_q[u][:, 0 : 2 * P])
 
-        weave_pair(0)
-        copy_pair(1)
-        copy_pair(0)
-        weave_pair(1)
-        nc.sync.dma_start(out=out_rows[:, :, 384:512], in_=y[3][:])
+        for u in range(2):
+            weave_pair(u)
+            copy_pair(u)
+            nc.sync.dma_start(out=out_rows[:, 2 * u : 2 * u + 2, 384:512], in_=y[3][:, 2 * u : 2 * u + 2, :])
         result_planes(384, 128)
-        nc.sync.dma_start(out=out_words[:, 384:512], in_=y_words[:, 384:512].bitcast(I32))
+        nc.scalar.dma_start(out=out_words[:, 256:512], in_=y_words[:, 256:512].bitcast(I32))
         for q in range(4):
             queue = nc.sync if q % 2 else nc.scalar
             queue.dma_start(

@@ -59,7 +59,7 @@ def tile_picked_wsagecat_max_lo_kernel(
             lists.append(offsets)
         w_raw = []
         for n, w in enumerate((w2, w3)):
-            raw = new_tile("w_raw%d" % n, [P, PACK, H], F32)
+            raw = tile_at("w_raw%d" % n, [P, PACK, H], F32, 24576 + 8192 * n)
             rows = w.rearrange("(q s r) c -> s q r c", s=PACK, r=8)
             for s in range(PACK):
                 nc.sync.dma_start(out=raw[:, s, :], in_=rows[s])
@@ -111,28 +111,12 @@ def tile_picked_wsagecat_max_lo_kernel(
 
         g0 = [new_tile("g0_%d" % u, [P, T, 2], BF16) for u in range(2)]
         g1 = [new_tile("g1_%d" % u, [P, T, 2], BF16) for u in range(2)]
-        g2 = new_tile("g2", [P, 2, T, 2], BF16)
-        g3 = new_tile("g3", [P, 2, 384, 2], BF16)
         for t in range(PACK):
             gather(g0[t // 2][:, :, t % 2], t, 0, 0, T)
             gather(g1[t // 2][:, :, t % 2], t, 1, 0, T)
-        for t in range(PACK):
-            gather(g2[:, t // 2, :, t % 2], t, 2, 0, T)
-            gather(g3[:, t // 2, :, t % 2], t, 3, 0, 384)
 
         def flat(ap):
             return ap.rearrange("p v e -> p (v e)")
-
-        m01 = new_tile("m01", [P, 3, 512], BF16)
-        for u, n, at in ((0, 1024, 0), (1, 512, 4096)):
-            diff = tile_at("diff%d" % u, [P, n], F32, at)
-            rise = tile_at("rise%d" % u, [P, n], F32, at + 4096)
-            a = flat(g0[u][:])[:, 0:n]
-            b = flat(g1[u][:])[:, 0:n]
-            nc.gpsimd.tensor_tensor(diff[:], b, a, mybir.AluOpType.subtract)
-            nc.scalar.activation(rise[:], diff[:], RELU)
-            dst = m01[:].rearrange("p r c -> p (r c)")[:, 1024 * u : 1024 * u + n]
-            nc.gpsimd.tensor_tensor(dst, a, rise[:], mybir.AluOpType.add)
 
         h_bf = new_tile("h_bf", [P, PACK * T], BF16)
         for u in range(2):
@@ -141,7 +125,8 @@ def tile_picked_wsagecat_max_lo_kernel(
                 in_=h[:, :, 256 * u : 256 * (u + 1)].rearrange("p t (c i) -> p c t i", i=4),
             )
         w_bf = []
-        for n in range(2):
+
+        def round_weights(n):
             wb = tile_at("w_bf%d" % n, [P, PACK * H], BF16, 12288 + 4096 * n)
             for u in range(2):
                 nc.scalar.copy(
@@ -149,6 +134,42 @@ def tile_picked_wsagecat_max_lo_kernel(
                     in_=w_raw[n][:].rearrange("p s (m t) -> p m t s", t=PACK)[:, 64 * u : 64 * (u + 1)],
                 )
             w_bf.append(wb)
+
+        round_weights(0)
+        g2 = tile_at("g2", [P, 2, T, 2], BF16, 28672)
+        for t in (0, 2, 1, 3):
+            gather(g2[:, t // 2, :, t % 2], t, 2, 0, T)
+        m01 = new_tile("m01", [P, 4, 512], BF16)
+        m01_low = m01[:, 0:2, :].rearrange("p r (v e) -> p (r v) e", e=2)
+        parts = [(g0[0][:, :, e], g1[0][:, :, e], m01_low[:, :, e]) for e in range(2)]
+        parts.append((flat(g0[1][:])[:, 0:512], flat(g1[1][:])[:, 0:512], m01[:, 2, :]))
+        parts.append((flat(g0[1][:])[:, 512:1024], flat(g1[1][:])[:, 512:1024], m01[:, 3, :]))
+        diff_at = (0, 16384, 24576, 26624)
+        rise_at = (4096, 25600, 2048, 8192)
+        diff, rise = [], []
+
+        def difference(r):
+            diff.append(tile_at("diff%d" % r, [P, 512], F32, diff_at[r]))
+            rise.append(tile_at("rise%d" % r, [P, 512], F32, rise_at[r]))
+            nc.gpsimd.tensor_tensor(diff[r][:], parts[r][1], parts[r][0], mybir.AluOpType.subtract)
+            nc.scalar.activation(rise[r][:], diff[r][:], RELU)
+
+        def total(r):
+            nc.gpsimd.tensor_tensor(parts[r][2], parts[r][0], rise[r][:], mybir.AluOpType.add)
+
+        difference(0)
+        difference(1)
+        round_weights(1)
+        g3 = tile_at("g3", [P, 2, 384, 2], BF16, 32768)
+        for t in (0, 2, 1, 3):
+            gather(g3[:, t // 2, :, t % 2], t, 3, 0, 384)
+        total(0)
+        total(1)
+        difference(2)
+        difference(3)
+        total(2)
+        total(3)
+
         h_codes = new_tile("h_codes", [P, T], U32)
         h_scales = [tile_at("h_scales0", [P, 2 * P], U8, 9216), tile_at("h_scales1", [P, 2 * P], U8, 20480)]
         w_codes = [new_tile("w_codes%d" % n, [P, H], U32) for n in range(2)]
@@ -215,7 +236,7 @@ def tile_picked_wsagecat_max_lo_kernel(
         z01 = new_tile("z01", [P, 2, 512], BF16)
 
         def third(ci):
-            fold(a0[:, ci], m01[:, 0:3:2, 256 * ci : 256 * (ci + 1)], g2f[:, :, 256 * ci : 256 * (ci + 1)])
+            fold(a0[:, ci], m01[:, 0:4:2, 256 * ci : 256 * (ci + 1)], g2f[:, :, 256 * ci : 256 * (ci + 1)])
 
         def fourth(ci):
             fold_woven(z01[:, ci, :], a0[:, ci], g3[:, :, P * ci : P * (ci + 1), :])
@@ -236,18 +257,15 @@ def tile_picked_wsagecat_max_lo_kernel(
         fourth(1)
         z_planes(1, z01[:, 1, :])
         finish_chunk(1)
-        b1 = tile_at("b1", [P, 512], BF16, 12288)
-        fold(b1[:], flat(g0[1][:])[:, 512:1024], flat(g1[1][:])[:, 512:1024])
         a1 = tile_at("a1", [P, 2, 512], BF16, 16384)
-        fold(a1[:, 0, :], m01[:, 1, :], g2f[:, 0, 512:1024])
-        fold(a1[:, 1, :], b1[:], g2f[:, 1, 512:1024])
+        fold(a1[:], m01[:, 1:4:2, :], g2f[:, :, 512:1024])
         quantize(h_codes[:, 256:512], h_scales[1][:], h_bf[:, 1024:2048])
         z2 = new_tile("z2", [P, 512], BF16)
         fold_woven(z2[:], a1[:, :, 0:256], g3[:, :, 256:384, :])
         quantize(z_codes[:, 256:384], z_scales[:, 256:384], z2[:])
         own_passes(2)
         for t in range(PACK):
-            own_pass(banks_q[t // 2][:, P * (t % 2) : P * (t % 2 + 1)], t, 384, t % 2 == 0)
+            own_pass(banks_q[t][:, 0:P], t, 384, True)
         finish_chunk(2)
         g3_last = tile_at("g3_last", [P, 2, P, 2], BF16, 21504)
         for t in (0, 2, 1, 3):
@@ -256,26 +274,20 @@ def tile_picked_wsagecat_max_lo_kernel(
         fold_woven(z3[:], a1[:, :, 256:512], g3_last[:])
         quantize(z_codes[:, 384:512], z_scales[:, 384:512], z3[:])
         result_planes(0, 256)
-        nc.sync.dma_start(out=out_words[:, 0:256], in_=y_words[:, 0:256].bitcast(I32))
         result_planes(256, 128)
+        nc.sync.dma_start(out=out_words[:, 0:384], in_=y_words[:, 0:384].bitcast(I32))
         for t in range(PACK):
-            neighbour_pass(banks_q[t // 2][:, P * (t % 2) : P * (t % 2 + 1)], t, 384, t % 2 == 1)
-
-        def weave_pair(u):
-            nc.vector.tensor_copy(
-                out=y_bf[:, PACK * 384 :].rearrange("p (v u e) -> p u v e", u=2, e=2)[:, u],
-                in_=banks_q[u][:, 0 : 2 * P].rearrange("p (e v) -> p v e", e=2),
-            )
-
-        def copy_pair(u):
-            nc.scalar.copy(out=y[3][:, 2 * u : 2 * u + 2, :].rearrange("p t v -> p (t v)"), in_=banks_q[u][:, 0 : 2 * P])
-
-        for u in range(2):
-            weave_pair(u)
-            copy_pair(u)
-            nc.sync.dma_start(out=out_rows[:, 2 * u : 2 * u + 2, 384:512], in_=y[3][:, 2 * u : 2 * u + 2, :])
+            neighbour_pass(banks_q[t][:, 0:P], t, 384, True)
+        for t in range(PACK):
+            copy = nc.vector.tensor_copy if t % 2 else nc.scalar.copy
+            copy(out=y[3][:, t, :], in_=banks_q[t][:, 0:P])
+        nc.sync.dma_start(out=out_rows[:, :, 384:512], in_=y[3][:])
+        nc.vector.tensor_copy(
+            out=y_bf[:, PACK * 384 :].rearrange("p (c i t) -> p c t i", i=4, t=PACK),
+            in_=y[3][:].rearrange("p t (c i) -> p c t i", i=4),
+        )
         result_planes(384, 128)
-        nc.scalar.dma_start(out=out_words[:, 256:512], in_=y_words[:, 256:512].bitcast(I32))
+        nc.sync.dma_start(out=out_words[:, 384:512], in_=y_words[:, 384:512].bitcast(I32))
         for q in range(4):
             queue = nc.sync if q % 2 else nc.scalar
             queue.dma_start(

@@ -17,7 +17,21 @@ P = 128
 PACK = 4
 T = 512
 H = 512
+WINDOW = 704
+EARLY = 384
 FLOPS = 3 * 2 * 512 * 512 * 512
+
+DIFF_AT = (0, 16384, 4096, 24576)
+RISE_AT = (4096, 25600, 2048, 8192)
+W_SCALES_AT = (8192, 8704)
+H_SCALES_AT = (9216, 20480)
+W_BF_AT = (12288, 16384)
+W_RAW_AT = (24576, 32768)
+MAX3_LOW_AT = 20480
+MAX3_HIGH_AT = 16384
+G2_AT = 28672
+G3_AT = 32768
+G3_LAST_AT = 21504
 
 
 def tile_picked_wsagecat_max_lo_kernel(
@@ -59,7 +73,7 @@ def tile_picked_wsagecat_max_lo_kernel(
             lists.append(offsets)
         w_raw = []
         for n, w in enumerate((w2, w3)):
-            raw = tile_at("w_raw%d" % n, [P, PACK, H], F32, 24576 + 8192 * n)
+            raw = tile_at("w_raw%d" % n, [P, PACK, H], F32, W_RAW_AT[n])
             rows = w.rearrange("(q s r) c -> s q r c", s=PACK, r=8)
             for s in range(PACK):
                 nc.sync.dma_start(out=raw[:, s, :], in_=rows[s])
@@ -68,7 +82,7 @@ def tile_picked_wsagecat_max_lo_kernel(
         banks_p = [psum.tile([P, T], F32, name="bank_p%d" % t) for t in range(PACK)]
         banks_q = [psum.tile([P, T], F32, name="bank_q%d" % t) for t in range(PACK)]
 
-        w1_bf = [new_tile("w1_bf%d" % t, [P, 512], BF16) for t in range(PACK)]
+        w1_bf = [new_tile("w1_bf%d" % t, [P, PACK * P], BF16) for t in range(PACK)]
         w1_codes = [new_tile("w1_codes%d" % t, [P, P], U32) for t in range(PACK)]
         w1_scales = [new_tile("w1_scales%d" % t, [P, P], U8) for t in range(PACK)]
 
@@ -81,27 +95,28 @@ def tile_picked_wsagecat_max_lo_kernel(
             round_w1(0, t, nc.vector.tensor_copy)
         for t in range(PACK):
             round_w1(1, t, nc.vector.tensor_copy if t < 2 else nc.scalar.copy)
-        h_wide = new_tile("h_wide", [P, PACK, 704], F32)
-        nc.gpsimd.memset(h_wide[:, :, T:704], 0.0)
+        h_wide = new_tile("h_wide", [P, PACK, WINDOW], F32)
+        nc.gpsimd.memset(h_wide[:, :, T:WINDOW], 0.0)
         h = h_wide[:, :, 0:T]
-        for t in range(PACK):
-            quantize(w1_codes[t][:], w1_scales[t][:], w1_bf[t][:])
-            if t == 0:
-                pieces = [(0, 256), (256, 128), (384, 128)]
-                for bank, (c0, n) in zip(banks_q, pieces):
-                    nc.tensor.matmul_mx(
-                        out=bank[:, 0:n], lhsT=w1_codes[t][:].bitcast(FP8X4), lhsT_scale=w1_scales[t][:],
-                        rhs=xw[:, 2 * c0 : 2 * (c0 + n)].bitcast(FP4X4), rhs_scale=xs[:, c0 : c0 + n],
-                        start=True, stop=True,
-                    )
-                nc.scalar.activation(h[:, 0, 0:256], banks_q[0][:, 0:256], RELU)
-                nc.vector.tensor_scalar_max(h[:, 0, 256:384], banks_q[1][:, 0:128], 0.0)
-                nc.scalar.activation(h[:, 0, 384:512], banks_q[2][:, 0:128], RELU)
-                continue
+
+        def first_product(out, t, c0, n):
             nc.tensor.matmul_mx(
-                out=banks_p[t][:], lhsT=w1_codes[t][:].bitcast(FP8X4), lhsT_scale=w1_scales[t][:],
-                rhs=xw[:].bitcast(FP4X4), rhs_scale=xs[:], start=True, stop=True,
+                out=out, lhsT=w1_codes[t][:].bitcast(FP8X4), lhsT_scale=w1_scales[t][:],
+                rhs=xw[:, 2 * c0 : 2 * (c0 + n)].bitcast(FP4X4), rhs_scale=xs[:, c0 : c0 + n],
+                start=True, stop=True,
             )
+
+        quantize(w1_codes[0][:], w1_scales[0][:], w1_bf[0][:])
+        for piece, bank in enumerate(banks_q):
+            c0 = P * piece
+            first_product(bank[:, 0:P], 0, c0, P)
+            if piece % 2:
+                nc.vector.tensor_scalar_max(h[:, 0, c0 : c0 + P], bank[:, 0:P], 0.0)
+            else:
+                nc.scalar.activation(h[:, 0, c0 : c0 + P], bank[:, 0:P], RELU)
+        for t in range(1, PACK):
+            quantize(w1_codes[t][:], w1_scales[t][:], w1_bf[t][:])
+            first_product(banks_p[t][:], t, 0, T)
             nc.scalar.activation(h[:, t, :], banks_p[t][:], RELU)
 
         def gather(dst, t, d, v0, n):
@@ -109,71 +124,69 @@ def tile_picked_wsagecat_max_lo_kernel(
                 out=dst, in_=(h_wide if n == T else h)[:, t, :].indirect(lists[d][:, v0 // 16 : (v0 + n) // 16])
             )
 
+        alternating = (0, 2, 1, 3)
         g0 = [new_tile("g0_%d" % u, [P, T, 2], BF16) for u in range(2)]
         g1 = [new_tile("g1_%d" % u, [P, T, 2], BF16) for u in range(2)]
         for t in range(PACK):
             gather(g0[t // 2][:, :, t % 2], t, 0, 0, T)
             gather(g1[t // 2][:, :, t % 2], t, 1, 0, T)
 
-        def flat(ap):
-            return ap.rearrange("p v e -> p (v e)")
-
         h_bf = new_tile("h_bf", [P, PACK * T], BF16)
-        for u in range(2):
+        for half in range(2):
             nc.scalar.copy(
-                out=h_bf[:, 1024 * u : 1024 * (u + 1)].rearrange("p (c i t) -> p c t i", i=4, t=PACK),
-                in_=h[:, :, 256 * u : 256 * (u + 1)].rearrange("p t (c i) -> p c t i", i=4),
+                out=h_bf[:, 1024 * half : 1024 * (half + 1)].rearrange("p (c i t) -> p c t i", i=4, t=PACK),
+                in_=h[:, :, 256 * half : 256 * (half + 1)].rearrange("p t (c i) -> p c t i", i=4),
             )
         w_bf = []
 
         def round_weights(n):
-            wb = tile_at("w_bf%d" % n, [P, PACK * H], BF16, 12288 + 4096 * n)
-            for u in range(2):
+            wb = tile_at("w_bf%d" % n, [P, PACK * H], BF16, W_BF_AT[n])
+            for half in range(2):
                 nc.scalar.copy(
-                    out=wb[:].rearrange("p (t m s) -> p m t s", t=PACK, s=PACK)[:, 64 * u : 64 * (u + 1)],
-                    in_=w_raw[n][:].rearrange("p s (m t) -> p m t s", t=PACK)[:, 64 * u : 64 * (u + 1)],
+                    out=wb[:].rearrange("p (t a s) -> p a t s", t=PACK, s=PACK)[:, 64 * half : 64 * (half + 1)],
+                    in_=w_raw[n][:].rearrange("p s (a t) -> p a t s", t=PACK)[:, 64 * half : 64 * (half + 1)],
                 )
             w_bf.append(wb)
 
         round_weights(0)
-        g2 = tile_at("g2", [P, 2, T, 2], BF16, 28672)
-        for t in (0, 2, 1, 3):
+        g2 = tile_at("g2", [P, 2, T, 2], BF16, G2_AT)
+        for t in alternating:
             gather(g2[:, t // 2, :, t % 2], t, 2, 0, T)
-        m01 = new_tile("m01", [P, 4, 512], BF16)
-        m01_low = m01[:, 0:2, :].rearrange("p r (v e) -> p (r v) e", e=2)
-        parts = [(g0[0][:, :, e], g1[0][:, :, e], m01_low[:, :, e]) for e in range(2)]
-        parts.append((flat(g0[1][:])[:, 0:512], flat(g1[1][:])[:, 0:512], m01[:, 2, :]))
-        parts.append((flat(g0[1][:])[:, 512:1024], flat(g1[1][:])[:, 512:1024], m01[:, 3, :]))
-        diff_at = (0, 16384, 24576, 26624)
-        rise_at = (4096, 25600, 2048, 8192)
+
+        max2 = new_tile("max2", [P, 4, 512], BF16)
+        max2_paired = max2[:].rearrange("p (u r) (v e) -> p u (r v) e", u=2, e=2)
         diff, rise = [], []
 
-        def difference(r):
-            diff.append(tile_at("diff%d" % r, [P, 512], F32, diff_at[r]))
-            rise.append(tile_at("rise%d" % r, [P, 512], F32, rise_at[r]))
-            nc.gpsimd.tensor_tensor(diff[r][:], parts[r][1], parts[r][0], mybir.AluOpType.subtract)
-            nc.scalar.activation(rise[r][:], diff[r][:], RELU)
+        def difference(t):
+            diff.append(tile_at("diff%d" % t, [P, T], F32, DIFF_AT[t]))
+            rise.append(tile_at("rise%d" % t, [P, T], F32, RISE_AT[t]))
+            nc.gpsimd.tensor_tensor(
+                diff[t][:], g1[t // 2][:, :, t % 2], g0[t // 2][:, :, t % 2], mybir.AluOpType.subtract
+            )
+            nc.scalar.activation(rise[t][:], diff[t][:], RELU)
 
-        def total(r):
-            nc.gpsimd.tensor_tensor(parts[r][2], parts[r][0], rise[r][:], mybir.AluOpType.add)
+        def total(t):
+            nc.gpsimd.tensor_tensor(
+                max2_paired[:, t // 2, :, t % 2], g0[t // 2][:, :, t % 2], rise[t][:], mybir.AluOpType.add
+            )
 
         difference(0)
         difference(1)
         round_weights(1)
-        g3 = tile_at("g3", [P, 2, 384, 2], BF16, 32768)
-        for t in (0, 2, 1, 3):
-            gather(g3[:, t // 2, :, t % 2], t, 3, 0, 384)
+        g3 = tile_at("g3", [P, 2, EARLY, 2], BF16, G3_AT)
+        for t in alternating:
+            gather(g3[:, t // 2, :, t % 2], t, 3, 0, EARLY)
         total(0)
-        total(1)
         difference(2)
+        total(1)
         difference(3)
         total(2)
         total(3)
 
         h_codes = new_tile("h_codes", [P, T], U32)
-        h_scales = [tile_at("h_scales0", [P, 2 * P], U8, 9216), tile_at("h_scales1", [P, 2 * P], U8, 20480)]
+        h_scales = [tile_at("h_scales%d" % half, [P, 2 * P], U8, H_SCALES_AT[half]) for half in range(2)]
         w_codes = [new_tile("w_codes%d" % n, [P, H], U32) for n in range(2)]
-        w_scales = [tile_at("w_scales%d" % n, [P, H], U8, 8192 + 512 * n) for n in range(2)]
+        w_scales = [tile_at("w_scales%d" % n, [P, H], U8, W_SCALES_AT[n]) for n in range(2)]
 
         y_words = new_tile("y_words", [P, T], U32)
         y_scales = new_tile("y_scales", [P, T], U8)
@@ -231,63 +244,65 @@ def tile_picked_wsagecat_max_lo_kernel(
                 in_=bank[:].rearrange("p (t v) -> p v t", t=PACK),
             )
 
-        g2f = g2[:].rearrange("p u v e -> p u (v e)")
-        a0 = tile_at("a0", [P, 2, 2, 256], BF16, 20480)
-        z01 = new_tile("z01", [P, 2, 512], BF16)
-
-        def third(ci):
-            fold(a0[:, ci], m01[:, 0:4:2, 256 * ci : 256 * (ci + 1)], g2f[:, :, 256 * ci : 256 * (ci + 1)])
-
-        def fourth(ci):
-            fold_woven(z01[:, ci, :], a0[:, ci], g3[:, :, P * ci : P * (ci + 1), :])
-
         def z_planes(ci, src):
             quantize(z_codes[:, P * ci : P * (ci + 1)], z_scales[:, P * ci : P * (ci + 1)], src)
 
-        third(0)
+        g2_rows = g2[:].rearrange("p u v e -> p u (v e)")
+        max3_low = tile_at("max3_low", [P, 2, 2, 256], BF16, MAX3_LOW_AT)
+        z_low = new_tile("z_low", [P, 2, 512], BF16)
+
+        def with_list2(ci):
+            cols = slice(256 * ci, 256 * (ci + 1))
+            fold(max3_low[:, ci], max2[:, 0:4:2, cols], g2_rows[:, :, cols])
+
+        def with_list3(ci):
+            fold_woven(z_low[:, ci, :], max3_low[:, ci], g3[:, :, P * ci : P * (ci + 1), :])
+
+        with_list2(0)
         quantize(w_codes[0][:], w_scales[0][:], w_bf[0][:])
-        fourth(0)
+        with_list3(0)
         quantize(h_codes[:, 0:256], h_scales[0][:], h_bf[:, 0:1024])
         quantize(w_codes[1][:], w_scales[1][:], w_bf[1][:])
-        z_planes(0, z01[:, 0, :])
+        z_planes(0, z_low[:, 0, :])
         own_passes(0)
         own_passes(1)
         finish_chunk(0)
-        third(1)
-        fourth(1)
-        z_planes(1, z01[:, 1, :])
+        with_list2(1)
+        with_list3(1)
+        z_planes(1, z_low[:, 1, :])
         finish_chunk(1)
-        a1 = tile_at("a1", [P, 2, 512], BF16, 16384)
-        fold(a1[:], m01[:, 1:4:2, :], g2f[:, :, 512:1024])
+
+        max3_high = tile_at("max3_high", [P, 2, 512], BF16, MAX3_HIGH_AT)
+        fold(max3_high[:], max2[:, 1:4:2, :], g2_rows[:, :, 512:1024])
         quantize(h_codes[:, 256:512], h_scales[1][:], h_bf[:, 1024:2048])
         z2 = new_tile("z2", [P, 512], BF16)
-        fold_woven(z2[:], a1[:, :, 0:256], g3[:, :, 256:384, :])
-        quantize(z_codes[:, 256:384], z_scales[:, 256:384], z2[:])
+        fold_woven(z2[:], max3_high[:, :, 0:256], g3[:, :, 256:EARLY, :])
+        z_planes(2, z2[:])
         own_passes(2)
         for t in range(PACK):
-            own_pass(banks_q[t][:, 0:P], t, 384, True)
+            own_pass(banks_q[t][:, 0:P], t, EARLY, True)
         finish_chunk(2)
-        g3_last = tile_at("g3_last", [P, 2, P, 2], BF16, 21504)
-        for t in (0, 2, 1, 3):
-            gather(g3_last[:, t // 2, :, t % 2], t, 3, 384, P)
+        g3_last = tile_at("g3_last", [P, 2, P, 2], BF16, G3_LAST_AT)
+        for t in alternating:
+            gather(g3_last[:, t // 2, :, t % 2], t, 3, EARLY, P)
         z3 = new_tile("z3", [P, 512], BF16)
-        fold_woven(z3[:], a1[:, :, 256:512], g3_last[:])
-        quantize(z_codes[:, 384:512], z_scales[:, 384:512], z3[:])
+        fold_woven(z3[:], max3_high[:, :, 256:512], g3_last[:])
+        z_planes(3, z3[:])
         result_planes(0, 256)
-        result_planes(256, 128)
-        nc.sync.dma_start(out=out_words[:, 0:384], in_=y_words[:, 0:384].bitcast(I32))
+        result_planes(256, P)
+        nc.sync.dma_start(out=out_words[:, 0:EARLY], in_=y_words[:, 0:EARLY].bitcast(I32))
         for t in range(PACK):
-            neighbour_pass(banks_q[t][:, 0:P], t, 384, True)
+            neighbour_pass(banks_q[t][:, 0:P], t, EARLY, True)
         for t in range(PACK):
-            copy = nc.vector.tensor_copy if t % 2 else nc.scalar.copy
+            copy = nc.scalar.copy if t % 2 else nc.vector.tensor_copy
             copy(out=y[3][:, t, :], in_=banks_q[t][:, 0:P])
-        nc.sync.dma_start(out=out_rows[:, :, 384:512], in_=y[3][:])
+        nc.sync.dma_start(out=out_rows[:, :, EARLY:T], in_=y[3][:])
         nc.vector.tensor_copy(
-            out=y_bf[:, PACK * 384 :].rearrange("p (c i t) -> p c t i", i=4, t=PACK),
+            out=y_bf[:, PACK * EARLY :].rearrange("p (c i t) -> p c t i", i=4, t=PACK),
             in_=y[3][:].rearrange("p t (c i) -> p c t i", i=4),
         )
-        result_planes(384, 128)
-        nc.sync.dma_start(out=out_words[:, 384:512], in_=y_words[:, 384:512].bitcast(I32))
+        result_planes(EARLY, P)
+        nc.sync.dma_start(out=out_words[:, EARLY:T], in_=y_words[:, EARLY:T].bitcast(I32))
         for q in range(4):
             queue = nc.sync if q % 2 else nc.scalar
             queue.dma_start(

@@ -11,27 +11,17 @@ U8 = mybir.dt.uint8
 FP8X4 = mybir.dt.float8_e4m3fn_x4
 FP4X4 = mybir.dt.float4_e2m1fn_x4
 RELU = mybir.ActivationFunctionType.Relu
+COPY = mybir.ActivationFunctionType.Copy
 MAX = mybir.AluOpType.max
+MULT = mybir.AluOpType.mult
+ADD = mybir.AluOpType.add
 
 P = 128
 PACK = 4
 T = 512
 H = 512
-WINDOW = 704
-EARLY = 384
+PAD = 192
 FLOPS = 3 * 2 * 512 * 512 * 512
-
-DIFF_AT = (0, 16384, 4096, 24576)
-RISE_AT = (4096, 25600, 2048, 8192)
-W_SCALES_AT = (8192, 8704)
-H_SCALES_AT = (9216, 20480)
-W_BF_AT = (12288, 16384)
-W_RAW_AT = (24576, 32768)
-MAX3_LOW_AT = 20480
-MAX3_HIGH_AT = 16384
-G2_AT = 28672
-G3_AT = 32768
-G3_LAST_AT = 21504
 
 
 def tile_picked_wsagecat_max_lo_kernel(
@@ -41,63 +31,57 @@ def tile_picked_wsagecat_max_lo_kernel(
     with ExitStack() as ctx:
         lists_pool = ctx.enter_context(tc.tile_pool(name="lists", bufs=1))
         sb = ctx.enter_context(tc.tile_pool(name="sb", bufs=1))
-        shared = ctx.enter_context(tc.tile_pool(name="shared", bufs=1))
         psum = ctx.enter_context(tc.psum_pool(name="psum", bufs=1))
 
         def new_tile(name, shape, dtype):
             return sb.tile(shape, dtype, name=name, align_bytes=64)
-
-        def tile_at(name, shape, dtype, offset):
-            return shared.tile(shape, dtype, name=name, align_bytes=64, offset=offset)
 
         def quantize(codes, scales, src):
             nc.vector.quantize_mx(out=codes.bitcast(FP8X4), scales=scales, in_=src)
 
         xs = new_tile("xs", [P, T], U8)
         nc.vector.memset(xs[:].bitcast(I32), 0)
-
         w1_rows = w1.rearrange("(p j) c -> p j c", j=PACK)
-        w1_raw = [new_tile("w1_raw%d" % c, [P, 2, H], F32) for c in range(2)]
+        w1_raw = [new_tile("w1_raw%d" % c, [P, PACK, H // 2], F32) for c in range(2)]
         for c in range(2):
-            nc.sync.dma_start(out=w1_raw[c][:], in_=w1_rows[:, 2 * c : 2 * c + 2, :])
+            nc.sync.dma_start(out=w1_raw[c][:], in_=w1_rows[:, :, 256 * c : 256 * (c + 1)])
         xw = new_tile("xw", [P, 2 * T], U8)
         nc.sync.dma_start(out=xw[:].bitcast(I32), in_=x_words[0].bitcast(I32))
         for q in range(4):
             nc.scalar.dma_start(
                 out=xs[32 * q : 32 * q + 4, :].bitcast(I32), in_=x_scales[0, 4 * q : 4 * q + 4, :].bitcast(I32)
             )
-        lists = []
-        for d, pos in enumerate((pos1, pos2, pos3, pos4)):
-            offsets = lists_pool.tile([P, T // 16], U16, name="pos%d" % d)
-            nc.sync.dma_start(offsets[:], pos)
-            lists.append(offsets)
-        w_raw = []
-        for n, w in enumerate((w2, w3)):
-            raw = tile_at("w_raw%d" % n, [P, PACK, H], F32, W_RAW_AT[n])
-            rows = w.rearrange("(q s r) c -> s q r c", s=PACK, r=8)
-            for s in range(PACK):
-                nc.sync.dma_start(out=raw[:, s, :], in_=rows[s])
-            w_raw.append(raw)
+        lists = [lists_pool.tile([P, T // 16], U16, name="pos%d" % d) for d in range(4)]
+        w_raw = [new_tile("w_raw%d" % n, [P, PACK, H], F32) for n in range(2)]
+        nc.sync.dma_start(lists[0][:], pos1)
+        nc.sync.dma_start(out=w_raw[0][:], in_=w2.rearrange("(p s) c -> p s c", s=PACK))
+        nc.sync.dma_start(lists[1][:], pos2)
+        nc.sync.dma_start(lists[2][:], pos3)
+        nc.sync.dma_start(lists[3][:], pos4)
+        nc.sync.dma_start(out=w_raw[1][:], in_=w3.rearrange("(p s) c -> p s c", s=PACK))
 
         banks_p = [psum.tile([P, T], F32, name="bank_p%d" % t) for t in range(PACK)]
         banks_q = [psum.tile([P, T], F32, name="bank_q%d" % t) for t in range(PACK)]
 
-        w1_bf = [new_tile("w1_bf%d" % t, [P, PACK * P], BF16) for t in range(PACK)]
+        w1_bf = [new_tile("w1_bf%d" % u, [P, 2, PACK * P], BF16) for u in range(2)]
         w1_codes = [new_tile("w1_codes%d" % t, [P, P], U32) for t in range(PACK)]
         w1_scales = [new_tile("w1_scales%d" % t, [P, P], U8) for t in range(PACK)]
 
-        def round_w1(c, t, copy):
-            src = w1_raw[c][:].rearrange("p j (q t r) -> p t q r j", t=PACK, r=8)[:, t]
-            dst = w1_bf[t][:].rearrange("p (q r c j) -> p c q r j", r=8, c=2, j=2)[:, c]
+        def round_w1(c, u, copy):
+            src = w1_raw[c][:].rearrange("p j (a u e) -> p u a e j", u=2, e=2)[:, u]
+            dst = w1_bf[u][:].rearrange("p e (c a j) -> p c a e j", c=2, j=PACK)[:, c]
             copy(out=dst, in_=src)
 
-        for t in range(PACK):
-            round_w1(0, t, nc.vector.tensor_copy)
-        for t in range(PACK):
-            round_w1(1, t, nc.vector.tensor_copy if t < 2 else nc.scalar.copy)
-        h_wide = new_tile("h_wide", [P, PACK, WINDOW], F32)
-        nc.gpsimd.memset(h_wide[:, :, T:WINDOW], 0.0)
-        h = h_wide[:, :, 0:T]
+        round_w1(0, 0, nc.vector.tensor_copy)
+        round_w1(0, 1, nc.vector.tensor_copy)
+        round_w1(1, 0, nc.vector.tensor_copy)
+        round_w1(1, 1, nc.scalar.copy)
+        h = [new_tile("h%d" % u, [P, 2 * T + PAD], F32) for u in range(2)]
+        for u in range(2):
+            nc.gpsimd.memset(h[u][:, 2 * T :], 0.0)
+
+        def plane(t):
+            return h[t // 2][:, T * (t % 2) : T * (t % 2 + 1)]
 
         def first_product(out, t, c0, n):
             nc.tensor.matmul_mx(
@@ -106,203 +90,153 @@ def tile_picked_wsagecat_max_lo_kernel(
                 start=True, stop=True,
             )
 
-        quantize(w1_codes[0][:], w1_scales[0][:], w1_bf[0][:])
+        quantize(w1_codes[1][:], w1_scales[1][:], w1_bf[0][:, 1, :])
         for piece, bank in enumerate(banks_q):
             c0 = P * piece
-            first_product(bank[:, 0:P], 0, c0, P)
+            first_product(bank[:, 0:P], 1, c0, P)
             if piece % 2:
-                nc.vector.tensor_scalar_max(h[:, 0, c0 : c0 + P], bank[:, 0:P], 0.0)
+                nc.vector.tensor_scalar_max(plane(1)[:, c0 : c0 + P], bank[:, 0:P], 0.0)
             else:
-                nc.scalar.activation(h[:, 0, c0 : c0 + P], bank[:, 0:P], RELU)
-        for t in range(1, PACK):
-            quantize(w1_codes[t][:], w1_scales[t][:], w1_bf[t][:])
+                nc.scalar.activation(plane(1)[:, c0 : c0 + P], bank[:, 0:P], RELU)
+        for t in (0, 3, 2):
+            quantize(w1_codes[t][:], w1_scales[t][:], w1_bf[t // 2][:, t % 2, :])
             first_product(banks_p[t][:], t, 0, T)
-            nc.scalar.activation(h[:, t, :], banks_p[t][:], RELU)
+            nc.scalar.activation(plane(t), banks_p[t][:], RELU)
 
-        def gather(dst, t, d, v0, n):
-            nc.vector.tensor_copy(
-                out=dst, in_=(h_wide if n == T else h)[:, t, :].indirect(lists[d][:, v0 // 16 : (v0 + n) // 16])
-            )
-
-        alternating = (0, 2, 1, 3)
-        g0 = [new_tile("g0_%d" % u, [P, T, 2], BF16) for u in range(2)]
-        g1 = [new_tile("g1_%d" % u, [P, T, 2], BF16) for u in range(2)]
-        for t in range(PACK):
-            gather(g0[t // 2][:, :, t % 2], t, 0, 0, T)
-            gather(g1[t // 2][:, :, t % 2], t, 1, 0, T)
+        g_vec = [new_tile("g_vec%d" % d, [P, 2, 2, 256], BF16) for d in range(3)]
+        g_sca = [new_tile("g_sca%d" % d, [P, 2, T], BF16) for d in range(3)]
+        for d in range(3):
+            for u in range(2):
+                nc.vector.tensor_copy(out=g_vec[d][:, :, u, :], in_=h[u][:, T:].indirect(lists[d][:]))
+        for d in range(3):
+            for u in range(2):
+                nc.scalar.activation(g_sca[d][:, u, :], h[u][:].indirect(lists[d][:]), COPY)
+        g3 = new_tile("g3", [P, PACK, T], F32)
+        for v0, n in ((0, 256), (256, 128), (384, 128)):
+            for t in range(PACK):
+                nc.scalar.activation(
+                    g3[:, t, v0 : v0 + n], plane(t).indirect(lists[3][:, v0 // 16 : (v0 + n) // 16]), COPY
+                )
 
         h_bf = new_tile("h_bf", [P, PACK * T], BF16)
         for half in range(2):
-            nc.scalar.copy(
-                out=h_bf[:, 1024 * half : 1024 * (half + 1)].rearrange("p (c i t) -> p c t i", i=4, t=PACK),
-                in_=h[:, :, 256 * half : 256 * (half + 1)].rearrange("p t (c i) -> p c t i", i=4),
-            )
-        w_bf = []
-
-        def round_weights(n):
-            wb = tile_at("w_bf%d" % n, [P, PACK * H], BF16, W_BF_AT[n])
-            for half in range(2):
-                nc.scalar.copy(
-                    out=wb[:].rearrange("p (t a s) -> p a t s", t=PACK, s=PACK)[:, 64 * half : 64 * (half + 1)],
-                    in_=w_raw[n][:].rearrange("p s (a t) -> p a t s", t=PACK)[:, 64 * half : 64 * (half + 1)],
+            for u in range(2):
+                cols = slice(256 * half, 256 * (half + 1))
+                nc.gpsimd.tensor_scalar(
+                    h_bf[:].rearrange("p (v u e) -> p u v e", u=2, e=2)[:, u, cols],
+                    h[u][:, 0 : 2 * T].rearrange("p (e v) -> p v e", e=2)[:, cols],
+                    1.0, 0.0, MULT, ADD,
                 )
-            w_bf.append(wb)
+        w_bf = [new_tile("w_bf%d" % n, [P, PACK * H], BF16) for n in range(2)]
 
-        round_weights(0)
-        g2 = tile_at("g2", [P, 2, T, 2], BF16, G2_AT)
-        for t in alternating:
-            gather(g2[:, t // 2, :, t % 2], t, 2, 0, T)
-
-        max2 = new_tile("max2", [P, 4, 512], BF16)
-        max2_paired = max2[:].rearrange("p (u r) (v e) -> p u (r v) e", u=2, e=2)
-        diff, rise = [], []
-
-        def difference(t):
-            diff.append(tile_at("diff%d" % t, [P, T], F32, DIFF_AT[t]))
-            rise.append(tile_at("rise%d" % t, [P, T], F32, RISE_AT[t]))
-            nc.gpsimd.tensor_tensor(
-                diff[t][:], g1[t // 2][:, :, t % 2], g0[t // 2][:, :, t % 2], mybir.AluOpType.subtract
-            )
-            nc.scalar.activation(rise[t][:], diff[t][:], RELU)
-
-        def total(t):
-            nc.gpsimd.tensor_tensor(
-                max2_paired[:, t // 2, :, t % 2], g0[t // 2][:, :, t % 2], rise[t][:], mybir.AluOpType.add
+        def weight_views(n, a0, a1):
+            return (
+                w_bf[n][:].rearrange("p (t a s) -> p a t s", t=PACK, s=PACK)[:, a0:a1],
+                w_raw[n][:].rearrange("p s (a t) -> p a t s", t=PACK)[:, a0:a1],
             )
 
-        difference(0)
-        difference(1)
-        round_weights(1)
-        g3 = tile_at("g3", [P, 2, EARLY, 2], BF16, G3_AT)
-        for t in alternating:
-            gather(g3[:, t // 2, :, t % 2], t, 3, 0, EARLY)
-        total(0)
-        difference(2)
-        total(1)
-        difference(3)
-        total(2)
-        total(3)
+        for quarter in range(4):
+            dst, src = weight_views(0, 32 * quarter, 32 * (quarter + 1))
+            nc.gpsimd.tensor_scalar(dst, src, 1.0, 0.0, MULT, ADD)
 
         h_codes = new_tile("h_codes", [P, T], U32)
-        h_scales = [tile_at("h_scales%d" % half, [P, 2 * P], U8, H_SCALES_AT[half]) for half in range(2)]
+        h_scales = new_tile("h_scales", [P, T], U8)
         w_codes = [new_tile("w_codes%d" % n, [P, H], U32) for n in range(2)]
-        w_scales = [tile_at("w_scales%d" % n, [P, H], U8, W_SCALES_AT[n]) for n in range(2)]
+        w_scales = [new_tile("w_scales%d" % n, [P, H], U8) for n in range(2)]
+
+        def fold(dst, acc, other):
+            nc.vector.tensor_tensor(dst, acc, other, MAX)
+
+        max2_vec = new_tile("max2_vec", [P, 2, 2, 256], BF16)
+        max2_sca = new_tile("max2_sca", [P, 2, T], BF16)
+        max3 = new_tile("max3", [P, PACK, T], BF16)
+        max3_ue = max3[:].rearrange("p (u e) v -> p e u v", e=2)
+        fold(max2_vec[:], g_vec[0][:], g_vec[1][:])
+        dst, src = weight_views(1, 0, P)
+        nc.vector.tensor_copy(out=dst, in_=src)
+        fold(
+            max3_ue[:, 1].rearrange("p u (r v) -> p u r v", r=2),
+            max2_vec[:].rearrange("p r u v -> p u r v"),
+            g_vec[2][:].rearrange("p r u v -> p u r v"),
+        )
+        quantize(h_codes[:], h_scales[:], h_bf[:])
+        fold(max2_sca[:], g_sca[0][:], g_sca[1][:])
+        quantize(w_codes[1][:], w_scales[1][:], w_bf[1][:])
+        fold(max3_ue[:, 0], max2_sca[:], g_sca[2][:])
+        quantize(w_codes[0][:], w_scales[0][:], w_bf[0][:])
 
         y_words = new_tile("y_words", [P, T], U32)
         y_scales = new_tile("y_scales", [P, T], U8)
         out_rows = out_0.rearrange("(p t) v -> p t v", t=PACK)
         out_words = out_1[0].rearrange("p c r -> p (c r)").bitcast(I32)
-
-        def fold(dst, acc, other):
-            nc.vector.tensor_tensor(dst, acc, other, MAX)
-
-        def fold_woven(dst, acc, other):
-            fold(
-                dst.rearrange("p (v u e) -> p v u e", u=2, e=2),
-                acc.rearrange("p u (v e) -> p v u e", e=2),
-                other.rearrange("p u v e -> p v u e"),
-            )
-
         z_codes = new_tile("z_codes", [P, T], U32)
         z_scales = new_tile("z_scales", [P, T], U8)
-
-        def own_pass(out, t, v0, start):
-            cols = slice(P * t, P * (t + 1))
-            nc.tensor.matmul_mx(
-                out=out, lhsT=w_codes[0][:, cols].bitcast(FP8X4), lhsT_scale=w_scales[0][:, cols],
-                rhs=h_codes[:, v0 : v0 + P].bitcast(FP8X4), rhs_scale=h_scales[v0 // 256][:, v0 % 256 : v0 % 256 + P],
-                start=start, stop=False,
-            )
-
-        def neighbour_pass(out, t, v0, stop):
-            cols = slice(P * t, P * (t + 1))
-            nc.tensor.matmul_mx(
-                out=out, lhsT=w_codes[1][:, cols].bitcast(FP8X4), lhsT_scale=w_scales[1][:, cols],
-                rhs=z_codes[:, v0 : v0 + P].bitcast(FP8X4), rhs_scale=z_scales[:, v0 : v0 + P],
-                start=False, stop=stop,
-            )
-
-        def result_planes(v0, n):
-            quantize(y_words[:, v0 : v0 + n], y_scales[:, v0 : v0 + n], y_bf[:, PACK * v0 : PACK * (v0 + n)])
-
+        z_bf = [new_tile("z_bf%d" % ci, [P, PACK * P], BF16) for ci in range(4)]
         y = [new_tile("y%d" % ci, [P, PACK, P], F32) for ci in range(4)]
-        y_bf = new_tile("y_bf", [P, PACK * T], BF16)
+        y_bf = [new_tile("y_bf%d" % ci, [P, PACK * P], BF16) for ci in range(4)]
 
-        def own_passes(ci):
-            for t in range(PACK):
-                own_pass(banks_p[ci][:, P * t : P * (t + 1)], t, P * ci, t == 0)
-
-        def finish_chunk(ci):
-            v0 = P * ci
-            bank = banks_p[ci]
-            for t in range(PACK):
-                neighbour_pass(bank[:, P * t : P * (t + 1)], t, v0, t == PACK - 1)
-            nc.scalar.copy(out=y[ci][:].rearrange("p t v -> p (t v)"), in_=bank[:])
-            nc.sync.dma_start(out=out_rows[:, :, v0 : v0 + P], in_=y[ci][:])
-            nc.scalar.copy(
-                out=y_bf[:, PACK * v0 : PACK * (v0 + P)].rearrange("p (v t) -> p v t", t=PACK),
-                in_=bank[:].rearrange("p (t v) -> p v t", t=PACK),
+        def second_pass(out, n, codes, scales, t, v0, start, stop):
+            cols = slice(P * t, P * (t + 1))
+            nc.tensor.matmul_mx(
+                out=out, lhsT=w_codes[n][:, cols].bitcast(FP8X4), lhsT_scale=w_scales[n][:, cols],
+                rhs=codes[:, v0 : v0 + P].bitcast(FP8X4), rhs_scale=scales[:, v0 : v0 + P],
+                start=start, stop=stop,
             )
 
-        def z_planes(ci, src):
-            quantize(z_codes[:, P * ci : P * (ci + 1)], z_scales[:, P * ci : P * (ci + 1)], src)
+        def region(ci, t):
+            return banks_q[t][:, 0:P] if ci == 3 else banks_p[ci][:, P * t : P * (t + 1)]
 
-        g2_rows = g2[:].rearrange("p u v e -> p u (v e)")
-        max3_low = tile_at("max3_low", [P, 2, 2, 256], BF16, MAX3_LOW_AT)
-        z_low = new_tile("z_low", [P, 2, 512], BF16)
+        for ci in range(4):
+            for t in range(PACK):
+                second_pass(region(ci, t), 0, h_codes, h_scales, t, P * ci, ci == 3 or t == 0, False)
 
-        def with_list2(ci):
-            cols = slice(256 * ci, 256 * (ci + 1))
-            fold(max3_low[:, ci], max2[:, 0:4:2, cols], g2_rows[:, :, cols])
+        def z_chunk(ci):
+            cols = slice(P * ci, P * (ci + 1))
+            fold(
+                z_bf[ci][:].rearrange("p (a i t) -> p a t i", i=2, t=PACK),
+                g3[:, :, cols].rearrange("p t (a i) -> p a t i", i=2),
+                max3[:, :, cols].rearrange("p t (a i) -> p a t i", i=2),
+            )
 
-        def with_list3(ci):
-            fold_woven(z_low[:, ci, :], max3_low[:, ci], g3[:, :, P * ci : P * (ci + 1), :])
+        def z_product(ci):
+            cols = slice(P * ci, P * (ci + 1))
+            quantize(z_codes[:, cols], z_scales[:, cols], z_bf[ci][:])
+            for t in range(PACK):
+                second_pass(region(ci, t), 1, z_codes, z_scales, t, P * ci, False, ci == 3 or t == PACK - 1)
+            if ci < 3:
+                nc.scalar.copy(out=y[ci][:].rearrange("p t v -> p (t v)"), in_=banks_p[ci][:])
+            else:
+                for t in range(PACK):
+                    copy = nc.scalar.copy if t % 2 else nc.vector.tensor_copy
+                    copy(out=y[3][:, t, :], in_=banks_q[t][:, 0:P])
+            nc.sync.dma_start(out=out_rows[:, :, cols], in_=y[ci][:])
 
-        with_list2(0)
-        quantize(w_codes[0][:], w_scales[0][:], w_bf[0][:])
-        with_list3(0)
-        quantize(h_codes[:, 0:256], h_scales[0][:], h_bf[:, 0:1024])
-        quantize(w_codes[1][:], w_scales[1][:], w_bf[1][:])
-        z_planes(0, z_low[:, 0, :])
-        own_passes(0)
-        own_passes(1)
-        finish_chunk(0)
-        with_list2(1)
-        with_list3(1)
-        z_planes(1, z_low[:, 1, :])
-        finish_chunk(1)
+        def weave(ci):
+            nc.vector.tensor_copy(
+                out=y_bf[ci][:].rearrange("p (c i t) -> p c t i", i=4, t=PACK),
+                in_=y[ci][:].rearrange("p t (c i) -> p c t i", i=4),
+            )
 
-        max3_high = tile_at("max3_high", [P, 2, 512], BF16, MAX3_HIGH_AT)
-        fold(max3_high[:], max2[:, 1:4:2, :], g2_rows[:, :, 512:1024])
-        quantize(h_codes[:, 256:512], h_scales[1][:], h_bf[:, 1024:2048])
-        z2 = new_tile("z2", [P, 512], BF16)
-        fold_woven(z2[:], max3_high[:, :, 0:256], g3[:, :, 256:EARLY, :])
-        z_planes(2, z2[:])
-        own_passes(2)
-        for t in range(PACK):
-            own_pass(banks_q[t][:, 0:P], t, EARLY, True)
-        finish_chunk(2)
-        g3_last = tile_at("g3_last", [P, 2, P, 2], BF16, G3_LAST_AT)
-        for t in alternating:
-            gather(g3_last[:, t // 2, :, t % 2], t, 3, EARLY, P)
-        z3 = new_tile("z3", [P, 512], BF16)
-        fold_woven(z3[:], max3_high[:, :, 256:512], g3_last[:])
-        z_planes(3, z3[:])
-        result_planes(0, 256)
-        result_planes(256, P)
-        nc.sync.dma_start(out=out_words[:, 0:EARLY], in_=y_words[:, 0:EARLY].bitcast(I32))
-        for t in range(PACK):
-            neighbour_pass(banks_q[t][:, 0:P], t, EARLY, True)
-        for t in range(PACK):
-            copy = nc.scalar.copy if t % 2 else nc.vector.tensor_copy
-            copy(out=y[3][:, t, :], in_=banks_q[t][:, 0:P])
-        nc.sync.dma_start(out=out_rows[:, :, EARLY:T], in_=y[3][:])
-        nc.vector.tensor_copy(
-            out=y_bf[:, PACK * EARLY :].rearrange("p (c i t) -> p c t i", i=4, t=PACK),
-            in_=y[3][:].rearrange("p t (c i) -> p c t i", i=4),
-        )
-        result_planes(EARLY, P)
-        nc.sync.dma_start(out=out_words[:, EARLY:T], in_=y_words[:, EARLY:T].bitcast(I32))
+        def result_planes(ci):
+            cols = slice(P * ci, P * (ci + 1))
+            quantize(y_words[:, cols], y_scales[:, cols], y_bf[ci][:])
+
+        z_chunk(0)
+        z_chunk(1)
+        z_product(0)
+        z_chunk(2)
+        z_product(1)
+        z_chunk(3)
+        z_product(2)
+        z_product(3)
+        for ci in range(4):
+            weave(ci)
+            if ci:
+                result_planes(ci - 1)
+            if ci == 3:
+                nc.sync.dma_start(out=out_words[:, 0:384], in_=y_words[:, 0:384].bitcast(I32))
+        result_planes(3)
+        nc.sync.dma_start(out=out_words[:, 384:T], in_=y_words[:, 384:T].bitcast(I32))
         for q in range(4):
             queue = nc.sync if q % 2 else nc.scalar
             queue.dma_start(

@@ -13,8 +13,6 @@ FP4X4 = mybir.dt.float4_e2m1fn_x4
 RELU = mybir.ActivationFunctionType.Relu
 COPY = mybir.ActivationFunctionType.Copy
 MAX = mybir.AluOpType.max
-MULT = mybir.AluOpType.mult
-ADD = mybir.AluOpType.add
 
 P = 128
 PACK = 4
@@ -111,22 +109,13 @@ def tile_picked_wsagecat_max_lo_kernel(
         for d in range(3):
             for u in range(2):
                 nc.scalar.activation(g_sca[d][:, u, :], h[u][:].indirect(lists[d][:]), COPY)
-        g3 = new_tile("g3", [P, PACK, T], F32)
-        for v0, n in ((0, 256), (256, 128), (384, 128)):
-            for t in range(PACK):
-                nc.scalar.activation(
-                    g3[:, t, v0 : v0 + n], plane(t).indirect(lists[3][:, v0 // 16 : (v0 + n) // 16]), COPY
-                )
-
+        h_pairs = new_tile("h_pairs", [P, 2, T, 2], BF16)
         h_bf = new_tile("h_bf", [P, PACK * T], BF16)
-        for half in range(2):
-            for u in range(2):
-                cols = slice(256 * half, 256 * (half + 1))
-                nc.gpsimd.tensor_scalar(
-                    h_bf[:].rearrange("p (v u e) -> p u v e", u=2, e=2)[:, u, cols],
-                    h[u][:, 0 : 2 * T].rearrange("p (e v) -> p v e", e=2)[:, cols],
-                    1.0, 0.0, MULT, ADD,
-                )
+        for u in range(2):
+            nc.vector.tensor_copy(
+                out=h_pairs[:, u].rearrange("p (c i) e -> p c e i", i=4),
+                in_=h[u][:, 0 : 2 * T].rearrange("p (e c i) -> p c e i", e=2, i=4),
+            )
         w_bf = [new_tile("w_bf%d" % n, [P, PACK * H], BF16) for n in range(2)]
 
         def weight_views(n, a0, a1):
@@ -135,9 +124,16 @@ def tile_picked_wsagecat_max_lo_kernel(
                 w_raw[n][:].rearrange("p s (a t) -> p a t s", t=PACK)[:, a0:a1],
             )
 
-        for quarter in range(4):
-            dst, src = weight_views(0, 32 * quarter, 32 * (quarter + 1))
-            nc.gpsimd.tensor_scalar(dst, src, 1.0, 0.0, MULT, ADD)
+        for half in range(2):
+            dst, src = weight_views(0, 64 * half, 64 * (half + 1))
+            nc.scalar.copy(out=dst, in_=src)
+
+        g3 = new_tile("g3", [P, PACK, T], F32)
+        for v0, n in ((0, 256), (256, 128), (384, 128)):
+            for t in range(PACK):
+                nc.scalar.activation(
+                    g3[:, t, v0 : v0 + n], plane(t).indirect(lists[3][:, v0 // 16 : (v0 + n) // 16]), COPY
+                )
 
         h_codes = new_tile("h_codes", [P, T], U32)
         h_scales = new_tile("h_scales", [P, T], U8)
@@ -152,6 +148,9 @@ def tile_picked_wsagecat_max_lo_kernel(
         max3 = new_tile("max3", [P, PACK, T], BF16)
         max3_ue = max3[:].rearrange("p (u e) v -> p e u v", e=2)
         fold(max2_vec[:], g_vec[0][:], g_vec[1][:])
+        nc.vector.tensor_copy(
+            out=h_bf[:].rearrange("p (v u e) -> p v u e", u=2, e=2), in_=h_pairs[:].rearrange("p u v e -> p v u e")
+        )
         dst, src = weight_views(1, 0, P)
         nc.vector.tensor_copy(out=dst, in_=src)
         fold(

@@ -13,6 +13,8 @@ FP4X4 = mybir.dt.float4_e2m1fn_x4
 RELU = mybir.ActivationFunctionType.Relu
 COPY = mybir.ActivationFunctionType.Copy
 MAX = mybir.AluOpType.max
+MULT = mybir.AluOpType.mult
+ADD = mybir.AluOpType.add
 
 P = 128
 PACK = 4
@@ -29,10 +31,14 @@ def tile_picked_wsagecat_max_lo_kernel(
     with ExitStack() as ctx:
         lists_pool = ctx.enter_context(tc.tile_pool(name="lists", bufs=1))
         sb = ctx.enter_context(tc.tile_pool(name="sb", bufs=1))
+        shared = ctx.enter_context(tc.tile_pool(name="shared", bufs=1))
         psum = ctx.enter_context(tc.psum_pool(name="psum", bufs=1))
 
         def new_tile(name, shape, dtype):
             return sb.tile(shape, dtype, name=name, align_bytes=64)
+
+        def tile_at(name, shape, dtype, offset):
+            return shared.tile(shape, dtype, name=name, align_bytes=64, offset=offset)
 
         def quantize(codes, scales, src):
             nc.vector.quantize_mx(out=codes.bitcast(FP8X4), scales=scales, in_=src)
@@ -50,13 +56,16 @@ def tile_picked_wsagecat_max_lo_kernel(
                 out=xs[32 * q : 32 * q + 4, :].bitcast(I32), in_=x_scales[0, 4 * q : 4 * q + 4, :].bitcast(I32)
             )
         lists = [lists_pool.tile([P, T // 16], U16, name="pos%d" % d) for d in range(4)]
-        w_raw = [new_tile("w_raw%d" % n, [P, PACK, H], F32) for n in range(2)]
+        w2_raw = [new_tile("w2_raw%d" % c, [P, PACK, H // 2], F32) for c in range(2)]
+        w3_raw = new_tile("w3_raw", [P, PACK, H], F32)
+        w2_rows = w2.rearrange("(p s) c -> p s c", s=PACK)
         nc.sync.dma_start(lists[0][:], pos1)
-        nc.sync.dma_start(out=w_raw[0][:], in_=w2.rearrange("(p s) c -> p s c", s=PACK))
+        nc.sync.dma_start(out=w2_raw[0][:], in_=w2_rows[:, :, 0:256])
         nc.sync.dma_start(lists[1][:], pos2)
+        nc.sync.dma_start(out=w2_raw[1][:], in_=w2_rows[:, :, 256:512])
         nc.sync.dma_start(lists[2][:], pos3)
         nc.sync.dma_start(lists[3][:], pos4)
-        nc.sync.dma_start(out=w_raw[1][:], in_=w3.rearrange("(p s) c -> p s c", s=PACK))
+        nc.sync.dma_start(out=w3_raw[:], in_=w3.rearrange("(p s) c -> p s c", s=PACK))
 
         banks_p = [psum.tile([P, T], F32, name="bank_p%d" % t) for t in range(PACK)]
         banks_q = [psum.tile([P, T], F32, name="bank_q%d" % t) for t in range(PACK)]
@@ -109,24 +118,18 @@ def tile_picked_wsagecat_max_lo_kernel(
         for d in range(3):
             for u in range(2):
                 nc.scalar.activation(g_sca[d][:, u, :], h[u][:].indirect(lists[d][:]), COPY)
-        h_pairs = new_tile("h_pairs", [P, 2, T, 2], BF16)
-        h_bf = new_tile("h_bf", [P, PACK * T], BF16)
+        h_pairs = tile_at("h_pairs", [P, 2, T, 2], BF16, 0)
+        h_bf = tile_at("h_bf", [P, PACK * T], BF16, 4096)
+        w_bf = [new_tile("w2_bf", [P, PACK * H], BF16), tile_at("w3_bf", [P, PACK * H], BF16, 0)]
         for u in range(2):
-            nc.vector.tensor_copy(
-                out=h_pairs[:, u].rearrange("p (c i) e -> p c e i", i=4),
-                in_=h[u][:, 0 : 2 * T].rearrange("p (e c i) -> p c e i", e=2, i=4),
+            nc.gpsimd.tensor_scalar(
+                w_bf[0][:].rearrange("p (t a s) -> p a t s", t=PACK, s=PACK)[:, 64 * u : 64 * (u + 1)],
+                w2_raw[u][:].rearrange("p s (a t) -> p a t s", t=PACK),
+                1.0, 0.0, MULT, ADD,
             )
-        w_bf = [new_tile("w_bf%d" % n, [P, PACK * H], BF16) for n in range(2)]
-
-        def weight_views(n, a0, a1):
-            return (
-                w_bf[n][:].rearrange("p (t a s) -> p a t s", t=PACK, s=PACK)[:, a0:a1],
-                w_raw[n][:].rearrange("p s (a t) -> p a t s", t=PACK)[:, a0:a1],
+            nc.gpsimd.tensor_scalar(
+                h_pairs[:, u], h[u][:, 0 : 2 * T].rearrange("p (e v) -> p v e", e=2), 1.0, 0.0, MULT, ADD
             )
-
-        for half in range(2):
-            dst, src = weight_views(0, 64 * half, 64 * (half + 1))
-            nc.scalar.copy(out=dst, in_=src)
 
         g3 = new_tile("g3", [P, PACK, T], F32)
         for v0, n in ((0, 256), (256, 128), (384, 128)):
@@ -143,26 +146,28 @@ def tile_picked_wsagecat_max_lo_kernel(
         def fold(dst, acc, other):
             nc.vector.tensor_tensor(dst, acc, other, MAX)
 
-        max2_vec = new_tile("max2_vec", [P, 2, 2, 256], BF16)
-        max2_sca = new_tile("max2_sca", [P, 2, T], BF16)
+        max2_vec = tile_at("max2_vec", [P, 2, 2, 256], BF16, 4096)
+        max2_sca = tile_at("max2_sca", [P, 2, T], BF16, 6144)
         max3 = new_tile("max3", [P, PACK, T], BF16)
         max3_ue = max3[:].rearrange("p (u e) v -> p e u v", e=2)
-        fold(max2_vec[:], g_vec[0][:], g_vec[1][:])
+        quantize(w_codes[0][:], w_scales[0][:], w_bf[0][:])
         nc.vector.tensor_copy(
             out=h_bf[:].rearrange("p (v u e) -> p v u e", u=2, e=2), in_=h_pairs[:].rearrange("p u v e -> p v u e")
         )
-        dst, src = weight_views(1, 0, P)
-        nc.vector.tensor_copy(out=dst, in_=src)
+        nc.vector.tensor_copy(
+            out=w_bf[1][:].rearrange("p (t a s) -> p a s t", t=PACK, s=PACK),
+            in_=w3_raw[:].rearrange("p s (a t) -> p a s t", t=PACK),
+        )
+        quantize(h_codes[:], h_scales[:], h_bf[:])
+        quantize(w_codes[1][:], w_scales[1][:], w_bf[1][:])
+        fold(max2_vec[:], g_vec[0][:], g_vec[1][:])
+        fold(max2_sca[:], g_sca[0][:], g_sca[1][:])
         fold(
             max3_ue[:, 1].rearrange("p u (r v) -> p u r v", r=2),
             max2_vec[:].rearrange("p r u v -> p u r v"),
             g_vec[2][:].rearrange("p r u v -> p u r v"),
         )
-        quantize(h_codes[:], h_scales[:], h_bf[:])
-        fold(max2_sca[:], g_sca[0][:], g_sca[1][:])
-        quantize(w_codes[1][:], w_scales[1][:], w_bf[1][:])
         fold(max3_ue[:, 0], max2_sca[:], g_sca[2][:])
-        quantize(w_codes[0][:], w_scales[0][:], w_bf[0][:])
 
         y_words = new_tile("y_words", [P, T], U32)
         y_scales = new_tile("y_scales", [P, T], U8)
@@ -172,7 +177,7 @@ def tile_picked_wsagecat_max_lo_kernel(
         z_scales = new_tile("z_scales", [P, T], U8)
         z_bf = [new_tile("z_bf%d" % ci, [P, PACK * P], BF16) for ci in range(4)]
         y = [new_tile("y%d" % ci, [P, PACK, P], F32) for ci in range(4)]
-        y_bf = [new_tile("y_bf%d" % ci, [P, PACK * P], BF16) for ci in range(4)]
+        y_bf = new_tile("y_bf", [P, PACK * T], BF16)
 
         def second_pass(out, n, codes, scales, t, v0, start, stop):
             cols = slice(P * t, P * (t + 1))
@@ -182,12 +187,9 @@ def tile_picked_wsagecat_max_lo_kernel(
                 start=start, stop=stop,
             )
 
-        def region(ci, t):
-            return banks_q[t][:, 0:P] if ci == 3 else banks_p[ci][:, P * t : P * (t + 1)]
-
         for ci in range(4):
             for t in range(PACK):
-                second_pass(region(ci, t), 0, h_codes, h_scales, t, P * ci, ci == 3 or t == 0, False)
+                second_pass(banks_p[ci][:, P * t : P * (t + 1)], 0, h_codes, h_scales, t, P * ci, t == 0, False)
 
         def z_chunk(ci):
             cols = slice(P * ci, P * (ci + 1))
@@ -201,24 +203,30 @@ def tile_picked_wsagecat_max_lo_kernel(
             cols = slice(P * ci, P * (ci + 1))
             quantize(z_codes[:, cols], z_scales[:, cols], z_bf[ci][:])
             for t in range(PACK):
-                second_pass(region(ci, t), 1, z_codes, z_scales, t, P * ci, False, ci == 3 or t == PACK - 1)
-            if ci < 3:
-                nc.scalar.copy(out=y[ci][:].rearrange("p t v -> p (t v)"), in_=banks_p[ci][:])
-            else:
-                for t in range(PACK):
-                    copy = nc.scalar.copy if t % 2 else nc.vector.tensor_copy
-                    copy(out=y[3][:, t, :], in_=banks_q[t][:, 0:P])
-            nc.sync.dma_start(out=out_rows[:, :, cols], in_=y[ci][:])
+                second_pass(banks_p[ci][:, P * t : P * (t + 1)], 1, z_codes, z_scales, t, P * ci, False, t == PACK - 1)
+
+        def store_chunk(ci, copy):
+            copy(out=y[ci][:].rearrange("p t v -> p (t v)"), in_=banks_p[ci][:])
+            nc.sync.dma_start(out=out_rows[:, :, P * ci : P * (ci + 1)], in_=y[ci][:])
+
+        def woven(ci):
+            return y_bf[:, PACK * P * ci : PACK * P * (ci + 1)]
+
+        def weave_bank(ci):
+            nc.scalar.copy(
+                out=woven(ci).rearrange("p (v t) -> p v t", t=PACK),
+                in_=banks_p[ci][:].rearrange("p (t v) -> p v t", t=PACK),
+            )
 
         def weave(ci):
             nc.vector.tensor_copy(
-                out=y_bf[ci][:].rearrange("p (c i t) -> p c t i", i=4, t=PACK),
+                out=woven(ci).rearrange("p (c i t) -> p c t i", i=4, t=PACK),
                 in_=y[ci][:].rearrange("p t (c i) -> p c t i", i=4),
             )
 
-        def result_planes(ci):
-            cols = slice(P * ci, P * (ci + 1))
-            quantize(y_words[:, cols], y_scales[:, cols], y_bf[ci][:])
+        def result_planes(v0, n):
+            quantize(y_words[:, v0 : v0 + n], y_scales[:, v0 : v0 + n], y_bf[:, PACK * v0 : PACK * (v0 + n)])
+            nc.sync.dma_start(out=out_words[:, v0 : v0 + n], in_=y_words[:, v0 : v0 + n].bitcast(I32))
 
         z_chunk(0)
         z_chunk(1)
@@ -228,14 +236,16 @@ def tile_picked_wsagecat_max_lo_kernel(
         z_chunk(3)
         z_product(2)
         z_product(3)
-        for ci in range(4):
-            weave(ci)
-            if ci:
-                result_planes(ci - 1)
-            if ci == 3:
-                nc.sync.dma_start(out=out_words[:, 0:384], in_=y_words[:, 0:384].bitcast(I32))
-        result_planes(3)
-        nc.sync.dma_start(out=out_words[:, 384:T], in_=y_words[:, 384:T].bitcast(I32))
+        store_chunk(0, nc.scalar.copy)
+        weave_bank(0)
+        store_chunk(1, nc.scalar.copy)
+        store_chunk(2, nc.scalar.copy)
+        weave_bank(1)
+        store_chunk(3, nc.vector.tensor_copy)
+        weave(2)
+        weave(3)
+        result_planes(0, 256)
+        result_planes(256, 256)
         for q in range(4):
             queue = nc.sync if q % 2 else nc.scalar
             queue.dma_start(

@@ -20,7 +20,9 @@ P = 128
 PACK = 4
 T = 512
 H = 512
-PAD = 192
+PAD = 256
+EARLY = 384
+RUN = 64
 FLOPS = 3 * 2 * 512 * 512 * 512
 
 
@@ -70,7 +72,7 @@ def tile_picked_wsagecat_max_lo_kernel(
         banks_p = [psum.tile([P, T], F32, name="bank_p%d" % t) for t in range(PACK)]
         banks_q = [psum.tile([P, T], F32, name="bank_q%d" % t) for t in range(PACK)]
 
-        w1_bf = [new_tile("w1_bf%d" % u, [P, 2, PACK * P], BF16) for u in range(2)]
+        w1_bf = [tile_at("w1_bf%d" % u, [P, 2, PACK * P], BF16, 16384 + 2048 * u) for u in range(2)]
         w1_codes = [new_tile("w1_codes%d" % t, [P, P], U32) for t in range(PACK)]
         w1_scales = [new_tile("w1_scales%d" % t, [P, P], U8) for t in range(PACK)]
 
@@ -110,17 +112,39 @@ def tile_picked_wsagecat_max_lo_kernel(
             first_product(banks_p[t][:], t, 0, T)
             nc.scalar.activation(plane(t), banks_p[t][:], RELU)
 
-        g_vec = [new_tile("g_vec%d" % d, [P, 2, 2, 256], BF16) for d in range(3)]
+        def offsets(d, v0, n):
+            return lists[d][:, v0 // 16 : (v0 + n) // 16]
+
+        def vector_gather(dst, u, d, v0, n):
+            nc.vector.tensor_copy(out=dst[:, :, u, :], in_=h[u][:, T:].indirect(offsets(d, v0, n)))
+
+        def scalar_gather(dst, u, d):
+            nc.scalar.activation(dst[:, u, :], h[u][:].indirect(lists[d][:]), COPY)
+
+        def last_list(v0, n):
+            part = new_tile("g3_%d" % v0, [P, PACK, n], F32)
+            for c0 in range(0, n, P):
+                g3.append(part[:, :, c0 : c0 + P])
+            for t in range(PACK):
+                nc.scalar.activation(part[:, t, :], h[t // 2][:, T * (t % 2) :].indirect(offsets(3, v0, n)), COPY)
+
+        widths = (T, T, EARLY)
+        g_vec = [new_tile("g_vec%d" % d, [P, widths[d] // RUN, 2, RUN], BF16) for d in range(3)]
         g_sca = [new_tile("g_sca%d" % d, [P, 2, T], BF16) for d in range(3)]
+        g3 = []
         for d in range(3):
             for u in range(2):
-                nc.vector.tensor_copy(out=g_vec[d][:, :, u, :], in_=h[u][:, T:].indirect(lists[d][:]))
+                vector_gather(g_vec[d], u, d, 0, widths[d])
         for d in range(3):
             for u in range(2):
-                nc.scalar.activation(g_sca[d][:, u, :], h[u][:].indirect(lists[d][:]), COPY)
+                scalar_gather(g_sca[d], u, d)
+        last_list(0, 256)
+        last_list(256, P)
+        last_list(EARLY, P)
+
         h_pairs = tile_at("h_pairs", [P, 2, T, 2], BF16, 0)
         h_bf = tile_at("h_bf", [P, PACK * T], BF16, 4096)
-        w_bf = [new_tile("w2_bf", [P, PACK * H], BF16), tile_at("w3_bf", [P, PACK * H], BF16, 0)]
+        w_bf = [tile_at("w2_bf", [P, PACK * H], BF16, 16384), new_tile("w3_bf", [P, PACK * H], BF16)]
         for u in range(2):
             nc.gpsimd.tensor_scalar(
                 w_bf[0][:].rearrange("p (t a s) -> p a t s", t=PACK, s=PACK)[:, 64 * u : 64 * (u + 1)],
@@ -131,13 +155,11 @@ def tile_picked_wsagecat_max_lo_kernel(
                 h_pairs[:, u], h[u][:, 0 : 2 * T].rearrange("p (e v) -> p v e", e=2), 1.0, 0.0, MULT, ADD
             )
 
-        g3 = new_tile("g3", [P, PACK, T], F32)
-        for v0, n in ((0, 256), (256, 128), (384, 128)):
-            for t in range(PACK):
-                nc.scalar.activation(
-                    g3[:, t, v0 : v0 + n], plane(t).indirect(lists[3][:, v0 // 16 : (v0 + n) // 16]), COPY
-                )
-
+        nc.gpsimd.tensor_scalar(
+            w_bf[1][:].rearrange("p (t a s) -> p a t s", t=PACK, s=PACK)[:, 0:64],
+            w3_raw[:].rearrange("p s (a t) -> p a t s", t=PACK)[:, 0:64],
+            1.0, 0.0, MULT, ADD,
+        )
         h_codes = new_tile("h_codes", [P, T], U32)
         h_scales = new_tile("h_scales", [P, T], U8)
         w_codes = [new_tile("w_codes%d" % n, [P, H], U32) for n in range(2)]
@@ -146,7 +168,7 @@ def tile_picked_wsagecat_max_lo_kernel(
         def fold(dst, acc, other):
             nc.vector.tensor_tensor(dst, acc, other, MAX)
 
-        max2_vec = tile_at("max2_vec", [P, 2, 2, 256], BF16, 4096)
+        max2_vec = tile_at("max2_vec", [P, T // RUN, 2, RUN], BF16, 4096)
         max2_sca = tile_at("max2_sca", [P, 2, T], BF16, 6144)
         max3 = new_tile("max3", [P, PACK, T], BF16)
         max3_ue = max3[:].rearrange("p (u e) v -> p e u v", e=2)
@@ -155,18 +177,22 @@ def tile_picked_wsagecat_max_lo_kernel(
             out=h_bf[:].rearrange("p (v u e) -> p v u e", u=2, e=2), in_=h_pairs[:].rearrange("p u v e -> p v u e")
         )
         nc.vector.tensor_copy(
-            out=w_bf[1][:].rearrange("p (t a s) -> p a s t", t=PACK, s=PACK),
-            in_=w3_raw[:].rearrange("p s (a t) -> p a s t", t=PACK),
+            out=w_bf[1][:].rearrange("p (t a s) -> p a s t", t=PACK, s=PACK)[:, 64:P],
+            in_=w3_raw[:].rearrange("p s (a t) -> p a s t", t=PACK)[:, 64:P],
         )
         quantize(h_codes[:], h_scales[:], h_bf[:])
         quantize(w_codes[1][:], w_scales[1][:], w_bf[1][:])
         fold(max2_vec[:], g_vec[0][:], g_vec[1][:])
         fold(max2_sca[:], g_sca[0][:], g_sca[1][:])
-        fold(
-            max3_ue[:, 1].rearrange("p u (r v) -> p u r v", r=2),
-            max2_vec[:].rearrange("p r u v -> p u r v"),
-            g_vec[2][:].rearrange("p r u v -> p u r v"),
-        )
+
+        def third_maximum(v0, n, from_vec):
+            fold(
+                max3_ue[:, 1, :, v0 : v0 + n].rearrange("p u (r v) -> p u r v", v=RUN),
+                max2_vec[:, v0 // RUN : (v0 + n) // RUN].rearrange("p r u v -> p u r v"),
+                from_vec[:].rearrange("p r u v -> p u r v"),
+            )
+
+        third_maximum(0, EARLY, g_vec[2])
         fold(max3_ue[:, 0], max2_sca[:], g_sca[2][:])
 
         y_words = new_tile("y_words", [P, T], U32)
@@ -175,9 +201,9 @@ def tile_picked_wsagecat_max_lo_kernel(
         out_words = out_1[0].rearrange("p c r -> p (c r)").bitcast(I32)
         z_codes = new_tile("z_codes", [P, T], U32)
         z_scales = new_tile("z_scales", [P, T], U8)
-        z_bf = [new_tile("z_bf%d" % ci, [P, PACK * P], BF16) for ci in range(4)]
+        z_bf = [tile_at("z_bf%d" % ci, [P, PACK * P], BF16, 8192 + 1024 * ci) for ci in range(4)]
         y = [new_tile("y%d" % ci, [P, PACK, P], F32) for ci in range(4)]
-        y_bf = new_tile("y_bf", [P, PACK * T], BF16)
+        y_bf = tile_at("y_bf", [P, PACK * T], BF16, 8192 + 3072)
 
         def second_pass(out, n, codes, scales, t, v0, start, stop):
             cols = slice(P * t, P * (t + 1))
@@ -187,15 +213,20 @@ def tile_picked_wsagecat_max_lo_kernel(
                 start=start, stop=stop,
             )
 
+        def region(ci, t):
+            if ci == 3:
+                return banks_q[t // 2][:, P * (t % 2) : P * (t % 2 + 1)]
+            return banks_p[ci][:, P * t : P * (t + 1)]
+
         for ci in range(4):
             for t in range(PACK):
-                second_pass(banks_p[ci][:, P * t : P * (t + 1)], 0, h_codes, h_scales, t, P * ci, t == 0, False)
+                second_pass(region(ci, t), 0, h_codes, h_scales, t, P * ci, t == 0 or (ci == 3 and t == 2), False)
 
         def z_chunk(ci):
             cols = slice(P * ci, P * (ci + 1))
             fold(
                 z_bf[ci][:].rearrange("p (a i t) -> p a t i", i=2, t=PACK),
-                g3[:, :, cols].rearrange("p t (a i) -> p a t i", i=2),
+                g3[ci].rearrange("p t (a i) -> p a t i", i=2),
                 max3[:, :, cols].rearrange("p t (a i) -> p a t i", i=2),
             )
 
@@ -203,7 +234,7 @@ def tile_picked_wsagecat_max_lo_kernel(
             cols = slice(P * ci, P * (ci + 1))
             quantize(z_codes[:, cols], z_scales[:, cols], z_bf[ci][:])
             for t in range(PACK):
-                second_pass(banks_p[ci][:, P * t : P * (t + 1)], 1, z_codes, z_scales, t, P * ci, False, t == PACK - 1)
+                second_pass(region(ci, t), 1, z_codes, z_scales, t, P * ci, False, t == 3 or (ci == 3 and t == 1))
 
         def store_chunk(ci, copy):
             copy(out=y[ci][:].rearrange("p t v -> p (t v)"), in_=banks_p[ci][:])
@@ -233,18 +264,24 @@ def tile_picked_wsagecat_max_lo_kernel(
         z_product(0)
         z_chunk(2)
         z_product(1)
-        z_chunk(3)
+        g_vec_late = tile_at("g_vec_late", [P, P // RUN, 2, RUN], BF16, 8192)
+        vector_gather(g_vec_late, 0, 2, EARLY, P)
+        vector_gather(g_vec_late, 1, 2, EARLY, P)
+        third_maximum(EARLY, P, g_vec_late)
         z_product(2)
+        z_chunk(3)
         z_product(3)
         store_chunk(0, nc.scalar.copy)
-        weave_bank(0)
         store_chunk(1, nc.scalar.copy)
         store_chunk(2, nc.scalar.copy)
-        weave_bank(1)
-        store_chunk(3, nc.vector.tensor_copy)
-        weave(2)
-        weave(3)
+        weave(0)
+        weave(1)
+        weave_bank(2)
         result_planes(0, 256)
+        for half, copy in enumerate((nc.vector.tensor_copy, nc.scalar.copy)):
+            copy(out=y[3][:, 2 * half : 2 * half + 2, :].rearrange("p t v -> p (t v)"), in_=banks_q[half][:, 0 : 2 * P])
+        nc.sync.dma_start(out=out_rows[:, :, EARLY:T], in_=y[3][:])
+        weave(3)
         result_planes(256, 256)
         for q in range(4):
             queue = nc.sync if q % 2 else nc.scalar

@@ -122,7 +122,7 @@ def tile_picked_wsagecat_max_lo_kernel(
             nc.scalar.activation(dst[:, u, :], h[u][:].indirect(lists[d][:]), COPY)
 
         def last_list(v0, n):
-            part = new_tile("g3_%d" % v0, [P, PACK, n], F32)
+            part = tile_at("g3_%d" % v0, [P, PACK, n], F32, 24576 + 16 * v0)
             for c0 in range(0, n, P):
                 g3.append(part[:, :, c0 : c0 + P])
             for t in range(PACK):
@@ -155,11 +155,6 @@ def tile_picked_wsagecat_max_lo_kernel(
                 h_pairs[:, u], h[u][:, 0 : 2 * T].rearrange("p (e v) -> p v e", e=2), 1.0, 0.0, MULT, ADD
             )
 
-        nc.gpsimd.tensor_scalar(
-            w_bf[1][:].rearrange("p (t a s) -> p a t s", t=PACK, s=PACK)[:, 0:64],
-            w3_raw[:].rearrange("p s (a t) -> p a t s", t=PACK)[:, 0:64],
-            1.0, 0.0, MULT, ADD,
-        )
         h_codes = new_tile("h_codes", [P, T], U32)
         h_scales = new_tile("h_scales", [P, T], U8)
         w_codes = [new_tile("w_codes%d" % n, [P, H], U32) for n in range(2)]
@@ -177,8 +172,8 @@ def tile_picked_wsagecat_max_lo_kernel(
             out=h_bf[:].rearrange("p (v u e) -> p v u e", u=2, e=2), in_=h_pairs[:].rearrange("p u v e -> p v u e")
         )
         nc.vector.tensor_copy(
-            out=w_bf[1][:].rearrange("p (t a s) -> p a s t", t=PACK, s=PACK)[:, 64:P],
-            in_=w3_raw[:].rearrange("p s (a t) -> p a s t", t=PACK)[:, 64:P],
+            out=w_bf[1][:].rearrange("p (t a s) -> p a s t", t=PACK, s=PACK),
+            in_=w3_raw[:].rearrange("p s (a t) -> p a s t", t=PACK),
         )
         quantize(h_codes[:], h_scales[:], h_bf[:])
         quantize(w_codes[1][:], w_scales[1][:], w_bf[1][:])
@@ -196,14 +191,14 @@ def tile_picked_wsagecat_max_lo_kernel(
         fold(max3_ue[:, 0], max2_sca[:], g_sca[2][:])
 
         y_words = new_tile("y_words", [P, T], U32)
-        y_scales = new_tile("y_scales", [P, T], U8)
+        y_scales = tile_at("y_scales", [P, T], U8, 8192 + 3072)
         out_rows = out_0.rearrange("(p t) v -> p t v", t=PACK)
         out_words = out_1[0].rearrange("p c r -> p (c r)").bitcast(I32)
         z_codes = new_tile("z_codes", [P, T], U32)
         z_scales = new_tile("z_scales", [P, T], U8)
         z_bf = [tile_at("z_bf%d" % ci, [P, PACK * P], BF16, 8192 + 1024 * ci) for ci in range(4)]
         y = [new_tile("y%d" % ci, [P, PACK, P], F32) for ci in range(4)]
-        y_bf = tile_at("y_bf", [P, PACK * T], BF16, 8192 + 3072)
+        y_bf = []
 
         def second_pass(out, n, codes, scales, t, v0, start, stop):
             cols = slice(P * t, P * (t + 1))
@@ -241,7 +236,7 @@ def tile_picked_wsagecat_max_lo_kernel(
             nc.sync.dma_start(out=out_rows[:, :, P * ci : P * (ci + 1)], in_=y[ci][:])
 
         def woven(ci):
-            return y_bf[:, PACK * P * ci : PACK * P * (ci + 1)]
+            return y_bf[ci // 2][:, PACK * P * (ci % 2) : PACK * P * (ci % 2 + 1)]
 
         def weave_bank(ci):
             nc.scalar.copy(
@@ -256,7 +251,10 @@ def tile_picked_wsagecat_max_lo_kernel(
             )
 
         def result_planes(v0, n):
-            quantize(y_words[:, v0 : v0 + n], y_scales[:, v0 : v0 + n], y_bf[:, PACK * v0 : PACK * (v0 + n)])
+            src = y_bf[v0 // 256][:, PACK * (v0 % 256) : PACK * (v0 % 256 + n)]
+            quantize(y_words[:, v0 : v0 + n], y_scales[:, v0 : v0 + n], src)
+
+        def store_words(v0, n):
             nc.sync.dma_start(out=out_words[:, v0 : v0 + n], in_=y_words[:, v0 : v0 + n].bitcast(I32))
 
         z_chunk(0)
@@ -271,6 +269,8 @@ def tile_picked_wsagecat_max_lo_kernel(
         z_product(2)
         z_chunk(3)
         z_product(3)
+        y_bf.append(tile_at("y_bf0", [P, PACK * 256], BF16, 24576 + 16 * EARLY))
+        y_bf.append(new_tile("y_bf1", [P, PACK * 256], BF16))
         store_chunk(0, nc.scalar.copy)
         store_chunk(1, nc.scalar.copy)
         store_chunk(2, nc.scalar.copy)
@@ -278,11 +278,14 @@ def tile_picked_wsagecat_max_lo_kernel(
         weave(1)
         weave_bank(2)
         result_planes(0, 256)
+        store_words(0, 256)
         for half, copy in enumerate((nc.vector.tensor_copy, nc.scalar.copy)):
             copy(out=y[3][:, 2 * half : 2 * half + 2, :].rearrange("p t v -> p (t v)"), in_=banks_q[half][:, 0 : 2 * P])
         nc.sync.dma_start(out=out_rows[:, :, EARLY:T], in_=y[3][:])
         weave(3)
-        result_planes(256, 256)
+        result_planes(256, P)
+        result_planes(EARLY, P)
+        store_words(256, 256)
         for q in range(4):
             queue = nc.sync if q % 2 else nc.scalar
             queue.dma_start(

@@ -21,8 +21,7 @@ PACK = 4
 T = 512
 H = 512
 PAD = 256
-EARLY = 384
-RUN = 64
+HALF = 256
 FLOPS = 3 * 2 * 512 * 512 * 512
 
 
@@ -48,9 +47,9 @@ def tile_picked_wsagecat_max_lo_kernel(
         xs = new_tile("xs", [P, T], U8)
         nc.vector.memset(xs[:].bitcast(I32), 0)
         w1_rows = w1.rearrange("(p j) c -> p j c", j=PACK)
-        w1_raw = [new_tile("w1_raw%d" % c, [P, PACK, H // 2], F32) for c in range(2)]
+        w1_raw = [new_tile("w1_raw%d" % c, [P, PACK, HALF], F32) for c in range(2)]
         for c in range(2):
-            nc.sync.dma_start(out=w1_raw[c][:], in_=w1_rows[:, :, 256 * c : 256 * (c + 1)])
+            nc.sync.dma_start(out=w1_raw[c][:], in_=w1_rows[:, :, HALF * c : HALF * (c + 1)])
         xw = new_tile("xw", [P, 2 * T], U8)
         nc.sync.dma_start(out=xw[:].bitcast(I32), in_=x_words[0].bitcast(I32))
         for q in range(4):
@@ -58,21 +57,22 @@ def tile_picked_wsagecat_max_lo_kernel(
                 out=xs[32 * q : 32 * q + 4, :].bitcast(I32), in_=x_scales[0, 4 * q : 4 * q + 4, :].bitcast(I32)
             )
         lists = [lists_pool.tile([P, T // 16], U16, name="pos%d" % d) for d in range(4)]
-        w2_raw = [new_tile("w2_raw%d" % c, [P, PACK, H // 2], F32) for c in range(2)]
-        w3_raw = new_tile("w3_raw", [P, PACK, H], F32)
+        w2_raw = [tile_at("w2_raw0", [P, PACK, HALF], F32, 16384), new_tile("w2_raw1", [P, PACK, HALF], F32)]
+        w3_raw = [new_tile("w3_raw0", [P, PACK, HALF], F32)]
         w2_rows = w2.rearrange("(p s) c -> p s c", s=PACK)
+        w3_rows = w3.rearrange("(p s) c -> p s c", s=PACK)
         nc.sync.dma_start(lists[0][:], pos1)
-        nc.sync.dma_start(out=w2_raw[0][:], in_=w2_rows[:, :, 0:256])
+        nc.sync.dma_start(out=w3_raw[0][:], in_=w3_rows[:, :, 0:HALF])
         nc.sync.dma_start(lists[1][:], pos2)
-        nc.sync.dma_start(out=w2_raw[1][:], in_=w2_rows[:, :, 256:512])
+        nc.sync.dma_start(out=w2_raw[0][:], in_=w2_rows[:, :, 0:HALF])
         nc.sync.dma_start(lists[2][:], pos3)
         nc.sync.dma_start(lists[3][:], pos4)
-        nc.sync.dma_start(out=w3_raw[:], in_=w3.rearrange("(p s) c -> p s c", s=PACK))
+        nc.sync.dma_start(out=w2_raw[1][:], in_=w2_rows[:, :, HALF:H])
 
         banks_p = [psum.tile([P, T], F32, name="bank_p%d" % t) for t in range(PACK)]
         banks_q = [psum.tile([P, T], F32, name="bank_q%d" % t) for t in range(PACK)]
 
-        w1_bf = [tile_at("w1_bf%d" % u, [P, 2, PACK * P], BF16, 16384 + 2048 * u) for u in range(2)]
+        w1_bf = [tile_at("w1_bf%d" % u, [P, 2, PACK * P], BF16, 2048 * u) for u in range(2)]
         w1_codes = [new_tile("w1_codes%d" % t, [P, P], U32) for t in range(PACK)]
         w1_scales = [new_tile("w1_scales%d" % t, [P, P], U8) for t in range(PACK)]
 
@@ -100,51 +100,51 @@ def tile_picked_wsagecat_max_lo_kernel(
             )
 
         quantize(w1_codes[1][:], w1_scales[1][:], w1_bf[0][:, 1, :])
-        for piece, bank in enumerate(banks_q):
-            c0 = P * piece
-            first_product(bank[:, 0:P], 1, c0, P)
-            if piece % 2:
-                nc.vector.tensor_scalar_max(plane(1)[:, c0 : c0 + P], bank[:, 0:P], 0.0)
-            else:
-                nc.scalar.activation(plane(1)[:, c0 : c0 + P], bank[:, 0:P], RELU)
+        for piece in range(2):
+            c0 = HALF * piece
+            first_product(banks_q[piece][:, 0:HALF], 1, c0, HALF)
+            nc.scalar.activation(plane(1)[:, c0 : c0 + HALF], banks_q[piece][:, 0:HALF], RELU)
         for t in (0, 3, 2):
             quantize(w1_codes[t][:], w1_scales[t][:], w1_bf[t // 2][:, t % 2, :])
             first_product(banks_p[t][:], t, 0, T)
             nc.scalar.activation(plane(t), banks_p[t][:], RELU)
 
+        w_bf = [new_tile("w2_bf", [P, PACK * H], BF16), tile_at("w3_bf", [P, PACK * H], BF16, 0)]
+
+        def round_w3(c):
+            nc.vector.tensor_copy(
+                out=w_bf[1][:].rearrange("p (t a e u) -> p a e u t", t=PACK, e=2, u=2)[:, 64 * c : 64 * (c + 1)],
+                in_=w3_raw[c][:].rearrange("p (u e) (a t) -> p a e u t", t=PACK, e=2),
+            )
+
+        round_w3(0)
+
+        h_late = [new_tile("h_late%d" % u, [P, T], F32) for u in range(2)]
+        for u in range(2):
+            nc.sync.dma_start(out=h_late[u][:], in_=plane(2 * u + 1))
+
         def offsets(d, v0, n):
             return lists[d][:, v0 // 16 : (v0 + n) // 16]
 
-        def vector_gather(dst, u, d, v0, n):
-            nc.vector.tensor_copy(out=dst[:, :, u, :], in_=h[u][:, T:].indirect(offsets(d, v0, n)))
-
-        def scalar_gather(dst, u, d):
-            nc.scalar.activation(dst[:, u, :], h[u][:].indirect(lists[d][:]), COPY)
-
-        def last_list(v0, n):
-            part = tile_at("g3_%d" % v0, [P, PACK, n], F32, 24576 + 16 * v0)
-            for c0 in range(0, n, P):
-                g3.append(part[:, :, c0 : c0 + P])
-            for t in range(PACK):
-                nc.scalar.activation(part[:, t, :], h[t // 2][:, T * (t % 2) :].indirect(offsets(3, v0, n)), COPY)
-
-        widths = (T, T, EARLY)
-        g_vec = [new_tile("g_vec%d" % d, [P, widths[d] // RUN, 2, RUN], BF16) for d in range(3)]
-        g_sca = [new_tile("g_sca%d" % d, [P, 2, T], BF16) for d in range(3)]
-        g3 = []
+        g = [new_tile("g%d" % d, [P, 2, T, 2], BF16) for d in range(3)]
         for d in range(3):
             for u in range(2):
-                vector_gather(g_vec[d], u, d, 0, widths[d])
+                nc.vector.tensor_copy(out=g[d][:, 1, :, u], in_=h[u][:, T:].indirect(lists[d][:]))
         for d in range(3):
             for u in range(2):
-                scalar_gather(g_sca[d], u, d)
-        last_list(0, 256)
-        last_list(256, P)
-        last_list(EARLY, P)
+                nc.scalar.activation(g[d][:, 0, :, u], h[u][:].indirect(lists[d][:]), COPY)
+        parts = ((0, 256), (256, 128), (384, 128))
+        g3 = [new_tile("g3_0", [P, 2, HALF, 2], BF16)]
 
-        h_pairs = tile_at("h_pairs", [P, 2, T, 2], BF16, 0)
-        h_bf = tile_at("h_bf", [P, PACK * T], BF16, 4096)
-        w_bf = [tile_at("w2_bf", [P, PACK * H], BF16, 16384), new_tile("w3_bf", [P, PACK * H], BF16)]
+        def last_list(c):
+            for e, windows in enumerate((h, h_late)):
+                for u in range(2):
+                    nc.scalar.activation(g3[c][:, e, :, u], windows[u][:].indirect(offsets(3, HALF * c, HALF)), COPY)
+
+        last_list(0)
+
+        h_pairs = tile_at("h_pairs", [P, 2, T, 2], BF16, 8192)
+        h_bf = new_tile("h_bf", [P, T, 2, 2], BF16)
         for u in range(2):
             nc.gpsimd.tensor_scalar(
                 w_bf[0][:].rearrange("p (t a s) -> p a t s", t=PACK, s=PACK)[:, 64 * u : 64 * (u + 1)],
@@ -160,132 +160,113 @@ def tile_picked_wsagecat_max_lo_kernel(
         w_codes = [new_tile("w_codes%d" % n, [P, H], U32) for n in range(2)]
         w_scales = [new_tile("w_scales%d" % n, [P, H], U8) for n in range(2)]
 
+        w3_raw.append(tile_at("w3_raw1", [P, PACK, HALF], F32, 16384))
+        nc.sync.dma_start(out=w3_raw[1][:], in_=w3_rows[:, :, HALF:H])
+        round_w3(1)
+        quantize(w_codes[0][:], w_scales[0][:], w_bf[0][:])
+        quantize(w_codes[1][:], w_scales[1][:], w_bf[1][:])
+        nc.vector.tensor_copy(out=h_bf[:], in_=h_pairs[:].rearrange("p u v e -> p v u e"))
+        quantize(h_codes[:], h_scales[:], h_bf[:].rearrange("p v e u -> p (v e u)"))
+        g3.append(tile_at("g3_1", [P, 2, HALF, 2], BF16, 10304))
+        last_list(1)
+
         def fold(dst, acc, other):
             nc.vector.tensor_tensor(dst, acc, other, MAX)
 
-        max2_vec = tile_at("max2_vec", [P, T // RUN, 2, RUN], BF16, 4096)
-        max2_sca = tile_at("max2_sca", [P, 2, T], BF16, 6144)
-        max3 = new_tile("max3", [P, PACK, T], BF16)
-        max3_ue = max3[:].rearrange("p (u e) v -> p e u v", e=2)
-        quantize(w_codes[0][:], w_scales[0][:], w_bf[0][:])
-        nc.vector.tensor_copy(
-            out=h_bf[:].rearrange("p (v u e) -> p v u e", u=2, e=2), in_=h_pairs[:].rearrange("p u v e -> p v u e")
-        )
-        nc.vector.tensor_copy(
-            out=w_bf[1][:].rearrange("p (t a s) -> p a s t", t=PACK, s=PACK),
-            in_=w3_raw[:].rearrange("p s (a t) -> p a s t", t=PACK),
-        )
-        quantize(h_codes[:], h_scales[:], h_bf[:])
-        quantize(w_codes[1][:], w_scales[1][:], w_bf[1][:])
-        fold(max2_vec[:], g_vec[0][:], g_vec[1][:])
-        fold(max2_sca[:], g_sca[0][:], g_sca[1][:])
+        max2 = [tile_at("max2_%d" % c, [P, 2, HALF, 2], BF16, 6208 + 2048 * c) for c in range(2)]
+        max3 = [new_tile("max3_%d" % v0, [P, 2, n, 2], BF16) for v0, n in parts]
 
-        def third_maximum(v0, n, from_vec):
-            fold(
-                max3_ue[:, 1, :, v0 : v0 + n].rearrange("p u (r v) -> p u r v", v=RUN),
-                max2_vec[:, v0 // RUN : (v0 + n) // RUN].rearrange("p r u v -> p u r v"),
-                from_vec[:].rearrange("p r u v -> p u r v"),
-            )
+        def in_half(tiles, k):
+            v0, n = parts[k]
+            return tiles[v0 // HALF][:, :, v0 % HALF : v0 % HALF + n]
 
-        third_maximum(0, EARLY, g_vec[2])
-        fold(max3_ue[:, 0], max2_sca[:], g_sca[2][:])
+        def first_maximum(c):
+            cols = slice(HALF * c, HALF * (c + 1))
+            fold(max2[c][:], g[0][:, :, cols], g[1][:, :, cols])
+
+        def second_maximum(k):
+            v0, n = parts[k]
+            fold(max3[k][:], in_half(max2, k), g[2][:, :, v0 : v0 + n])
 
         y_words = new_tile("y_words", [P, T], U32)
-        y_scales = tile_at("y_scales", [P, T], U8, 8192 + 3072)
+        y_scales = new_tile("y_scales", [P, T], U8)
         out_rows = out_0.rearrange("(p t) v -> p t v", t=PACK)
         out_words = out_1[0].rearrange("p c r -> p (c r)").bitcast(I32)
         z_codes = new_tile("z_codes", [P, T], U32)
         z_scales = new_tile("z_scales", [P, T], U8)
-        z_bf = [tile_at("z_bf%d" % ci, [P, PACK * P], BF16, 8192 + 1024 * ci) for ci in range(4)]
-        y = [new_tile("y%d" % ci, [P, PACK, P], F32) for ci in range(4)]
-        y_bf = []
+        z_bf = [new_tile("z_bf%d" % v0, [P, n, 2, 2], BF16) for v0, n in parts]
+        y = [new_tile("y%d" % v0, [P, PACK, n], F32) for v0, n in parts]
+        y_bf = [new_tile("y_bf%d" % v0, [P, PACK * n], BF16) for v0, n in parts]
+        part_banks = [(banks_p[1], banks_q[2]), (banks_q[3],), (banks_q[0], banks_q[1])]
 
-        def second_pass(out, n, codes, scales, t, v0, start, stop):
-            cols = slice(P * t, P * (t + 1))
-            nc.tensor.matmul_mx(
-                out=out, lhsT=w_codes[n][:, cols].bitcast(FP8X4), lhsT_scale=w_scales[n][:, cols],
-                rhs=codes[:, v0 : v0 + P].bitcast(FP8X4), rhs_scale=scales[:, v0 : v0 + P],
-                start=start, stop=stop,
-            )
-
-        def region(ci, t):
-            if ci == 3:
-                return banks_q[t // 2][:, P * (t % 2) : P * (t % 2 + 1)]
-            return banks_p[ci][:, P * t : P * (t + 1)]
-
-        for ci in range(4):
+        def second_passes(k, n, codes, scales):
+            v0, width = parts[k]
+            per_bank = PACK // len(part_banks[k])
             for t in range(PACK):
-                second_pass(region(ci, t), 0, h_codes, h_scales, t, P * ci, t == 0 or (ci == 3 and t == 2), False)
+                slot = t % per_bank
+                cols = slice(P * t, P * (t + 1))
+                nc.tensor.matmul_mx(
+                    out=part_banks[k][t // per_bank][:, width * slot : width * (slot + 1)],
+                    lhsT=w_codes[n][:, cols].bitcast(FP8X4), lhsT_scale=w_scales[n][:, cols],
+                    rhs=codes[:, v0 : v0 + width].bitcast(FP8X4), rhs_scale=scales[:, v0 : v0 + width],
+                    start=n == 0 and slot == 0, stop=n == 1 and slot == per_bank - 1,
+                )
 
-        def z_chunk(ci):
-            cols = slice(P * ci, P * (ci + 1))
-            fold(
-                z_bf[ci][:].rearrange("p (a i t) -> p a t i", i=2, t=PACK),
-                g3[ci].rearrange("p t (a i) -> p a t i", i=2),
-                max3[:, :, cols].rearrange("p t (a i) -> p a t i", i=2),
-            )
+        def last_maximum(k):
+            fold(z_bf[k][:], max3[k][:].rearrange("p e v u -> p v e u"), in_half(g3, k).rearrange("p e v u -> p v e u"))
 
-        def z_product(ci):
-            cols = slice(P * ci, P * (ci + 1))
-            quantize(z_codes[:, cols], z_scales[:, cols], z_bf[ci][:])
-            for t in range(PACK):
-                second_pass(region(ci, t), 1, z_codes, z_scales, t, P * ci, False, t == 3 or (ci == 3 and t == 1))
+        def z_product(k):
+            v0, n = parts[k]
+            quantize(z_codes[:, v0 : v0 + n], z_scales[:, v0 : v0 + n], z_bf[k][:].rearrange("p v e u -> p (v e u)"))
+            second_passes(k, 1, z_codes, z_scales)
 
-        def store_chunk(ci, copy):
-            copy(out=y[ci][:].rearrange("p t v -> p (t v)"), in_=banks_p[ci][:])
-            nc.sync.dma_start(out=out_rows[:, :, P * ci : P * (ci + 1)], in_=y[ci][:])
+        def read_bank(k, b, copy):
+            n = parts[k][1]
+            per_bank = PACK // len(part_banks[k])
+            planes = slice(per_bank * b, per_bank * (b + 1))
+            copy(out=y[k][:, planes, :].rearrange("p t v -> p (t v)"), in_=part_banks[k][b][:, 0 : per_bank * n])
+            return planes
 
-        def woven(ci):
-            return y_bf[ci // 2][:, PACK * P * (ci % 2) : PACK * P * (ci % 2 + 1)]
+        def store(k, planes):
+            v0, n = parts[k]
+            nc.sync.dma_start(out=out_rows[:, planes, v0 : v0 + n], in_=y[k][:, planes, :])
 
-        def weave_bank(ci):
-            nc.scalar.copy(
-                out=woven(ci).rearrange("p (v t) -> p v t", t=PACK),
-                in_=banks_p[ci][:].rearrange("p (t v) -> p v t", t=PACK),
-            )
-
-        def weave(ci):
+        def result_planes(k):
+            v0, n = parts[k]
             nc.vector.tensor_copy(
-                out=woven(ci).rearrange("p (c i t) -> p c t i", i=4, t=PACK),
-                in_=y[ci][:].rearrange("p t (c i) -> p c t i", i=4),
+                out=y_bf[k][:].rearrange("p (c i t) -> p c t i", i=4, t=PACK),
+                in_=y[k][:].rearrange("p t (c i) -> p c t i", i=4),
             )
-
-        def result_planes(v0, n):
-            src = y_bf[v0 // 256][:, PACK * (v0 % 256) : PACK * (v0 % 256 + n)]
-            quantize(y_words[:, v0 : v0 + n], y_scales[:, v0 : v0 + n], src)
+            quantize(y_words[:, v0 : v0 + n], y_scales[:, v0 : v0 + n], y_bf[k][:])
 
         def store_words(v0, n):
             nc.sync.dma_start(out=out_words[:, v0 : v0 + n], in_=y_words[:, v0 : v0 + n].bitcast(I32))
 
-        z_chunk(0)
-        z_chunk(1)
+        second_passes(0, 0, h_codes, h_scales)
+        first_maximum(0)
+        second_maximum(0)
+        last_maximum(0)
         z_product(0)
-        z_chunk(2)
+        second_passes(1, 0, h_codes, h_scales)
+        second_passes(2, 0, h_codes, h_scales)
+        first_maximum(1)
+        second_maximum(1)
+        second_maximum(2)
+        last_maximum(1)
+        last_maximum(2)
         z_product(1)
-        g_vec_late = tile_at("g_vec_late", [P, P // RUN, 2, RUN], BF16, 8192)
-        vector_gather(g_vec_late, 0, 2, EARLY, P)
-        vector_gather(g_vec_late, 1, 2, EARLY, P)
-        third_maximum(EARLY, P, g_vec_late)
         z_product(2)
-        z_chunk(3)
-        z_product(3)
-        y_bf.append(tile_at("y_bf0", [P, PACK * 256], BF16, 24576 + 16 * EARLY))
-        y_bf.append(new_tile("y_bf1", [P, PACK * 256], BF16))
-        store_chunk(0, nc.scalar.copy)
-        store_chunk(1, nc.scalar.copy)
-        store_chunk(2, nc.scalar.copy)
-        weave(0)
-        weave(1)
-        weave_bank(2)
-        result_planes(0, 256)
-        store_words(0, 256)
-        for half, copy in enumerate((nc.vector.tensor_copy, nc.scalar.copy)):
-            copy(out=y[3][:, 2 * half : 2 * half + 2, :].rearrange("p t v -> p (t v)"), in_=banks_q[half][:, 0 : 2 * P])
-        nc.sync.dma_start(out=out_rows[:, :, EARLY:T], in_=y[3][:])
-        weave(3)
-        result_planes(256, P)
-        result_planes(EARLY, P)
-        store_words(256, 256)
+        for b in range(2):
+            store(0, read_bank(0, b, nc.scalar.copy))
+        store(1, read_bank(1, 0, nc.scalar.copy))
+        result_planes(0)
+        store_words(0, HALF)
+        result_planes(1)
+        read_bank(2, 0, nc.vector.tensor_copy)
+        read_bank(2, 1, nc.scalar.copy)
+        store(2, slice(0, PACK))
+        result_planes(2)
+        store_words(HALF, HALF)
         for q in range(4):
             queue = nc.sync if q % 2 else nc.scalar
             queue.dma_start(

@@ -47,9 +47,9 @@ def tile_picked_wsagecat_max_lo_kernel(
         xs = new_tile("xs", [P, T], U8)
         nc.vector.memset(xs[:].bitcast(I32), 0)
         w1_rows = w1.rearrange("(p j) c -> p j c", j=PACK)
-        w1_raw = [new_tile("w1_raw%d" % c, [P, PACK, HALF], F32) for c in range(2)]
+        w1_raw = [new_tile("w1_raw%d" % c, [P, 2, H], F32) for c in range(2)]
         for c in range(2):
-            nc.sync.dma_start(out=w1_raw[c][:], in_=w1_rows[:, :, HALF * c : HALF * (c + 1)])
+            nc.sync.dma_start(out=w1_raw[c][:], in_=w1_rows[:, 2 * c : 2 * c + 2, :])
         xw = new_tile("xw", [P, 2 * T], U8)
         nc.sync.dma_start(out=xw[:].bitcast(I32), in_=x_words[0].bitcast(I32))
         for q in range(4):
@@ -76,14 +76,15 @@ def tile_picked_wsagecat_max_lo_kernel(
         w1_codes = [new_tile("w1_codes%d" % t, [P, P], U32) for t in range(PACK)]
         w1_scales = [new_tile("w1_scales%d" % t, [P, P], U8) for t in range(PACK)]
 
-        def round_w1(c, u, copy):
-            src = w1_raw[c][:].rearrange("p j (a u e) -> p u a e j", u=2, e=2)[:, u]
-            dst = w1_bf[u][:].rearrange("p e (c a j) -> p c a e j", c=2, j=PACK)[:, c]
+        def round_w1(c, u, copy, e=slice(0, 2)):
+            src = w1_raw[c][:].rearrange("p j (a u e) -> p u a e j", u=2, e=2)[:, u, :, e]
+            dst = w1_bf[u][:].rearrange("p e (a c j) -> p c a e j", c=2, j=2)[:, c, :, e]
             copy(out=dst, in_=src)
 
         round_w1(0, 0, nc.vector.tensor_copy)
         round_w1(0, 1, nc.vector.tensor_copy)
-        round_w1(1, 0, nc.vector.tensor_copy)
+        round_w1(1, 0, nc.vector.tensor_copy, slice(1, 2))
+        round_w1(1, 0, nc.vector.tensor_copy, slice(0, 1))
         round_w1(1, 1, nc.scalar.copy)
         h = [new_tile("h%d" % u, [P, 2 * T + PAD], F32) for u in range(2)]
         for u in range(2):
@@ -145,10 +146,11 @@ def tile_picked_wsagecat_max_lo_kernel(
 
         h_pairs = tile_at("h_pairs", [P, 2, T, 2], BF16, 8192)
         h_bf = new_tile("h_bf", [P, T, 2, 2], BF16)
-        for u in range(2):
+        w2_dealt = w_bf[0][:].rearrange("p (t a s) -> p a t s", t=PACK, s=PACK)
+        for u, n in enumerate((64, 32)):
             nc.gpsimd.tensor_scalar(
-                w_bf[0][:].rearrange("p (t a s) -> p a t s", t=PACK, s=PACK)[:, 64 * u : 64 * (u + 1)],
-                w2_raw[u][:].rearrange("p s (a t) -> p a t s", t=PACK),
+                w2_dealt[:, 64 * u : 64 * u + n],
+                w2_raw[u][:].rearrange("p s (a t) -> p a t s", t=PACK)[:, 0:n],
                 1.0, 0.0, MULT, ADD,
             )
             nc.gpsimd.tensor_scalar(
@@ -162,6 +164,10 @@ def tile_picked_wsagecat_max_lo_kernel(
 
         w3_raw.append(tile_at("w3_raw1", [P, PACK, HALF], F32, 16384))
         nc.sync.dma_start(out=w3_raw[1][:], in_=w3_rows[:, :, HALF:H])
+        nc.vector.tensor_copy(
+            out=w2_dealt[:, 96:128].rearrange("p a t s -> p a s t"),
+            in_=w2_raw[1][:].rearrange("p s (a t) -> p a s t", t=PACK)[:, 32:64],
+        )
         round_w3(1)
         quantize(w_codes[0][:], w_scales[0][:], w_bf[0][:])
         quantize(w_codes[1][:], w_scales[1][:], w_bf[1][:])
@@ -231,12 +237,14 @@ def tile_picked_wsagecat_max_lo_kernel(
             v0, n = parts[k]
             nc.sync.dma_start(out=out_rows[:, planes, v0 : v0 + n], in_=y[k][:, planes, :])
 
-        def result_planes(k):
-            v0, n = parts[k]
+        def weave(k):
             nc.vector.tensor_copy(
                 out=y_bf[k][:].rearrange("p (c i t) -> p c t i", i=4, t=PACK),
                 in_=y[k][:].rearrange("p t (c i) -> p c t i", i=4),
             )
+
+        def result_planes(k):
+            v0, n = parts[k]
             quantize(y_words[:, v0 : v0 + n], y_scales[:, v0 : v0 + n], y_bf[k][:])
 
         def store_words(v0, n):
@@ -259,12 +267,18 @@ def tile_picked_wsagecat_max_lo_kernel(
         for b in range(2):
             store(0, read_bank(0, b, nc.scalar.copy))
         store(1, read_bank(1, 0, nc.scalar.copy))
-        result_planes(0)
-        store_words(0, HALF)
-        result_planes(1)
+        weave(0)
         read_bank(2, 0, nc.vector.tensor_copy)
         read_bank(2, 1, nc.scalar.copy)
         store(2, slice(0, PACK))
+        nc.scalar.copy(
+            out=y_bf[1][:].rearrange("p (v t) -> p v t", t=PACK),
+            in_=part_banks[1][0][:].rearrange("p (t v) -> p v t", t=PACK),
+        )
+        result_planes(0)
+        store_words(0, HALF)
+        weave(2)
+        result_planes(1)
         result_planes(2)
         store_words(HALF, HALF)
         for q in range(4):

from contextlib import ExitStack

import concourse.mybir as mybir

F32 = mybir.dt.float32
BF16 = mybir.dt.bfloat16
I32 = mybir.dt.int32
U32 = mybir.dt.uint32
U16 = mybir.dt.uint16
U8 = mybir.dt.uint8
FP8X4 = mybir.dt.float8_e4m3fn_x4
FP4X4 = mybir.dt.float4_e2m1fn_x4
RELU = mybir.ActivationFunctionType.Relu
COPY = mybir.ActivationFunctionType.Copy
MAX = mybir.AluOpType.max
MULT = mybir.AluOpType.mult
ADD = mybir.AluOpType.add

P = 128
PACK = 4
T = 512
H = 512
PAD = 256
HALF = 256
FLOPS = 3 * 2 * 512 * 512 * 512


def tile_picked_wsagecat_max_lo_kernel(
    tc, x_words, x_scales, w1, w2, w3, pos1, pos2, pos3, pos4, out_0, out_1, out_2
):
    nc = tc.nc
    with ExitStack() as ctx:
        lists_pool = ctx.enter_context(tc.tile_pool(name="lists", bufs=1))
        sb = ctx.enter_context(tc.tile_pool(name="sb", bufs=1))
        shared = ctx.enter_context(tc.tile_pool(name="shared", bufs=1))
        psum = ctx.enter_context(tc.psum_pool(name="psum", bufs=1))

        def new_tile(name, shape, dtype):
            return sb.tile(shape, dtype, name=name, align_bytes=64)

        def tile_at(name, shape, dtype, offset):
            return shared.tile(shape, dtype, name=name, align_bytes=64, offset=offset)

        def quantize(codes, scales, src):
            nc.vector.quantize_mx(out=codes.bitcast(FP8X4), scales=scales, in_=src)

        xs = new_tile("xs", [P, T], U8)
        nc.vector.memset(xs[:].bitcast(I32), 0)
        w1_rows = w1.rearrange("(p j) c -> p j c", j=PACK)
        w1_raw = [new_tile("w1_raw%d" % c, [P, 2, H], F32) for c in range(2)]
        for c in range(2):
            nc.sync.dma_start(out=w1_raw[c][:], in_=w1_rows[:, 2 * c : 2 * c + 2, :])
        xw = new_tile("xw", [P, 2 * T], U8)
        nc.sync.dma_start(out=xw[:].bitcast(I32), in_=x_words[0].bitcast(I32))
        for q in range(4):
            nc.scalar.dma_start(
                out=xs[32 * q : 32 * q + 4, :].bitcast(I32), in_=x_scales[0, 4 * q : 4 * q + 4, :].bitcast(I32)
            )
        lists = [lists_pool.tile([P, T // 16], U16, name="pos%d" % d) for d in range(4)]
        w2_raw = [tile_at("w2_raw0", [P, PACK, HALF], F32, 16384), new_tile("w2_raw1", [P, PACK, HALF], F32)]
        w3_raw = [new_tile("w3_raw0", [P, PACK, HALF], F32)]
        w2_rows = w2.rearrange("(p s) c -> p s c", s=PACK)
        w3_rows = w3.rearrange("(p s) c -> p s c", s=PACK)
        nc.sync.dma_start(lists[0][:], pos1)
        nc.sync.dma_start(out=w3_raw[0][:], in_=w3_rows[:, :, 0:HALF])
        nc.sync.dma_start(lists[1][:], pos2)
        nc.sync.dma_start(out=w2_raw[0][:], in_=w2_rows[:, :, 0:HALF])
        nc.sync.dma_start(lists[2][:], pos3)
        nc.sync.dma_start(lists[3][:], pos4)
        nc.sync.dma_start(out=w2_raw[1][:], in_=w2_rows[:, :, HALF:H])

        banks_p = [psum.tile([P, T], F32, name="bank_p%d" % t) for t in range(PACK)]
        banks_q = [psum.tile([P, T], F32, name="bank_q%d" % t) for t in range(PACK)]

        w1_bf = [tile_at("w1_bf%d" % u, [P, 2, PACK * P], BF16, 2048 * u) for u in range(2)]
        w1_codes = [new_tile("w1_codes%d" % t, [P, P], U32) for t in range(PACK)]
        w1_scales = [new_tile("w1_scales%d" % t, [P, P], U8) for t in range(PACK)]

        def round_w1(c, u, copy, e=slice(0, 2)):
            src = w1_raw[c][:].rearrange("p j (a u e) -> p u a e j", u=2, e=2)[:, u, :, e]
            dst = w1_bf[u][:].rearrange("p e (a c j) -> p c a e j", c=2, j=2)[:, c, :, e]
            copy(out=dst, in_=src)

        round_w1(0, 0, nc.vector.tensor_copy)
        round_w1(0, 1, nc.vector.tensor_copy)
        round_w1(1, 0, nc.vector.tensor_copy, slice(1, 2))
        round_w1(1, 0, nc.vector.tensor_copy, slice(0, 1))
        round_w1(1, 1, nc.scalar.copy)
        h = [new_tile("h%d" % u, [P, 2 * T + PAD], F32) for u in range(2)]
        for u in range(2):
            nc.gpsimd.memset(h[u][:, 2 * T :], 0.0)

        def plane(t):
            return h[t // 2][:, T * (t % 2) : T * (t % 2 + 1)]

        def first_product(out, t, c0, n):
            nc.tensor.matmul_mx(
                out=out, lhsT=w1_codes[t][:].bitcast(FP8X4), lhsT_scale=w1_scales[t][:],
                rhs=xw[:, 2 * c0 : 2 * (c0 + n)].bitcast(FP4X4), rhs_scale=xs[:, c0 : c0 + n],
                start=True, stop=True,
            )

        quantize(w1_codes[1][:], w1_scales[1][:], w1_bf[0][:, 1, :])
        for piece in range(2):
            c0 = HALF * piece
            first_product(banks_q[piece][:, 0:HALF], 1, c0, HALF)
            nc.scalar.activation(plane(1)[:, c0 : c0 + HALF], banks_q[piece][:, 0:HALF], RELU)
        for t in (0, 3, 2):
            quantize(w1_codes[t][:], w1_scales[t][:], w1_bf[t // 2][:, t % 2, :])
            first_product(banks_p[t][:], t, 0, T)
            nc.scalar.activation(plane(t), banks_p[t][:], RELU)

        w_bf = [new_tile("w2_bf", [P, PACK * H], BF16), tile_at("w3_bf", [P, PACK * H], BF16, 0)]

        def round_w3(c):
            nc.vector.tensor_copy(
                out=w_bf[1][:].rearrange("p (t a e u) -> p a e u t", t=PACK, e=2, u=2)[:, 64 * c : 64 * (c + 1)],
                in_=w3_raw[c][:].rearrange("p (u e) (a t) -> p a e u t", t=PACK, e=2),
            )

        round_w3(0)

        h_late = [new_tile("h_late%d" % u, [P, T], F32) for u in range(2)]
        for u in range(2):
            nc.sync.dma_start(out=h_late[u][:], in_=plane(2 * u + 1))

        def offsets(d, v0, n):
            return lists[d][:, v0 // 16 : (v0 + n) // 16]

        g = [new_tile("g%d" % d, [P, 2, T, 2], BF16) for d in range(3)]
        for d in range(3):
            for u in range(2):
                nc.vector.tensor_copy(out=g[d][:, 1, :, u], in_=h[u][:, T:].indirect(lists[d][:]))
        for d in range(3):
            for u in range(2):
                nc.scalar.activation(g[d][:, 0, :, u], h[u][:].indirect(lists[d][:]), COPY)
        parts = ((0, 256), (256, 128), (384, 128))
        g3 = [new_tile("g3_0", [P, 2, HALF, 2], BF16)]

        def last_list(c):
            for e, windows in enumerate((h, h_late)):
                for u in range(2):
                    nc.scalar.activation(g3[c][:, e, :, u], windows[u][:].indirect(offsets(3, HALF * c, HALF)), COPY)

        last_list(0)

        h_pairs = tile_at("h_pairs", [P, 2, T, 2], BF16, 8192)
        h_bf = new_tile("h_bf", [P, T, 2, 2], BF16)
        w2_dealt = w_bf[0][:].rearrange("p (t a s) -> p a t s", t=PACK, s=PACK)
        for u, n in enumerate((64, 32)):
            nc.gpsimd.tensor_scalar(
                w2_dealt[:, 64 * u : 64 * u + n],
                w2_raw[u][:].rearrange("p s (a t) -> p a t s", t=PACK)[:, 0:n],
                1.0, 0.0, MULT, ADD,
            )
            nc.gpsimd.tensor_scalar(
                h_pairs[:, u], h[u][:, 0 : 2 * T].rearrange("p (e v) -> p v e", e=2), 1.0, 0.0, MULT, ADD
            )

        h_codes = new_tile("h_codes", [P, T], U32)
        h_scales = new_tile("h_scales", [P, T], U8)
        w_codes = [new_tile("w_codes%d" % n, [P, H], U32) for n in range(2)]
        w_scales = [new_tile("w_scales%d" % n, [P, H], U8) for n in range(2)]

        w3_raw.append(tile_at("w3_raw1", [P, PACK, HALF], F32, 16384))
        nc.sync.dma_start(out=w3_raw[1][:], in_=w3_rows[:, :, HALF:H])
        nc.vector.tensor_copy(
            out=w2_dealt[:, 96:128].rearrange("p a t s -> p a s t"),
            in_=w2_raw[1][:].rearrange("p s (a t) -> p a s t", t=PACK)[:, 32:64],
        )
        round_w3(1)
        quantize(w_codes[0][:], w_scales[0][:], w_bf[0][:])
        quantize(w_codes[1][:], w_scales[1][:], w_bf[1][:])
        nc.vector.tensor_copy(out=h_bf[:], in_=h_pairs[:].rearrange("p u v e -> p v u e"))
        quantize(h_codes[:], h_scales[:], h_bf[:].rearrange("p v e u -> p (v e u)"))
        g3.append(tile_at("g3_1", [P, 2, HALF, 2], BF16, 10304))
        last_list(1)

        def fold(dst, acc, other):
            nc.vector.tensor_tensor(dst, acc, other, MAX)

        max2 = [tile_at("max2_%d" % c, [P, 2, HALF, 2], BF16, 6208 + 2048 * c) for c in range(2)]
        max3 = [new_tile("max3_%d" % v0, [P, 2, n, 2], BF16) for v0, n in parts]

        def in_half(tiles, k):
            v0, n = parts[k]
            return tiles[v0 // HALF][:, :, v0 % HALF : v0 % HALF + n]

        def first_maximum(c):
            cols = slice(HALF * c, HALF * (c + 1))
            fold(max2[c][:], g[0][:, :, cols], g[1][:, :, cols])

        def second_maximum(k):
            v0, n = parts[k]
            fold(max3[k][:], in_half(max2, k), g[2][:, :, v0 : v0 + n])

        y_words = new_tile("y_words", [P, T], U32)
        y_scales = new_tile("y_scales", [P, T], U8)
        out_rows = out_0.rearrange("(p t) v -> p t v", t=PACK)
        out_words = out_1[0].rearrange("p c r -> p (c r)").bitcast(I32)
        z_codes = new_tile("z_codes", [P, T], U32)
        z_scales = new_tile("z_scales", [P, T], U8)
        z_bf = [new_tile("z_bf%d" % v0, [P, n, 2, 2], BF16) for v0, n in parts]
        y = [new_tile("y%d" % v0, [P, PACK, n], F32) for v0, n in parts]
        y_bf = [new_tile("y_bf%d" % v0, [P, PACK * n], BF16) for v0, n in parts]
        part_banks = [(banks_p[1], banks_q[2]), (banks_q[3],), (banks_q[0], banks_q[1])]

        def second_passes(k, n, codes, scales):
            v0, width = parts[k]
            per_bank = PACK // len(part_banks[k])
            for t in range(PACK):
                slot = t % per_bank
                cols = slice(P * t, P * (t + 1))
                nc.tensor.matmul_mx(
                    out=part_banks[k][t // per_bank][:, width * slot : width * (slot + 1)],
                    lhsT=w_codes[n][:, cols].bitcast(FP8X4), lhsT_scale=w_scales[n][:, cols],
                    rhs=codes[:, v0 : v0 + width].bitcast(FP8X4), rhs_scale=scales[:, v0 : v0 + width],
                    start=n == 0 and slot == 0, stop=n == 1 and slot == per_bank - 1,
                )

        def last_maximum(k):
            fold(z_bf[k][:], max3[k][:].rearrange("p e v u -> p v e u"), in_half(g3, k).rearrange("p e v u -> p v e u"))

        def z_product(k):
            v0, n = parts[k]
            quantize(z_codes[:, v0 : v0 + n], z_scales[:, v0 : v0 + n], z_bf[k][:].rearrange("p v e u -> p (v e u)"))
            second_passes(k, 1, z_codes, z_scales)

        def read_bank(k, b, copy):
            n = parts[k][1]
            per_bank = PACK // len(part_banks[k])
            planes = slice(per_bank * b, per_bank * (b + 1))
            copy(out=y[k][:, planes, :].rearrange("p t v -> p (t v)"), in_=part_banks[k][b][:, 0 : per_bank * n])
            return planes

        def store(k, planes):
            v0, n = parts[k]
            nc.sync.dma_start(out=out_rows[:, planes, v0 : v0 + n], in_=y[k][:, planes, :])

        def weave(k):
            nc.vector.tensor_copy(
                out=y_bf[k][:].rearrange("p (c i t) -> p c t i", i=4, t=PACK),
                in_=y[k][:].rearrange("p t (c i) -> p c t i", i=4),
            )

        def result_planes(k):
            v0, n = parts[k]
            quantize(y_words[:, v0 : v0 + n], y_scales[:, v0 : v0 + n], y_bf[k][:])

        def store_words(v0, n):
            nc.sync.dma_start(out=out_words[:, v0 : v0 + n], in_=y_words[:, v0 : v0 + n].bitcast(I32))

        second_passes(0, 0, h_codes, h_scales)
        first_maximum(0)
        second_maximum(0)
        last_maximum(0)
        z_product(0)
        second_passes(1, 0, h_codes, h_scales)
        second_passes(2, 0, h_codes, h_scales)
        first_maximum(1)
        second_maximum(1)
        second_maximum(2)
        last_maximum(1)
        last_maximum(2)
        z_product(1)
        z_product(2)
        for b in range(2):
            store(0, read_bank(0, b, nc.scalar.copy))
        store(1, read_bank(1, 0, nc.scalar.copy))
        weave(0)
        read_bank(2, 0, nc.vector.tensor_copy)
        read_bank(2, 1, nc.scalar.copy)
        store(2, slice(0, PACK))
        nc.scalar.copy(
            out=y_bf[1][:].rearrange("p (v t) -> p v t", t=PACK),
            in_=part_banks[1][0][:].rearrange("p (t v) -> p v t", t=PACK),
        )
        result_planes(0)
        store_words(0, HALF)
        weave(2)
        result_planes(1)
        result_planes(2)
        store_words(HALF, HALF)
        for q in range(4):
            queue = nc.sync if q % 2 else nc.scalar
            queue.dma_start(
                out=out_2[0, 4 * q : 4 * q + 4, :].bitcast(I32), in_=y_scales[32 * q : 32 * q + 4, :].bitcast(I32)
            )
